import numpy as np, ml_dtypes
CORES = [2,6,10,14,18,22,26,30]
N = 8
import mx_ref
BF = ml_dtypes.bfloat16
def gcols(t, e):
    v = np.concatenate([t.reshape(8, 16, -1, 4), np.zeros((8, 16, 1, 4), BF)], axis=2)
    return np.ascontiguousarray(np.stack([v[g][:, e[g]] for g in range(8)])).reshape(128, -1)
def tile(rs):
    return np.stack(rs, axis=2).reshape(128, -1).astype(BF)
def pick(q, e):
    c = np.concatenate([q[0].reshape(128, -1, 4), np.zeros((128, 1, 4), np.uint8)], axis=1); s = np.concatenate([q[1], np.ones((16, 1), np.uint8)], axis=1)
    return (np.ascontiguousarray(c[:, e].reshape(128, -1)), np.ascontiguousarray(s[:, e]))
def join(*qs):
    return (np.concatenate([q[0] for q in qs], axis=1), np.concatenate([q[1] for q in qs], axis=1))
def put(q, e, v):
    c, s = q[0].reshape(128, -1, 4).copy(), q[1].copy(); c[:, e] = v[0].reshape(128, -1, 4); s[:, e] = v[1]
    return (c.reshape(128, -1), s)
def pk(c, s):
    return (np.ascontiguousarray(c), mx_ref.live(s))
def emit(q):
    return q[0], q[1]
def packed(v, rng):
    q = [mx_ref.quantize(np.ascontiguousarray(v[r])) for r in range(N)]
    return np.stack([a for a, b in q]), np.stack([mx_ref.plane(b, rng) for a, b in q])
def values_of_codes():
    e, c = np.zeros((128, 128, 4), np.float32), np.zeros((128, 2, 4), np.uint8)
    e[np.arange(128), np.arange(128), 0] = 1
    c[:127, :, 0] = np.arange(256).reshape(2, 128).T[:127]
    return mx_ref.matmul(mx_ref.quantize(e.reshape(128, 512).astype(BF)), (c.reshape(128, 8), np.full((16, 2), 127, np.uint8))).T.reshape(-1).astype(np.float64)
CODE_VALUE, SCALE_VALUE = values_of_codes(), 2.0 ** (np.arange(256) - 127.0)
def decode(q):
    return (CODE_VALUE[q[0]].reshape(16, 8, -1, 4) * SCALE_VALUE[q[1]][:, None, :, None] + 0.0).reshape(128, -1).astype(np.float32)
def f(rng, *shape):
    return mx_ref.flush((rng.standard_normal(shape, dtype=np.float32) * np.exp2(rng.integers(-2, 3, shape[:-1] + (1,)))).astype(BF))
def wide(rng, *shape, cols=0):
    v = rng.standard_normal(shape, dtype=np.float32) * np.exp2(rng.integers(-12, 13, shape)).astype(np.float32)
    if cols: v *= np.repeat(np.exp2(rng.integers(-cols, cols + 1, shape[:-2] + (1, shape[-1] // 4))) * (rng.random(shape[:-2] + (1, shape[-1] // 4)) > 0.0625), 4, axis=-1).astype(np.float32)
    return mx_ref.flush(v.astype(BF))
C, H, M, R = 512, 6, 64, 2
def keys(p):
    b = p.reshape(8, 16, -1)[:, :H] > 0
    return np.sum(b * (1 << np.arange(H))[:, None], axis=1)
def cells(a, key):
    a = a.reshape(8, 16, C, 4)
    c = np.zeros((8, 16, M, 4), np.float32)
    for g in range(8):
        for k in np.unique(key[g]): c[g, :, k] = np.max(a[g][:, key[g] == k], axis=1)
    return c.reshape(128, 4 * M).astype(BF)
def big(v, k):
    v = v.astype(np.float32) * np.float32(k)
    v[np.abs(v) < np.float32(2.0 ** -16)] = 0
    return v.astype(BF)
def weights(rng, k, still=0):
    w = big(f(rng, 128, 2048), k).reshape(128, 4, 128, 4)
    w[:, :, np.arange(128) % 16 < still] = 0
    w = w.reshape(128, 2048)
    c, p = packed(np.stack([w] * N), rng)
    return {"wc": c, "ws": p}
def numbers_of(rng):
    return {"x": big(f(rng, N, 128, 4 * C), 1), "u": np.array(f(rng, N, 128, 512)), "v": np.array(f(rng, N, 128, 512))}
def aim(d, x, key, size):
    u = d["u"].reshape(N, 128, 128, 4)
    for i in range(H):
        x[:, :, i // 4, :, i % 4] = np.where((key >> i) & 1, size, -size)
        for g in range(8):
            u[:, :, 16 * g + i] = 0
            u[:, 16 * g + i // 4, 16 * g + i, i % 4] = 1
def setup_inputs(rng):
    return {**numbers_of(rng), **weights(rng, 1)}
def setup_inputs_ties(rng):
    d = numbers_of(rng)
    d["u"].reshape(N, 8, 16, 128, 4)[:, :, 8:] = 0
    x = d["x"].reshape(N, 8, 16, C, 4)
    e = rng.permutation(N)
    for r in range(N):
        a = x[r][:, :, :1].copy()
        k = rng.permutation(C) % 4
        if r == e[1]: k[:] = 2
        x[r][:, :, k == 0] = 0
        x[r][:, :8, k == 1] = 0
        x[r][:, :, k == 2] = a
    x[e[0]] = 0
    return {**d, "x": x.reshape(N, 128, 4 * C), **weights(rng, 1)}
def setup_inputs_near(rng):
    d = numbers_of(rng)
    x = rng.integers(4, 8, (N, 8, 16, C, 4)) * rng.choice([-0.25, 0.25], (N, 8, 16, C, 4))
    x[:, :, :8] = 0
    s = rng.choice([-1.0, 1.0], (N, 8, C))
    x[:, :, 8, :, 0] = s
    x[:, :, 9, :, 0] = -s
    o = rng.permutation(N)
    a = int(np.argmax(o == 1))
    x[a, :, 8:10, :, 0] = 0
    x[a, :, 7, :, 0] = -s[a] * 2.0 ** -27
    k = np.where(o % 2 == 0, 1.0, 2.0 ** -30).astype(np.float32).astype(BF)
    u = d["u"].reshape(N, 128, 128, 4)
    for i in range(H):
        c = rng.choice([-1.0, 0.0, 1.0, 1.0], (N, 8, C))
        x[:, :, i // 4, :, i % 4] = c * 2.0 ** -23
        x[a, :, i // 4, :, i % 4] = (s[a] + c[a] * 0.125) * 2.0 ** -27
        for g in range(8):
            u[:, :, 16 * g + i] = 0
            u[:, 16 * g + i // 4, 16 * g + i, i % 4] = k
            u[:, 16 * g + 7:16 * g + 10, 16 * g + i, 0] = k[:, None]
    return {**d, "x": x.astype(np.float32).reshape(N, 128, 4 * C).astype(BF), **weights(rng, 1, 10)}
def setup_inputs_huge(rng):
    d = numbers_of(rng)
    key = np.stack([np.stack([rng.permutation(C) % M for g in range(8)]) for r in range(N)])
    sign = np.stack([rng.permutation(M) % 2 * 2.0 - 1.0 for g in range(8)])
    size = rng.integers(8, 17, (N, 8, 16, C, 4))
    size[..., :2] = 16
    x = size * 2.0 ** 26 * sign[np.arange(8)[:, None], key][:, :, None, :, None]
    aim(d, x, key, 2.0 ** 30)
    d["u"] = big(d["u"], 2.0 ** 25)
    return {**d, "x": x.astype(np.float32).reshape(N, 128, 4 * C).astype(BF), **weights(rng, 2.0 ** -3, 2)}
def setup_inputs_crowd(rng):
    d = numbers_of(rng)
    e = rng.permutation(N)
    half = rng.permutation(8) < 4
    nil = rng.permutation(8) < 2
    p = int(e[3]) * (M // N) + M // N - 2
    gone = rng.choice([r for r in range(1, N) if r != e[3]])
    there = np.array([k for k in range(M) if k // (M // N) != gone and k not in (p, p + 1)])
    j = rng.permutation(C)
    key, low = np.zeros((N, 8, C), int), np.zeros((N, 8, C), bool)
    for g in range(8):
        c = rng.permutation(there)
        if nil[g]: c = np.concatenate([[0], c[c != 0]])
        for r in range(N):
            k = np.concatenate([c[:1], rng.choice(c[2:], C - 1)])
            if r == e[1] or r == e[0] and half[g]: k[:] = c[0]
            if r == e[2]: k = np.resize(c, C)
            if r == e[3]: key[r, g, j] = np.concatenate([[p, p + 1, p + 1], rng.permutation(k[:-3])])
            else: key[r, g] = rng.permutation(k)
        low[:, g] = (key[:, g] == c[0]) | (key[:, g] == c[1])
    x = d["x"].astype(np.float32).reshape(N, 8, 16, C, 4)
    x = np.where(low[:, :, None, :, None], -1 - np.abs(x), x)
    a = x[e[1]]
    a[:, 2:, 0, 1] = 0
    a[:, 2:, -1, 2] = 0
    b = x[e[3]]
    b[:, 8:, j[0]] = (1 + rng.random((8, 8, 4))) * np.exp2(rng.integers(-1, 4, (8, 8, 4)))
    b[:, 15, j[0], 3] = -127 * 2.0 ** 10
    b[:, 8:, j[1]] = 1 + rng.random((8, 8, 4))
    b[:, 15, j[1], 3] = -2.0 ** 22
    b[:, 8:, j[2]] = -1 - rng.random((8, 8, 4))
    aim(d, x, key, 1.0)
    a[nil, :, -1] = 0
    return {**d, "x": x.astype(np.float32).reshape(N, 128, 4 * C).astype(BF), **weights(rng, 1, 2)}
def setup_inputs_spread(rng):
    d = setup_inputs(rng)
    d["x"] = big(wide(rng, N, 128, 4 * C, cols=6), 1)
    return d
def check_inputs(d):
    b = []
    for k in ("x", "u", "v"):
        a = np.abs(d[k].astype(np.float32))
        if not (np.isfinite(a).all() and ((a == 0) | (a >= 2.0 ** -30) & (a <= 2.0 ** 30)).all()): b.append("a value of " + k)
    if (d["wc"] != d["wc"][:1]).any(): b.append("wc differs between ranks")
    s = [mx_ref.live(p) for p in d["ws"]]
    if any((p != s[0]).any() for p in s): b.append("ws differs between ranks")
    try:
        a = np.abs(decode(pk(d["wc"][0], d["ws"][0])))
        m = np.max(a.reshape(16, 8, 512, 4), axis=(1, 3))
        good = bool(np.isfinite(a).all() and ((m == 0) | (m >= 2.0 ** -30) & (m <= 2.0 ** 30)).all())
    except Exception:
        good = False
    if not good: b.append("a value of W")
    return b
def reference(x, u, v, wc, ws):
    w = pk(wc[0], ws[0])
    qu = [mx_ref.quantize(u[r]) for r in range(N)]
    now = [x[r] for r in range(N)]
    kl = np.zeros((N, 8 * R, C), np.float32)
    for t in range(R):
        held, key, made = [], [], []
        for r in range(N):
            q = mx_ref.quantize(now[r])
            key.append(keys(mx_ref.matmul(qu[r], q)))
            held.append(decode(q))
            made.append(mx_ref.quantize(cells(held[r], key[r])))
            kl[r, 8 * t:8 * t + 8] = key[r]
        merged = np.max(decode(join(*made)).reshape(128, N, 4 * M), axis=1)
        z = mx_ref.quantize(np.ascontiguousarray(merged.astype(BF)))
        g = tile([np.maximum(mx_ref.matmul(pick(w, np.arange(128 * b, 128 * b + 128)), z), np.float32(0.0)) * np.float32(0.015625) for b in range(4)])
        back = decode(mx_ref.quantize(g)).astype(BF)
        for r in range(N):
            now[r] = ((held[r] + gcols(back, key[r]).astype(np.float32)) * np.float32(0.5)).astype(BF)
    y = np.zeros((N, 128, C), np.float32)
    oc, osc = np.zeros((N, 128, 4 * C), np.uint8), np.zeros((N, 16, C), np.uint8)
    for r in range(N):
        q = mx_ref.quantize(now[r])
        y[r] = mx_ref.matmul(mx_ref.quantize(v[r]), q)
        oc[r], osc[r] = emit(q)
    return {"y": y, "kl": kl, "oc": oc, "osc": osc}

@@ -1,0 +1,655 @@
+from concourse.bass import DstId, RemoteDMATransfer
+from concourse.mybir import dt, AluOpType, AxisListType, ActivationFunctionType
+
+OP, ACT, AX = AluOpType, ActivationFunctionType, AxisListType
+ROUNDS = 2
+BIG = 2.0 ** 60
+M16 = 3072.0
+TRIES = 24
+VR = 108
+RW = 1032.0
+RS = 520.0
+
+SCRATCH = {}
+
+
+def _b(names, n, dtype="bfloat16"):
+    for name in names.split():
+        SCRATCH[name] = ("sbuf", [128, n], dtype)
+
+
+def _codes(names, n):
+    for name in names.split():
+        SCRATCH[name] = ("sbuf", [128, n], "float8_e4m3fn_x4")
+        SCRATCH[name + "s"] = ("sbuf", [128, n], "uint8")
+
+
+_b("xs st1 st2 ebt ebk dd sd ge", 2048)
+_b("us vs bt at zt gt vals lo lsw ltr sj", 512)
+_b("jk", 2560)
+_b("one nul idm blk upd lod prm", 128)
+_b("gw0 gw1 gw2", 8)
+_b("kc", 66)
+_b("ktt", 1248)
+_b("lt", 4096)
+_b("prt", 1024)
+_b("ot", 2080)
+_b("tt", 560)
+_b("msk0 msk1", 592)
+_b("sc", 2304)
+_b("neg", 64)
+_b("own mm gb", 256)
+_b("hi", 140)
+_b("rw rv", 140, "float32")
+_b("kf yb", 512, "float32")
+_b("lj lk", 32, "float32")
+_b("kng", 8, "float32")
+_b("acc b5 cneg tb", 5, "float32")
+_b("em dm mk pk dum c16", 4, "float32")
+_b("icf icb wcl", 1, "float32")
+_b("ip ia", 1, "int32")
+_b("po ko l16", 32, "uint16")
+_b("mk16 pk16", 4, "uint16")
+_codes("qu qv qb qa0 qa1 qz qg", 128)
+_codes("qx0 qx1 qx2 qw qe qh qr", 512)
+_codes("qk", 312)
+_codes("ql", 1280)
+_codes("qo", 520)
+_codes("qt", 140)
+_codes("lc0 lc1", 448)
+for _i in range(8):
+    SCRATCH["ps%d" % _i] = ("psum", [128, 512], "float32")
+
+SEMAPHORES = ["cv", "cs", "ct", "cq", "ar0", "ar1", "br0", "br1", "sent",
+              "dx0", "dx1", "du", "dv", "dwc", "dws", "dlo", "dz0", "dz1", "dk0", "dk1", "dy0", "dy1", "do0", "do1", "ds"]
+
+_MASKS = {}
+_PLAN = []
+
+
+def _cols(a, b, st):
+    if (a, b, st) not in _MASKS:
+        m = 0
+        for i in range(a, b, st):
+            m |= 1 << i
+        _MASKS[(a, b, st)] = m
+    return _MASKS[(a, b, st)]
+
+
+def plan(ops, tries):
+    wr, rd, pred = {}, {}, []
+    for i, o in enumerate(ops):
+        p = set()
+        for name, m in o["reads"]:
+            for wm, j in wr.get(name, []):
+                if wm & m:
+                    p.add(j)
+            if name[:2] == "ps":
+                for rm, j in rd.get(name, []):
+                    if ops[j]["e"] != o["e"]:
+                        p.add(j)
+        for name, m in o["writes"]:
+            for om, j in wr.get(name, []) + rd.get(name, []):
+                if om & m:
+                    p.add(j)
+        p.discard(i)
+        for name, m in o["writes"]:
+            wr[name] = [w for w in wr.get(name, []) if w[0] & ~m] + [(m, i)]
+            rd[name] = [r for r in rd.get(name, []) if r[0] & ~m]
+        for name, m in o["reads"]:
+            rd[name] = rd.get(name, []) + [(m, i)]
+        pred.append(sorted(p))
+    n = len(ops)
+    every = range(n)
+    succ = [[] for _ in ops]
+    for i in every:
+        for j in pred[i]:
+            succ[j].append(i)
+    eng = [o["e"] for o in ops]
+    hold = [o["hold"] for o in ops]
+    lat = [o["lat"] for o in ops]
+    WAKE = 0.18
+
+    def free_of(j, i):
+        return eng[j] == "t" and eng[i] == "t" or eng[i] == "n"
+
+    def gap(j, i):
+        return lat[j] if free_of(j, i) else lat[j] + WAKE
+
+    def place(order, early):
+        t = [0.0] * n
+        busy = {e: [] for e in eng}
+        for i in order:
+            d = hold[i]
+            if early:
+                lo = max([0.0] + [t[j] + gap(j, i) for j in pred[i]])
+            else:
+                lo = max([lat[i]] + [t[k] + gap(i, k) for k in succ[i]]) - d
+            if eng[i] != "n":
+                b = busy[eng[i]]
+                z = len(b)
+                while z and b[z - 1][1] > lo + 1e-9:
+                    z -= 1
+                while z < len(b) and b[z][0] < lo + d - 1e-9:
+                    lo = max(lo, b[z][1])
+                    z += 1
+                b.insert(z, (lo, lo + d))
+            t[i] = lo if early else lo + d
+        return t
+
+    def run(order, tensor, wake, others):
+        t = [0.0] * n
+        free = {}
+        end = 0.0
+        for i in order:
+            s = free.get(eng[i], 0.0)
+            for j in pred[i]:
+                x = t[j] if free_of(j, i) else t[j] + wake
+                if x > s:
+                    s = x
+            f = tensor if eng[i] == "t" else others if eng[i] == "n" else 1.0
+            if eng[i] != "n":
+                free[eng[i]] = s + hold[i] * f
+            t[i] = s + lat[i] * f
+            end = max(end, t[i])
+        return end
+    best, seed = None, 1
+    for k in range(tries):
+        way = [0.0] * n
+        for i in range(n - 1, -1, -1):
+            seed = (seed * 1103515245 + 12345) % 2147483648
+            w = lat[i] * (1.0 + (0.8 * seed / 2147483648 - 0.4 if k else 0.0))
+            way[i] = max([w] + [w + gap(i, x) - lat[i] + way[x] for x in succ[i]])
+        t = place(sorted(every, key=lambda i: (-way[i], i)), True)
+        for _ in range(3):
+            order = sorted(every, key=lambda i: (t[i], i))
+            score = sum(run(order, *v) for v in ((1.0, 0.1, 1.0), (1.0, 0.18, 1.3), (2.0, 0.18, 1.0), (1.0, 0.25, 0.8)))
+            if best is None or score < best[0]:
+                best = (score, order)
+            late = place(sorted(every, key=lambda i: (-(t[i] + lat[i]), -i)), False)
+            t = place(sorted(every, key=lambda i: (-late[i], i)), True)
+    return best[1]
+
+
+def prog(g, T):
+    eng = {"v": g.vector, "s": g.scalar, "t": g.tensor, "q": g, "y": g.sync}
+    csem = {"v": "cv", "s": "cs", "t": "ct", "q": "cq"}
+    count = {s: 0 for s in SEMAPHORES}
+    known = {e: {} for e in eng}
+    snap = {}
+    wr, rd = {}, {}
+
+    def wait(e, sem, val):
+        if known[e].get(sem, 0) < val:
+            eng[e].wait_ge(T.sem[sem], val)
+            for s, k in snap.get((sem, val), {}).items():
+                if known[e].get(s, 0) < k:
+                    known[e][s] = k
+            known[e][sem] = val
+
+    def need(e, reads, writes):
+        n = {}
+
+        def add(tok):
+            if n.get(tok[0], 0) < tok[1]:
+                n[tok[0]] = tok[1]
+        for name, m in reads:
+            psum = name[:2] == "ps"
+            for wm, tok, we in wr.get(name, []):
+                if wm & m and not (psum and we == e):
+                    add(tok)
+            if psum:
+                for rm, tok, re_ in rd.get(name, []):
+                    if re_ != e:
+                        add(tok)
+        for name, m in writes:
+            for om, tok, oe in wr.get(name, []) + rd.get(name, []):
+                if om & m and not (e == "t" and oe == "t"):
+                    add(tok)
+        return n
+
+    def note(e, reads, writes, tok):
+        for name, m in writes:
+            wr[name] = [w for w in wr.get(name, []) if w[0] & ~m] + [(m, tok, e)]
+            rd[name] = [r for r in rd.get(name, []) if r[0] & ~m]
+        for name, m in reads:
+            rd[name] = [r for r in rd.get(name, [])
+                        if not (r[2] == e and e != "dma" and r[0] & ~m == 0)] + [(m, tok, e)]
+
+    def issue(o):
+        e = o["e"]
+        if e == "n":
+            return
+        reads = [r for r in o["reads"] if r[0][0] != "@"]
+        writes = [w for w in o["writes"] if w[0][0] != "@"]
+        for s, v in o["pre"]:
+            wait(e, s, v)
+        n = need(e, reads, writes)
+        for s in sorted(n, key=lambda s: -n[s]):
+            wait(e, s, n[s])
+        if o["sem"] == "sent":
+            o["call"]()
+            return
+        s = o["sem"] or csem[e]
+        k = 16 if o["sem"] else 1
+        o["call"]().then_inc(T.sem[s], k)
+        count[s] += k
+        snap[(s, count[s])] = dict(known[e])
+        note("dma" if o["sem"] else e, reads, writes, (s, count[s]))
+    return eng, count, wait, issue
+
+
+def rank_program(g, core, T, topo):
+    rank = T.rank_of(core)
+    if rank is None:
+        return
+    N = len(T.cores)
+    eng, count, wait, issue = prog(g, T)
+    V, S, PE = g.vector, g.scalar, g.tensor
+    ops = []
+    CYC = 0.00083
+
+    def emit(e, call, reads, writes, cost, sem=None, lat=None, pre=()):
+        ops.append({"e": e, "call": call, "reads": reads, "writes": writes, "sem": sem, "pre": list(pre),
+                    "hold": cost, "lat": cost if lat is None else lat})
+
+    def R(name, a=0, b=None, st=1):
+        if name[:2] == "ps":
+            return (name, 1)
+        return (name, _cols(a, SCRATCH[name][1][1] if b is None else b, st))
+
+    def A(name, a=0, b=None, st=1):
+        b = SCRATCH[name][1][1] if b is None else b
+        return T[name][:, a:b] if st == 1 else T[name][:, a:b:st]
+
+    def both(x):
+        return A(*x), R(*x)
+
+    def size(x):
+        return len(range(x[1] if len(x) > 1 else 0, x[2] if len(x) > 2 else SCRATCH[x[0]][1][1], x[3] if len(x) > 3 else 1))
+
+    def vcost(*xs, half=True):
+        short = all(SCRATCH[x[0]][2] in ("bfloat16", "uint16") for x in xs)
+        return 0.05 + CYC * max(64, max(size(x) for x in xs) * (0.5 if short and half else 1.0))
+
+    def fill(x, c):
+        a, r = both(x)
+        emit("v", lambda: V.memset(a, c), [], [r], vcost(x))
+
+    def vcopy(o, i):
+        (oa, orr), (ia, ir) = both(o), both(i)
+        emit("v", lambda: V.tensor_copy(oa, ia), [ir], [orr], vcost(o, i))
+
+    def vts(o, i, s1, s2, op0, op1=None, off=None):
+        (oa, orr), (ia, ir) = both(o), both(i)
+        rs = [ir]
+        if isinstance(s1, tuple):
+            s1, r1 = both(s1)
+            rs.append(r1)
+        cost = vcost(o, i)
+        if off:
+            fa, fr = both(off)
+            ia = ia.indirect(fa)
+            rs.append(fr)
+            cost = 0.05 + 1.5 * CYC * size(o)
+        if op1 is None:
+            emit("v", lambda: V.tensor_scalar(oa, ia, s1, None, op0), rs, [orr], cost)
+        else:
+            emit("v", lambda: V.tensor_scalar(oa, ia, s1, s2, op0, op1), rs, [orr], cost)
+
+    def vtt(o, i0, i1, op, off=None):
+        (oa, orr), (a0, r0), (a1, r1) = both(o), both(i0), both(i1)
+        rs = [r0, r1]
+        cost = vcost(o, i1, half=False)
+        if off:
+            fa, fr = both(off)
+            a0 = a0.indirect(fa)
+            rs.append(fr)
+            cost = 0.05 + 1.5 * CYC * size(o)
+        emit("v", lambda: V.tensor_tensor(oa, a0, a1, op), rs, [orr], cost)
+
+    def vscan(o, mask, data):
+        (oa, orr), (ma, mr), (da, dr) = both(o), both(mask), both(data)
+        emit("v", lambda: V.tensor_tensor_scan(oa, ma, da, -BIG, OP.min, OP.max), [mr, dr], [orr], vcost(o, data))
+
+    def vgather(o, i, off):
+        (oa, orr), (ia, ir), (fa, fr) = both(o), both(i), both(off)
+        emit("v", lambda: V.tensor_copy(oa, ia.indirect(fa)), [ir, fr], [orr], 0.05 + 1.5 * CYC * size(o))
+
+    def vscatter(o, i, off):
+        (oa, orr), (ia, ir), (fa, fr) = both(o), both(i), both(off)
+        emit("v", lambda: V.tensor_copy(oa.indirect(fa), ia), [ir, fr], [orr], 0.05 + 3.0 * CYC * size(i))
+
+    def vtrans(o, i):
+        (oa, orr), (ia, ir) = both(o), both(i)
+        emit("v", lambda: V.transpose(oa, ia), [ir], [orr], vcost(o, i))
+
+    def vreduce(o, i, op):
+        (oa, orr), (ia, ir) = both(o), both(i)
+        emit("v", lambda: V.tensor_reduce(oa, ia, AX.X, op), [ir], [orr], vcost(i, half=False))
+
+    def quant(q, a, b, x, xa, xb):
+        emit("v", lambda: V.quantize_mx(T[q][:, a:b], T[q + "s"][:, a:b], T[x][:, xa:xb]),
+             [R(x, xa, xb)], [R(q, a, b)], 0.012 + 0.00022 * (xb - xa))
+
+    def act(o, i, f, bias=0.0, scale=1.0, off=None, accum=None, lat=None):
+        (oa, orr), (ia, ir) = both(o), both(i)
+        rs, ws = [ir], [orr]
+        if isinstance(bias, tuple):
+            bias, r1 = both(bias)
+            rs.append(r1)
+        if isinstance(scale, tuple):
+            scale, r1 = both(scale)
+            rs.append(r1)
+        cost = 0.065 + CYC * size(o)
+        if off:
+            fa, fr = both(off)
+            ia = ia.indirect(fa)
+            rs.append(fr)
+            cost = 0.065 + 1.5 * CYC * size(o)
+        if accum:
+            aa, ar = both(accum)
+            ws.append(ar)
+            emit("s", lambda: S.activation(oa, ia, f, bias=bias, scale=scale, accum_out=aa), rs, ws, cost + 0.02)
+        else:
+            emit("s", lambda: S.activation(oa, ia, f, bias=bias, scale=scale), rs, ws, cost, lat=lat)
+
+    def mm(ps, n, w, wa, x, xa, start=True, stop=True, pre=()):
+        emit("t", lambda: PE.matmul_mx(T[ps][:, 0:n], T[w][:, wa:wa + 128], T[w + "s"][:, wa:wa + 128],
+                                       T[x][:, xa:xa + n], T[x + "s"][:, xa:xa + n], start, stop),
+             [R(w, wa, wa + 128), R(w + "s", wa, wa + 128), R(x, xa, xa + n)], [R(ps)], 0.5 * CYC * (n + 16), pre=pre)
+
+    def dma(q, sem, oap, iap, reads, writes, lat=1.5):
+        emit(q, lambda: eng[q].dma_start(oap, iap), reads, writes, 0.06, sem=sem, lat=lat)
+
+    def sel(o, i, pattern, cmp, fillv, base, cm):
+        (oa, orr), (ia, ir) = both(o), both(i)
+        emit("q", lambda: g.affine_select(oa, ia, pattern, cmp, fillv, base, cm), [ir], [orr], 0.17 + 2 * CYC * size(o))
+
+    def iota(o, pattern, base, cm):
+        oa, orr = both(o)
+        cost = 0.13 + 2 * CYC * size(o)
+        if SCRATCH[o[0]][2] == "int32":
+            emit("q", lambda: g.iota(oa, pattern, base, cm), [], [orr], cost)
+        else:
+            emit("q", lambda: g.iota(oa, pattern, base, cm, allow_small_or_imprecise_dtypes=True), [], [orr], cost)
+
+    dma("y", "dx0", T.xs[:, 0:1024], T.x[:, 0:1024], [], [R("xs", 0, 1024)])
+    dma("s", "du", T.us[:, 0:512], T.u[:, 0:512], [], [R("us")])
+    dma("y", "dx1", T.xs[:, 1024:2048], T.x[:, 1024:2048], [], [R("xs", 1024, 2048)], lat=2.0)
+
+    fill(("one",), 1.0)
+    fill(("gw0",), 0.0)
+    fill(("nul",), 0.0)
+    fill(("prt",), 0.0)
+    fill(("ktt",), 0.0)
+    fill(("rw", 0, VR), RW)
+    fill(("rw", VR, 140), RS)
+    fill(("neg",), -BIG)
+    for h in (0, 1):
+        dma("y", "dz%d" % h, T.ebt[:, 1024 * h:1024 * h + 1024], T.prt[:, 0:1024], [R("prt")],
+            [R("ebt", 1024 * h, 1024 * h + 1024)], lat=2.5)
+        act(("ebk", 1024 * h, 1024 * h + 1024), ("prt",), ACT.Copy)
+    dma("y", "dwc", T.qw[:, 0:512].bitcast(dt.uint8), T.wc[:, 0:2048], [], [R("qw")], lat=4.0)
+    dma("y", "dws", T.qws[:, 0:512], T.ws[:, 0:512], [], [R("qws")], lat=4.0)
+    dma("y", "dv", T.vs[:, 0:512], T.v[:, 0:512], [], [R("vs")], lat=4.0)
+    for i in range(6):
+        sel(("gw0",), ("gw0",), [[-16, 8]], OP.not_equal, 2.0 ** (i - 1), -i, 1)
+    sel(("gw1",), ("gw0",), [[16, 8]], OP.is_ge, 0.0, 1, -1)
+    sel(("gw2",), ("gw0",), [[-16, 8]], OP.is_ge, 0.0, -2, 1)
+    sel(("upd",), ("one",), [[1, 128]], OP.is_gt, 0.0, 0, -1)
+    sel(("upd",), ("upd",), [[1, 128]], OP.not_equal, 1024.0, 0, -1)
+    sel(("lod",), ("one",), [[-1, 128]], OP.is_gt, 0.0, 0, 1)
+    sel(("lod",), ("lod",), [[-1, 128]], OP.not_equal, -1024.0, 0, 1)
+    iota(("kc", 0, 65), [[1, 65]], -32, 0)
+    sel(("blk",), ("one",), [[-16, 8], [0, 16]], OP.is_ge, 0.0, 0, 1)
+    sel(("blk",), ("blk",), [[16, 8], [0, 16]], OP.is_ge, 0.0, 15, -1)
+    sel(("idm",), ("one",), [[-1, 128]], OP.is_equal, 0.0, 0, 1)
+    sel(("prm",), ("one",), [[-1, 4], [-4, 32]], OP.is_equal, 0.0, 0, 1)
+    iota(("ip",), [[0, 1]], 0, 1)
+    iota(("cneg",), [[-1, 5]], 0, 0)
+    iota(("c16",), [[16, 4]], 513, 0)
+    iota(("lo",), [[0, 2], [1, 256]], 0, 0)
+    iota(("vals",), [[256, 2], [0, 256]], 0, 0)
+    for b in range(4):
+        iota(("sc", 576 * b + 512, 576 * b + 576), [[0, 64]], 0, 0)
+    for n in ("at", "zt", "gt"):
+        iota((n, 256, 512), [[0, 256]], 0, 0)
+    dma("y", "dlo", T.vals[1:128:16, :], T.lo[1:128:16, :], [R("lo")], [R("vals")])
+
+    for b in range(4):
+        act(("ktt", 5 * b, 128, 16), ("gw0",), ACT.Copy)
+        act(("ktt", 128 + 48 + 5 * b, 688, 64), ("gw1",), ACT.Copy, scale=16.0)
+        act(("ktt", 688 + 48 + 5 * b, 1248, 64), ("gw2",), ACT.Copy, scale=0.25)
+    quant("qk", 0, 312, "ktt", 0, 1248)
+    quant("qu", 0, 128, "us", 0, 512)
+    for c in range(4):
+        for s, d in ((0, "upd"), (1, "lod")):
+            for b in range(4):
+                x = ("lt", 2048 * s + 512 * c + b, 2048 * s + 512 * c + 512, 4)
+                w = 0.5 if b == 3 else 1.0
+                if b == c:
+                    vts(x, (d,), w, None, OP.mult)
+                elif c < 3:
+                    fill(x, w if (s == 0) == (b < c) else 0.0)
+                else:
+                    act(x, ("one" if (s == 0) == (b < c) else "nul",), ACT.Copy)
+            quant("ql", 256 + 512 * s + 128 * c, 384 + 512 * s + 128 * c, "lt", 2048 * s + 512 * c, 2048 * s + 512 * c + 512)
+    vreduce(("wcl",), ("gw0",), OP.add)
+    for b in range(4):
+        vcopy(("ebt", 512 * b + b, 512 * b + 512, 4), ("idm",))
+    quant("qe", 0, 512, "ebt", 0, 2048)
+    for b in range(4):
+        act(("ebk", 512 * b + b, 512 * b + 512, 4), ("blk",), ACT.Identity, scale=("wcl",))
+    quant("qr", 0, 512, "ebk", 0, 2048)
+    act(("prt", 0, 512, 4), ("prm",), ACT.Copy, scale=0.0625)
+    act(("prt", 1, 512, 4), ("prm",), ACT.Copy, scale=32.0)
+    act(("prt", 514, 1024, 4), ("prm",), ACT.Copy)
+    act(("prt", 515, 1024, 4), ("prm",), ACT.Copy)
+    quant("ql", 0, 256, "prt", 0, 1024)
+    vts(("ia",), ("ip",), 15, None, OP.bitwise_and)
+    vcopy(("icf",), ("ia",))
+    vts(("icb",), ("icf",), -4.0, 0.5, OP.mult, OP.add)
+    vts(("tb",), ("cneg",), ("icb",), None, OP.add)
+    vts(("dum",), ("c16",), ("icf",), None, OP.add)
+    fill(("msk0",), BIG)
+    fill(("msk1",), BIG)
+
+    lots = ((1, 2, 4, 6), (3, 5, 7))
+    near = [x for x in range(1, N) if topo.chip(T.cores[rank ^ x]) == topo.chip(core)]
+    far = [x for x in range(1, N) if x not in near]
+    fmask = topo.mask(core, T.cores[rank ^ far[0]])
+    nmask = topo.mask(core, T.cores[rank ^ near[0]]) & ~fmask
+
+    def arrive(lot):
+        return sum(2 * bin(nmask if x in near else fmask).count("1") for x in lots[lot])
+
+    def send(t):
+        qa, lc = "qa%d" % t, "lc%d" % t
+
+        def call(lot, plane):
+            ts = []
+            for group, m in ((far, fmask), (near, nmask)):
+                ids, dsts = [], []
+                for x in lots[lot]:
+                    if x in group:
+                        rid, pid = topo.addr(T.cores[rank ^ x])[:2]
+                        c = 256 * lot + 64 * lots[lot].index(x)
+                        ids.append(DstId(rid=rid, pnc=pid))
+                        dsts.append(T[lc + "s"][:, c:c + 64] if plane else T[lc][:, c:c + 64].bitcast(dt.uint8))
+                if ids:
+                    src = T[qa + "s"][:, 0:64] if plane else T[qa][:, 0:64].bitcast(dt.uint8)
+                    ts.append(RemoteDMATransfer(dst_ids=ids, dma_engine_mask=m, remote_sem=T.sem["%sr%d" % ("ab"[lot], t)],
+                                                srcs=[src], dsts=dsts))
+                    count["sent"] += bin(m).count("1")
+            g.remote_dma_fused(ts, local_sem=T.sem.sent)
+        for lot in (0, 1):
+            for plane in (0, 1):
+                emit("q", lambda lot=lot, plane=plane: call(lot, plane), [R(qa)], [("@q", 1), ("@w%d" % lot, 1)], 0.4, sem="sent")
+            emit("n", None, [("@w%d" % lot, 1)], [R(lc, 256 * lot, 256 + 192 * lot)], 0.0, lat=2.5 + 1.5 * lot)
+
+    def ps(i):
+        return "ps%d" % i
+    HB = {2: 4, 3: 5, 0: 6}
+
+    def key_half(t, state, h):
+        qx = "qx%d" % t
+        quant(qx, 256 * h, 256 * h + 256, state, 1024 * h, 1024 * h + 1024)
+        if t < ROUNDS:
+            mm(ps(h), 256, "qu", 0, qx, 256 * h)
+            act(("bt", 256 * h, 256 * h + 256), (ps(h), 0, 256), ACT.Sign, bias=-(2.0 ** -100))
+        else:
+            mm(ps(h), 256, "qv", 0, qx, 256 * h)
+            act(("yb", 256 * h, 256 * h + 256), (ps(h), 0, 256), ACT.Copy)
+            dma("y", "do%d" % h, T.oc[:, 1024 * h:1024 * h + 1024], T[qx][:, 256 * h:256 * h + 256].bitcast(dt.uint8),
+                [R(qx, 256 * h, 256 * h + 256)], [])
+            dma("s", "dy%d" % h, T.y[:, 256 * h:256 * h + 256], T.yb[:, 256 * h:256 * h + 256],
+                [R("yb", 256 * h, 256 * h + 256)], [])
+
+    key_half(0, "xs", 0)
+    key_half(0, "xs", 1)
+    for t in range(ROUNDS):
+        qx, qa, lc = "qx%d" % t, "qa%d" % t, "lc%d" % t
+        new = "st%d" % (t + 1)
+        quant("qb", 0, 128, "bt", 0, 512)
+        mm("ps2", 128, "qb", 0, "qk", 0)
+        mm("ps3", 280, "qb", 0, "qk", 32)
+        act(("tt", 2, 560, 4), ("ps3", 0, 140), ACT.Copy)
+        act(("tt", 3, 560, 4), ("ps3", 140, 280), ACT.Copy)
+        for b in range(4):
+            mm(ps(6 + b % 2), 512, "qe", 128 * b, qx, 0)
+            act(("dd", 512 * b, 512 * b + 512), (ps(6 + b % 2), 0, 512), ACT.Copy, scale=0.5)
+        act(("kng",), ("ps2", 3, 32, 4), ACT.Copy, scale=-1.0)
+        for h in (0, 1):
+            for gg in range(4):
+                for b in range(4):
+                    c = 4 * (4 * h + gg) + b
+                    o = ("ot", 1040 * h + 4 * gg + b, 1040 * h + 1040, 16)
+                    if b == 3:
+                        act(o, ("kc", 0, 65), ACT.Sign, bias=("kng", c // 4, c // 4 + 1))
+                    else:
+                        vts(o, ("kc", 0, 65), ("ps2", c, c + 1), 0.5, OP.is_gt, OP.subtract)
+            quant("qo", 260 * h, 260 * h + 260, "ot", 1040 * h, 1040 * h + 1040)
+        for b in range(4):
+            mm("ps3", 128, "qr", 128 * b, "qb", 0)
+            act(("kf", b, 512, 4), ("ps3", 0, 128), ACT.Identity, bias=31.5)
+        for c in range(5):
+            act(("jk", 512 * c, 512 * c + 512), ("kf",), ACT.Sign, bias=("tb", c, c + 1), accum=("acc", c, c + 1))
+        act(("b5",), ("acc",), ACT.Copy, bias=256.0, scale=-0.5, lat=0.8)
+        dma("y", "dk%d" % t, T.kl[8 * t:8 * t + 8, :], T.kf[0:128:16, :], [R("kf")], [])
+        for h in (0, 1):
+            for c in range(4):
+                p = ps(((0, 1, 4, 5), (0, 1, 4, 2))[h][c])
+                mm(p, 256, "ql", 256 + 128 * c, "qo", 260 * h + 4, True, False)
+                mm(p, 256, "ql", 768 + 128 * c, "qo", 260 * h, False, True)
+                for gg in range(4):
+                    k = 12 + 16 * (4 * h + gg) + c
+                    if k < VR:
+                        vreduce(("rw", k, k + 1), (p, gg, 256, 4), OP.max)
+                    else:
+                        z = 64 * (2 * c + gg - 2)
+                        act(("sj", z, z + 64), (p, gg, 256, 4), ACT.Relu, bias=-512.0, accum=("rw", k, k + 1))
+        for o in ("hi", "rv"):
+            vts((o, 0, VR), ("rw", 0, VR), M16 - RW, None, OP.add)
+            act((o, VR, 140), ("rw", VR, 140), ACT.Identity, bias=M16 - RS)
+        vts(("tt", 0, 560, 4), ("hi",), M16, None, OP.subtract)
+        vtt(("tt", 1, 560, 4), ("rv",), ("hi",), OP.subtract)
+        quant("qt", 0, 140, "tt", 0, 560)
+        for q in range(4):
+            mm("ps0", 128, "qt", 12 - 4 * q, "ql", 32 * q, q == 0, q == 3)
+        for q in range(4):
+            mm("ps1", 128, "qt", 12 - 4 * q, "ql", 128 + 32 * q, q == 0, q == 3)
+        vts(("po",), ("ps0", 0, 32), 256.0, None, OP.add)
+        vts(("ko",), ("ps1", 0, 32), 31.5, None, OP.add)
+        msk = "msk%d" % t
+        vtt(("em",), ("b5", 1, 5), ("b5", 0, 4), OP.is_equal)
+        vtt(("dm",), ("em",), ("dum",), OP.mult)
+        vtt(("mk",), ("b5", 0, 4), ("dm",), OP.max)
+        vtt(("pk",), ("b5", 1, 5), ("dm",), OP.max)
+        vcopy(("mk16",), ("mk",))
+        vts(("pk16",), ("pk",), 1.0, None, OP.subtract)
+        vscatter((msk,), ("neg",), ("mk16",))
+        vscatter(("lsw",), ("vals",), ("po",))
+        vtrans(("ltr",), ("lsw",))
+        for gg in (0, 1):
+            vtt(("lj", 16 * gg, 16 * gg + 16), ("ltr", 16 * gg, 512, 32), ("ltr", 16 * gg + 1, 512, 32), OP.add)
+        vtrans(("lk",), ("lj",))
+        vcopy(("l16",), ("lk",))
+        for b in (0, 2, 1, 3):
+            o, i = ("sd", 512 * b, 512 * b + 512), ("dd", 512 * b, 512 * b + 512)
+            if b < 2:
+                vgather(o, i, ("l16",))
+            else:
+                act(o, i, ACT.Copy, off=("l16",))
+        for b in (0, 2, 1, 3):
+            vscan(("sc", 576 * b, 576 * b + 512), (msk, 0, 512), ("sd", 512 * b, 512 * b + 512))
+            o, i = ("at", b, 256, 4), ("sc", 576 * b, 576 * b + 576)
+            if b < 3:
+                act(o, i, ACT.Copy, scale=2.0, off=("pk16",))
+            else:
+                vts(o, i, 2.0, None, OP.mult, off=("pk16",))
+        quant(qa, 0, 128, "at", 0, 512)
+        send(t)
+        for b in range(4):
+            mm(ps(b), 128, "qe", 128 * b, qa, 0)
+        for b in range(4):
+            act(("own", 64 * b, 64 * b + 64), (ps(b), 0, 64), ACT.Copy)
+        if t == 0:
+            for b in range(4):
+                act(("ebt", 512 * b + b, 512 * b + 512, 4), ("idm",), ACT.Copy, scale=0.5)
+            quant("qv", 0, 128, "vs", 0, 512)
+            quant("qh", 0, 512, "ebt", 0, 2048)
+        for b in (2, 3, 0):
+            mm(ps(HB[b]), 512, "qh", 128 * b, qx, 0)
+        for b in range(4):
+            mm(ps(b), 256, "qe", 128 * b, lc, 0, pre=[("ar%d" % t, arrive(0))])
+        for s in range(4):
+            for b in range(4):
+                o, w = ("mm", 64 * b, 64 * b + 64), ("own" if s == 0 else "mm", 64 * b, 64 * b + 64)
+                vtt(o, (ps(b), 64 * s, 64 * s + 64), w, OP.max)
+        for b in range(4):
+            mm(ps(b), 192, "qe", 128 * b, lc, 256, pre=[("br%d" % t, arrive(1))])
+        for s in range(3):
+            for b in range(4):
+                w = ("mm", 64 * b, 64 * b + 64)
+                vtt(("zt", b, 256, 4) if s == 2 else w, (ps(b), 64 * s, 64 * s + 64), w, OP.max)
+        quant("qz", 0, 128, "zt", 0, 512)
+        for b in range(4):
+            mm(ps(b), 128, "qw", 128 * b, "qz", 0)
+        for b in range(4):
+            vts(("gt", b, 256, 4), (ps(b), 0, 64), 0.0, 0.015625, OP.max, OP.mult)
+        quant("qg", 0, 128, "gt", 0, 512)
+        for b in (0, 2, 1, 3):
+            mm(ps(b), 128, "qe", 128 * b, "qg", 0)
+        for b in (0, 2, 1, 3):
+            o, i = ("gb", 64 * b, 64 * b + 64), (ps(b), 0, 64)
+            if b in (0, 1):
+                vts(o, i, 0.5, None, OP.mult)
+            else:
+                act(o, i, ACT.Copy, scale=0.5)
+        for h in (0, 1):
+            mine = (2, 3) if h == 0 else (2, 3, 0)
+            off = ("ko", 16 * h, 16 * h + 16)
+            for b in mine:
+                act(("ge", 1024 * h + 256 * b, 1024 * h + 256 * b + 256), ("gb", 64 * b, 64 * b + 64), ACT.Copy, off=off)
+            for b in [b for b in range(4) if b not in mine] + list(mine):
+                o = (new, 1024 * h + b, 1024 * h + 1024, 4)
+                if b in mine:
+                    vtt(o, (ps(HB[b]), 256 * h, 256 * h + 256), ("ge", 1024 * h + 256 * b, 1024 * h + 256 * b + 256), OP.add)
+                else:
+                    vtt(o, ("gb", 64 * b, 64 * b + 64), ("dd", 512 * b + 256 * h, 512 * b + 256 * h + 256), OP.add, off=off)
+        for h in (0, 1):
+            key_half(t + 1, new, h)
+
+    qx = "qx%d" % ROUNDS
+    for k in range(4):
+        dma("y", "ds", T.osc[4 * k:4 * k + 4, :], T[qx + "s"][32 * k:32 * k + 4, :], [R(qx)], [])
+    if not _PLAN:
+        _PLAN.extend(plan(ops, TRIES))
+    for i in _PLAN:
+        issue(ops[i])
+    count["ar0"] = count["ar1"] = arrive(0)
+    count["br0"] = count["br1"] = arrive(1)
+    for s in SEMAPHORES:
+        if count[s]:
+            wait("q", s, count[s])

@@ -6,9 +6,14 @@ ROUNDS = 2
 BIG = 2.0 ** 60
 M16 = 3072.0
 TRIES = 24
-VR = 108
-RW = 1032.0
-RS = 520.0
+SG = 3
+SR = 12 + 16 * SG
+RW = 775.5
+RS = 264.0
+FWD = 2
+STHR = (7, 8)
+CUTS = ((0, 256, 512), (0, 384, 512), (0, 384, 512))
+MINE = (((2, 3), (2, 3, 0)), ((2, 3), (2, 3, 0)))
 
 SCRATCH = {}
 
@@ -24,44 +29,49 @@ def _codes(names, n):
         SCRATCH[name + "s"] = ("sbuf", [128, n], "uint8")
 
 
-_b("xs st1 st2 ebt ebk dd sd ge", 2048)
-_b("us vs bt at zt gt vals lo lsw ltr sj", 512)
-_b("jk", 2560)
-_b("one nul idm blk upd lod prm", 128)
-_b("gw0 gw1 gw2", 8)
+_b("xs st1 st2 dd sd ge", 2048)
+_b("us vs at zt gt vals lsw ltr ktt prt own", 512)
+_b("sj", 1024)
+_b("bt zu zl ze zh", 528)
+_b("gw0", 8)
 _b("kc", 66)
-_b("ktt", 1248)
-_b("lt", 4096)
-_b("prt", 1024)
+_b("wtt", 576)
 _b("ot", 2080)
 _b("tt", 560)
-_b("msk0 msk1", 592)
-_b("sc", 2304)
+_b("dsr msk0 msk1", 592)
+_b("sc", 2112)
 _b("neg", 64)
-_b("own mm gb", 256)
+_b("mm gb", 256)
 _b("hi", 140)
+_b("lj lk", 32)
 _b("rw rv", 140, "float32")
 _b("kf yb", 512, "float32")
-_b("lj lk", 32, "float32")
-_b("kng", 8, "float32")
-_b("acc b5 cneg tb", 5, "float32")
+_b("cnt", 520, "float32")
+_b("cg ctr", 256, "float32")
+_b("kng", 32, "float32")
+_b("ci", 16, "float32")
 _b("em dm mk pk dum c16", 4, "float32")
-_b("icf icb wcl", 1, "float32")
+_b("c2", 2, "float32")
+_b("i4", 1, "float32")
 _b("ip ia", 1, "int32")
 _b("po ko l16", 32, "uint16")
+_b("cl16", 16, "uint16")
 _b("mk16 pk16", 4, "uint16")
-_codes("qu qv qb qa0 qa1 qz qg", 128)
-_codes("qx0 qx1 qx2 qw qe qh qr", 512)
-_codes("qk", 312)
-_codes("ql", 1280)
+_b("l2", 2, "uint16")
+_codes("qu qv qk qc qa0 qa1 qz qg", 128)
+_codes("qb qd", 130)
+_codes("qn", 144)
+_codes("qx0 qx1 qx2 qw qe qh", 512)
+_codes("ql", 1152)
 _codes("qo", 520)
 _codes("qt", 140)
 _codes("lc0 lc1", 448)
+_codes("lf0 lf1", 192)
 for _i in range(8):
     SCRATCH["ps%d" % _i] = ("psum", [128, 512], "float32")
 
-SEMAPHORES = ["cv", "cs", "ct", "cq", "ar0", "ar1", "br0", "br1", "sent",
-              "dx0", "dx1", "du", "dv", "dwc", "dws", "dlo", "dz0", "dz1", "dk0", "dk1", "dy0", "dy1", "do0", "do1", "ds"]
+SEMAPHORES = ["cv", "cs", "ct", "cq", "sa0", "sa1", "ca0", "ca1", "cb0", "cb1", "fw0", "fw1", "sent",
+              "dx0", "dx1", "du", "dv", "dwc", "dws", "dk0", "dk1", "dy0", "dy1", "do0", "do1", "ds"]
 
 _MASKS = {}
 _PLAN = []
@@ -248,9 +258,11 @@ def rank_program(g, core, T, topo):
     V, S, PE = g.vector, g.scalar, g.tensor
     ops = []
     CYC = 0.00083
+    own_calls = [0]
+    aside = []
 
     def emit(e, call, reads, writes, cost, sem=None, lat=None, pre=()):
-        ops.append({"e": e, "call": call, "reads": reads, "writes": writes, "sem": sem, "pre": list(pre),
+        ops.append({"e": e, "call": call, "reads": reads + aside, "writes": writes, "sem": sem, "pre": list(pre),
                     "hold": cost, "lat": cost if lat is None else lat})
 
     def R(name, a=0, b=None, st=1):
@@ -306,6 +318,8 @@ def rank_program(g, core, T, topo):
             a0 = a0.indirect(fa)
             rs.append(fr)
             cost = 0.05 + 1.5 * CYC * size(o)
+        elif i0[0][:2] != "ps":
+            cost = 0.05 + CYC * max(64, 1.5 * size(o))
         emit("v", lambda: V.tensor_tensor(oa, a0, a1, op), rs, [orr], cost)
 
     def vscan(o, mask, data):
@@ -332,16 +346,16 @@ def rank_program(g, core, T, topo):
         emit("v", lambda: V.quantize_mx(T[q][:, a:b], T[q + "s"][:, a:b], T[x][:, xa:xb]),
              [R(x, xa, xb)], [R(q, a, b)], 0.012 + 0.00022 * (xb - xa))
 
-    def act(o, i, f, bias=0.0, scale=1.0, off=None, accum=None, lat=None):
+    def act(o, i, f, bias=0.0, scale=1.0, off=None, accum=None, more=0.0, rs=(), ws=()):
         (oa, orr), (ia, ir) = both(o), both(i)
-        rs, ws = [ir], [orr]
+        rs, ws = [ir] + list(rs), [orr] + list(ws)
         if isinstance(bias, tuple):
             bias, r1 = both(bias)
             rs.append(r1)
         if isinstance(scale, tuple):
             scale, r1 = both(scale)
             rs.append(r1)
-        cost = 0.065 + CYC * size(o)
+        cost = 0.065 + CYC * size(o) + more
         if off:
             fa, fr = both(off)
             ia = ia.indirect(fa)
@@ -352,7 +366,7 @@ def rank_program(g, core, T, topo):
             ws.append(ar)
             emit("s", lambda: S.activation(oa, ia, f, bias=bias, scale=scale, accum_out=aa), rs, ws, cost + 0.02)
         else:
-            emit("s", lambda: S.activation(oa, ia, f, bias=bias, scale=scale), rs, ws, cost, lat=lat)
+            emit("s", lambda: S.activation(oa, ia, f, bias=bias, scale=scale), rs, ws, cost)
 
     def mm(ps, n, w, wa, x, xa, start=True, stop=True, pre=()):
         emit("t", lambda: PE.matmul_mx(T[ps][:, 0:n], T[w][:, wa:wa + 128], T[w + "s"][:, wa:wa + 128],
@@ -362,131 +376,135 @@ def rank_program(g, core, T, topo):
     def dma(q, sem, oap, iap, reads, writes, lat=1.5):
         emit(q, lambda: eng[q].dma_start(oap, iap), reads, writes, 0.06, sem=sem, lat=lat)
 
+    def mark():
+        own_calls[0] += 1
+        return ("@g", 1 << own_calls[0])
+
     def sel(o, i, pattern, cmp, fillv, base, cm):
         (oa, orr), (ia, ir) = both(o), both(i)
-        emit("q", lambda: g.affine_select(oa, ia, pattern, cmp, fillv, base, cm), [ir], [orr], 0.17 + 2 * CYC * size(o))
+        emit("q", lambda: g.affine_select(oa, ia, pattern, cmp, fillv, base, cm), [ir], [orr, mark()], 0.17 + 2 * CYC * size(o))
 
     def iota(o, pattern, base, cm):
         oa, orr = both(o)
         cost = 0.13 + 2 * CYC * size(o)
         if SCRATCH[o[0]][2] == "int32":
-            emit("q", lambda: g.iota(oa, pattern, base, cm), [], [orr], cost)
+            emit("q", lambda: g.iota(oa, pattern, base, cm), [], [orr, mark()], cost)
         else:
-            emit("q", lambda: g.iota(oa, pattern, base, cm, allow_small_or_imprecise_dtypes=True), [], [orr], cost)
+            emit("q", lambda: g.iota(oa, pattern, base, cm, allow_small_or_imprecise_dtypes=True), [], [orr, mark()], cost)
 
-    dma("y", "dx0", T.xs[:, 0:1024], T.x[:, 0:1024], [], [R("xs", 0, 1024)])
-    dma("s", "du", T.us[:, 0:512], T.u[:, 0:512], [], [R("us")])
-    dma("y", "dx1", T.xs[:, 1024:2048], T.x[:, 1024:2048], [], [R("xs", 1024, 2048)], lat=2.0)
-
-    fill(("one",), 1.0)
-    fill(("gw0",), 0.0)
-    fill(("nul",), 0.0)
-    fill(("prt",), 0.0)
-    fill(("ktt",), 0.0)
-    fill(("rw", 0, VR), RW)
-    fill(("rw", VR, 140), RS)
-    fill(("neg",), -BIG)
-    for h in (0, 1):
-        dma("y", "dz%d" % h, T.ebt[:, 1024 * h:1024 * h + 1024], T.prt[:, 0:1024], [R("prt")],
-            [R("ebt", 1024 * h, 1024 * h + 1024)], lat=2.5)
-        act(("ebk", 1024 * h, 1024 * h + 1024), ("prt",), ACT.Copy)
+    dma("y", "dx0", T.xs[:, 0:1024], T.x[:, 0:1024], [], [R("xs", 0, 1024)], lat=2.2)
+    dma("s", "du", T.us[:, 0:512], T.u[:, 0:512], [], [R("us")], lat=2.0)
+    dma("y", "dx1", T.xs[:, 1024:2048], T.x[:, 1024:2048], [], [R("xs", 1024, 2048)], lat=2.8)
     dma("y", "dwc", T.qw[:, 0:512].bitcast(dt.uint8), T.wc[:, 0:2048], [], [R("qw")], lat=4.0)
     dma("y", "dws", T.qws[:, 0:512], T.ws[:, 0:512], [], [R("qws")], lat=4.0)
     dma("y", "dv", T.vs[:, 0:512], T.v[:, 0:512], [], [R("vs")], lat=4.0)
+
+    iota(("dsr",), [[1, 592]], -3, -4)
+    act(("zu", 0, 516), ("dsr", 0, 516), ACT.Sigmoid, bias=-128.0, scale=256.0, more=1.3, ws=[("@s", 1)])
+    act(("zl", 0, 516), ("dsr", 0, 516), ACT.Sigmoid, bias=-128.0, scale=-256.0, rs=[("@s", 1)])
+    sel(("zu", 3, 515, 4), ("zu", 3, 515, 4), [[-1, 128]], OP.not_equal, 512.0, 0, 1)
+    sel(("zl", 3, 515, 4), ("zl", 3, 515, 4), [[-1, 128]], OP.not_equal, -512.0, 0, 1)
+    vts(("ze", 0, 516), ("dsr", 0, 516), 0.0, None, OP.is_equal)
+    for c in range(4):
+        quant("ql", 128 + 128 * c, 256 + 128 * c, "zu", 3 - c, 515 - c)
+        quant("ql", 640 + 128 * c, 768 + 128 * c, "zl", 3 - c, 515 - c)
+        quant("qe", 128 * c, 128 + 128 * c, "ze", 3 - c, 515 - c)
+    fill(("gw0",), 0.0)
+    fill(("ktt",), 0.0)
+    fill(("prt",), 0.0)
+    fill(("rw", 0, SR), RS)
+    fill(("rw", SR, 140), RW)
+    fill(("bt", 512, 528), 0.0)
+    fill(("sc", 512, 2112, 528), 0.0)
     for i in range(6):
         sel(("gw0",), ("gw0",), [[-16, 8]], OP.not_equal, 2.0 ** (i - 1), -i, 1)
-    sel(("gw1",), ("gw0",), [[16, 8]], OP.is_ge, 0.0, 1, -1)
-    sel(("gw2",), ("gw0",), [[-16, 8]], OP.is_ge, 0.0, -2, 1)
-    sel(("upd",), ("one",), [[1, 128]], OP.is_gt, 0.0, 0, -1)
-    sel(("upd",), ("upd",), [[1, 128]], OP.not_equal, 1024.0, 0, -1)
-    sel(("lod",), ("one",), [[-1, 128]], OP.is_gt, 0.0, 0, 1)
-    sel(("lod",), ("lod",), [[-1, 128]], OP.not_equal, -1024.0, 0, 1)
-    iota(("kc", 0, 65), [[1, 65]], -32, 0)
-    sel(("blk",), ("one",), [[-16, 8], [0, 16]], OP.is_ge, 0.0, 0, 1)
-    sel(("blk",), ("blk",), [[16, 8], [0, 16]], OP.is_ge, 0.0, 15, -1)
-    sel(("idm",), ("one",), [[-1, 128]], OP.is_equal, 0.0, 0, 1)
-    sel(("prm",), ("one",), [[-1, 4], [-4, 32]], OP.is_equal, 0.0, 0, 1)
-    iota(("ip",), [[0, 1]], 0, 1)
-    iota(("cneg",), [[-1, 5]], 0, 0)
-    iota(("c16",), [[16, 4]], 513, 0)
-    iota(("lo",), [[0, 2], [1, 256]], 0, 0)
-    iota(("vals",), [[256, 2], [0, 256]], 0, 0)
     for b in range(4):
-        iota(("sc", 576 * b + 512, 576 * b + 576), [[0, 64]], 0, 0)
+        vcopy(("ktt", 5 * b, 128, 16), ("gw0",))
+    quant("qk", 0, 128, "ktt", 0, 512)
+    quant("qu", 0, 128, "us", 0, 512)
+    iota(("kc", 0, 65), [[1, 65]], -32, 0)
+    sel(("prt", 0, 512, 4), ("prt", 0, 512, 4), [[-1, 4], [-4, 32]], OP.not_equal, 0.0625, 0, 1)
+    sel(("prt", 1, 512, 4), ("prt", 1, 512, 4), [[-1, 4], [-4, 32]], OP.not_equal, 32.0, 0, 1)
+    quant("ql", 0, 128, "prt", 0, 512)
+    iota(("tt", 2, 560, 4), [[0, 140]], 0, 0)
+    iota(("tt", 3, 560, 4), [[0, 140]], 0, 0)
+    iota(("vals",), [[1, 512]], -256, 0)
+    iota(("ip",), [[0, 1]], 0, 1)
+    iota(("c2",), [[2, 2]], 0, 0)
+    iota(("c16",), [[64, 4]], 4 * 513, 0)
+    iota(("ci",), [[4, 2], [64, 4], [1, 2]], 0, 0)
+    vts(("ia",), ("ip",), 15, None, OP.bitwise_and)
+    vts(("i4",), ("ia",), 4.0, None, OP.mult)
+    for a in range(4):
+        emit("v", lambda a=a: V.tensor_scalar(T.cl16[32 * a:32 * a + 32, :], T.ci[32 * a:32 * a + 32, :], T.i4[32 * a:32 * a + 32, :],
+                                              260.0 * (a // 2) + 2.0 * (a % 2), OP.add, OP.add),
+             [R("ci"), R("i4")], [("cl16", 1 << a)], 0.1)
+    vts(("l2",), ("c2",), ("i4",), 8.0, OP.add, OP.mult)
+    vts(("dum",), ("c16",), ("i4",), 0.25, OP.add, OP.mult)
+    sel(("msk0",), ("dsr",), [[0, 592]], OP.is_gt, BIG, -1, 0)
+    sel(("neg",), ("dsr", 0, 64), [[0, 64]], OP.is_gt, -BIG, -1, 0)
     for n in ("at", "zt", "gt"):
         iota((n, 256, 512), [[0, 256]], 0, 0)
-    dma("y", "dlo", T.vals[1:128:16, :], T.lo[1:128:16, :], [R("lo")], [R("vals")])
+    iota(("wtt",), [[0, 576]], 0, 0)
 
-    for b in range(4):
-        act(("ktt", 5 * b, 128, 16), ("gw0",), ACT.Copy)
-        act(("ktt", 128 + 48 + 5 * b, 688, 64), ("gw1",), ACT.Copy, scale=16.0)
-        act(("ktt", 688 + 48 + 5 * b, 1248, 64), ("gw2",), ACT.Copy, scale=0.25)
-    quant("qk", 0, 312, "ktt", 0, 1248)
-    quant("qu", 0, 128, "us", 0, 512)
-    for c in range(4):
-        for s, d in ((0, "upd"), (1, "lod")):
-            for b in range(4):
-                x = ("lt", 2048 * s + 512 * c + b, 2048 * s + 512 * c + 512, 4)
-                w = 0.5 if b == 3 else 1.0
-                if b == c:
-                    vts(x, (d,), w, None, OP.mult)
-                elif c < 3:
-                    fill(x, w if (s == 0) == (b < c) else 0.0)
-                else:
-                    act(x, ("one" if (s == 0) == (b < c) else "nul",), ACT.Copy)
-            quant("ql", 256 + 512 * s + 128 * c, 384 + 512 * s + 128 * c, "lt", 2048 * s + 512 * c, 2048 * s + 512 * c + 512)
-    vreduce(("wcl",), ("gw0",), OP.add)
-    for b in range(4):
-        vcopy(("ebt", 512 * b + b, 512 * b + 512, 4), ("idm",))
-    quant("qe", 0, 512, "ebt", 0, 2048)
-    for b in range(4):
-        act(("ebk", 512 * b + b, 512 * b + 512, 4), ("blk",), ACT.Identity, scale=("wcl",))
-    quant("qr", 0, 512, "ebk", 0, 2048)
-    act(("prt", 0, 512, 4), ("prm",), ACT.Copy, scale=0.0625)
-    act(("prt", 1, 512, 4), ("prm",), ACT.Copy, scale=32.0)
-    act(("prt", 514, 1024, 4), ("prm",), ACT.Copy)
-    act(("prt", 515, 1024, 4), ("prm",), ACT.Copy)
-    quant("ql", 0, 256, "prt", 0, 1024)
-    vts(("ia",), ("ip",), 15, None, OP.bitwise_and)
-    vcopy(("icf",), ("ia",))
-    vts(("icb",), ("icf",), -4.0, 0.5, OP.mult, OP.add)
-    vts(("tb",), ("cneg",), ("icb",), None, OP.add)
-    vts(("dum",), ("c16",), ("icf",), None, OP.add)
-    fill(("msk0",), BIG)
-    fill(("msk1",), BIG)
+    def other(x):
+        return T.cores[rank ^ x]
+    near = [x for x in range(1, N) if topo.chip(other(x)) == topo.chip(core)][0]
 
-    lots = ((1, 2, 4, 6), (3, 5, 7))
-    near = [x for x in range(1, N) if topo.chip(T.cores[rank ^ x]) == topo.chip(core)]
-    far = [x for x in range(1, N) if x not in near]
-    fmask = topo.mask(core, T.cores[rank ^ far[0]])
-    nmask = topo.mask(core, T.cores[rank ^ near[0]]) & ~fmask
+    def hops(x):
+        a, b = topo.chip(core), topo.chip(other(x))
+        return 0 if topo.mates(a, b) else 1 if topo.same_plane(a, b) else 2
+    level = sorted([x for x in range(1, N) if x != near and topo.die(other(x)) == topo.die(core)], key=lambda x: -hops(x))
+    handed = level[:FWD]
+    late = level[FWD:] + [x ^ near for x in level[FWD:]]
+    first = handed + [near]
+    slot = {x: 64 * k for k, x in enumerate(first + late)}
+    fmask = topo.mask(core, other(level[0]))
+    nmask = topo.mask(core, other(near)) & ~fmask
+    nf, nn = bin(fmask).count("1"), bin(nmask).count("1")
+    arrive = {"sa": nf * (len(handed) + len(late)) + nn, "ca": nf * len(handed) + nn, "cb": nf * len(late),
+              "fw": 2 * nn if handed else 0}
 
-    def arrive(lot):
-        return sum(2 * bin(nmask if x in near else fmask).count("1") for x in lots[lot])
+    def view(name, a, b, plane):
+        return T[name + "s"][:, a:b] if plane else T[name][:, a:b].bitcast(dt.uint8)
+
+    def dst(x):
+        rid, pid = topo.addr(other(x))[:2]
+        return DstId(rid=rid, pnc=pid)
 
     def send(t):
-        qa, lc = "qa%d" % t, "lc%d" % t
+        qa, lc, lf = "qa%d" % t, "lc%d" % t, "lf%d" % t
 
-        def call(lot, plane):
+        def call(xs, plane, sem):
             ts = []
-            for group, m in ((far, fmask), (near, nmask)):
-                ids, dsts = [], []
-                for x in lots[lot]:
-                    if x in group:
-                        rid, pid = topo.addr(T.cores[rank ^ x])[:2]
-                        c = 256 * lot + 64 * lots[lot].index(x)
-                        ids.append(DstId(rid=rid, pnc=pid))
-                        dsts.append(T[lc + "s"][:, c:c + 64] if plane else T[lc][:, c:c + 64].bitcast(dt.uint8))
-                if ids:
-                    src = T[qa + "s"][:, 0:64] if plane else T[qa][:, 0:64].bitcast(dt.uint8)
-                    ts.append(RemoteDMATransfer(dst_ids=ids, dma_engine_mask=m, remote_sem=T.sem["%sr%d" % ("ab"[lot], t)],
-                                                srcs=[src], dsts=dsts))
+            for group, m in (([x for x in xs if x != near], fmask), ([x for x in xs if x == near], nmask)):
+                if group:
+                    ts.append(RemoteDMATransfer(dst_ids=[dst(x) for x in group], dma_engine_mask=m, remote_sem=T.sem[sem],
+                                                srcs=[view(qa, 0, 64, plane)],
+                                                dsts=[view(lc, slot[x], slot[x] + 64, plane) for x in group]))
                     count["sent"] += bin(m).count("1")
             g.remote_dma_fused(ts, local_sem=T.sem.sent)
-        for lot in (0, 1):
-            for plane in (0, 1):
-                emit("q", lambda lot=lot, plane=plane: call(lot, plane), [R(qa)], [("@q", 1), ("@w%d" % lot, 1)], 0.4, sem="sent")
-            emit("n", None, [("@w%d" % lot, 1)], [R(lc, 256 * lot, 256 + 192 * lot)], 0.0, lat=2.5 + 1.5 * lot)
+
+        def hand(plane):
+            w = 64 * len(handed)
+            g.remote_dma_fused([RemoteDMATransfer(dst_ids=[dst(near)], dma_engine_mask=nmask, remote_sem=T.sem["fw%d" % t],
+                                                  srcs=[view(lc, 0, w, plane)], dsts=[view(lf, 0, w, plane)])],
+                               local_sem=T.sem.sent)
+            count["sent"] += nn
+        every = ("@g", (1 << own_calls[0] + 1) - 1)
+        emit("q", lambda: call(first + late, 1, "sa%d" % t), [R(qa), every], [("@q", 1), ("@ws", 1)], 0.4, sem="sent")
+        emit("q", lambda: call(first, 0, "ca%d" % t), [R(qa)], [("@q", 1), ("@wa", 1)], 0.4, sem="sent")
+        if late:
+            emit("q", lambda: call(late, 0, "cb%d" % t), [R(qa)], [("@q", 1), ("@wb", 1)], 0.4, sem="sent")
+        emit("n", None, [("@ws", 1)], [("@as", 1)], 0.0, lat=2.0)
+        emit("n", None, [("@wa", 1)], [R(lc, 0, 64 * len(first))], 0.0, lat=2.6)
+        if late:
+            emit("n", None, [("@wb", 1)], [R(lc, 64 * len(first), 448)], 0.0, lat=3.2)
+        if handed:
+            emit("q", lambda: hand(1), [("@as", 1)], [("@q", 1)], 0.4, sem="sent", pre=[("sa%d" % t, arrive["sa"])])
+            emit("q", lambda: hand(0), [R(lc, 0, 64 * len(first))], [("@q", 1), ("@wf", 1)], 0.4, sem="sent",
+                 pre=[("ca%d" % t, arrive["ca"])])
+            emit("n", None, [("@wf", 1)], [R(lf)], 0.0, lat=1.5)
 
     def ps(i):
         return "ps%d" % i
@@ -494,130 +512,149 @@ def rank_program(g, core, T, topo):
 
     def key_half(t, state, h):
         qx = "qx%d" % t
-        quant(qx, 256 * h, 256 * h + 256, state, 1024 * h, 1024 * h + 1024)
+        a, z = CUTS[t][h], CUTS[t][h + 1]
+        quant(qx, a, z, state, 4 * a, 4 * z)
         if t < ROUNDS:
-            mm(ps(h), 256, "qu", 0, qx, 256 * h)
-            act(("bt", 256 * h, 256 * h + 256), (ps(h), 0, 256), ACT.Sign, bias=-(2.0 ** -100))
+            mm(ps(h), z - a, "qu", 0, qx, a)
+            act(("bt", a, z), (ps(h), 0, z - a), ACT.Sign, bias=-(2.0 ** -100))
         else:
-            mm(ps(h), 256, "qv", 0, qx, 256 * h)
-            act(("yb", 256 * h, 256 * h + 256), (ps(h), 0, 256), ACT.Copy)
-            dma("y", "do%d" % h, T.oc[:, 1024 * h:1024 * h + 1024], T[qx][:, 256 * h:256 * h + 256].bitcast(dt.uint8),
-                [R(qx, 256 * h, 256 * h + 256)], [])
-            dma("s", "dy%d" % h, T.y[:, 256 * h:256 * h + 256], T.yb[:, 256 * h:256 * h + 256],
-                [R("yb", 256 * h, 256 * h + 256)], [])
+            mm(ps(h), z - a, "qv", 0, qx, a)
+            act(("yb", a, z), (ps(h), 0, z - a), ACT.Copy)
+            dma("y", "do%d" % h, T.oc[:, 4 * a:4 * z], T[qx][:, a:z].bitcast(dt.uint8), [R(qx, a, z)], [])
+            dma("s", "dy%d" % h, T.y[:, a:z], T.yb[:, a:z], [R("yb", a, z)], [])
 
     key_half(0, "xs", 0)
     key_half(0, "xs", 1)
     for t in range(ROUNDS):
-        qx, qa, lc = "qx%d" % t, "qa%d" % t, "lc%d" % t
+        qx, qa, lc, lf = "qx%d" % t, "qa%d" % t, "lc%d" % t, "lf%d" % t
         new = "st%d" % (t + 1)
-        quant("qb", 0, 128, "bt", 0, 512)
+        quant("qb", 0, 130, "bt", 0, 520)
+        mm("ps3", 128, "qb", 0, "qk", 0)
         mm("ps2", 128, "qb", 0, "qk", 0)
-        mm("ps3", 280, "qb", 0, "qk", 32)
-        act(("tt", 2, 560, 4), ("ps3", 0, 140), ACT.Copy)
-        act(("tt", 3, 560, 4), ("ps3", 140, 280), ACT.Copy)
-        for b in range(4):
-            mm(ps(6 + b % 2), 512, "qe", 128 * b, qx, 0)
-            act(("dd", 512 * b, 512 * b + 512), (ps(6 + b % 2), 0, 512), ACT.Copy, scale=0.5)
-        act(("kng",), ("ps2", 3, 32, 4), ACT.Copy, scale=-1.0)
+        act(("kng",), ("ps3", 0, 32), ACT.Copy, scale=-256.0)
         for h in (0, 1):
-            for gg in range(4):
-                for b in range(4):
-                    c = 4 * (4 * h + gg) + b
-                    o = ("ot", 1040 * h + 4 * gg + b, 1040 * h + 1040, 16)
-                    if b == 3:
-                        act(o, ("kc", 0, 65), ACT.Sign, bias=("kng", c // 4, c // 4 + 1))
-                    else:
-                        vts(o, ("kc", 0, 65), ("ps2", c, c + 1), 0.5, OP.is_gt, OP.subtract)
+            for z in range(16):
+                c = 16 * h + z
+                o = ("ot", 1040 * h + z, 1040 * h + 1040, 16)
+                if z >= 16 - STHR[h]:
+                    act(o, ("kc", 0, 65), ACT.Sigmoid, bias=("kng", c, c + 1), scale=256.0, rs=[("@s", 1)])
+                else:
+                    vts(o, ("kc", 0, 65), ("ps2", c, c + 1), None, OP.is_gt)
             quant("qo", 260 * h, 260 * h + 260, "ot", 1040 * h, 1040 * h + 1040)
-        for b in range(4):
-            mm("ps3", 128, "qr", 128 * b, "qb", 0)
-            act(("kf", b, 512, 4), ("ps3", 0, 128), ACT.Identity, bias=31.5)
-        for c in range(5):
-            act(("jk", 512 * c, 512 * c + 512), ("kf",), ACT.Sign, bias=("tb", c, c + 1), accum=("acc", c, c + 1))
-        act(("b5",), ("acc",), ACT.Copy, bias=256.0, scale=-0.5, lat=0.8)
-        dma("y", "dk%d" % t, T.kl[8 * t:8 * t + 8, :], T.kf[0:128:16, :], [R("kf")], [])
         for h in (0, 1):
             for c in range(4):
-                p = ps(((0, 1, 4, 5), (0, 1, 4, 2))[h][c])
-                mm(p, 256, "ql", 256 + 128 * c, "qo", 260 * h + 4, True, False)
-                mm(p, 256, "ql", 768 + 128 * c, "qo", 260 * h, False, True)
+                p = ps(4 * (1 - h) + c)
+                mm(p, 256, "ql", 128 + 128 * c, "qo", 260 * h + 4, True, False)
+                mm(p, 256, "ql", 640 + 128 * c, "qo", 260 * h, False, True)
                 for gg in range(4):
                     k = 12 + 16 * (4 * h + gg) + c
-                    if k < VR:
+                    if k >= SR:
                         vreduce(("rw", k, k + 1), (p, gg, 256, 4), OP.max)
                     else:
-                        z = 64 * (2 * c + gg - 2)
-                        act(("sj", z, z + 64), (p, gg, 256, 4), ACT.Relu, bias=-512.0, accum=("rw", k, k + 1))
+                        z = 64 * (4 * gg + c)
+                        act(("sj", z, z + 64), (p, gg, 256, 4), ACT.Relu, bias=-511.5, accum=("rw", k, k + 1))
         for o in ("hi", "rv"):
-            vts((o, 0, VR), ("rw", 0, VR), M16 - RW, None, OP.add)
-            act((o, VR, 140), ("rw", VR, 140), ACT.Identity, bias=M16 - RS)
-        vts(("tt", 0, 560, 4), ("hi",), M16, None, OP.subtract)
+            act((o, 0, SR), ("rw", 0, SR), ACT.Identity, bias=M16 - RS)
+            vts((o, SR, 140), ("rw", SR, 140), M16 - RW, None, OP.add)
+        act(("tt", 0, 560, 4), ("hi",), ACT.Identity, bias=-M16)
         vtt(("tt", 1, 560, 4), ("rv",), ("hi",), OP.subtract)
         quant("qt", 0, 140, "tt", 0, 560)
         for q in range(4):
             mm("ps0", 128, "qt", 12 - 4 * q, "ql", 32 * q, q == 0, q == 3)
-        for q in range(4):
-            mm("ps1", 128, "qt", 12 - 4 * q, "ql", 128 + 32 * q, q == 0, q == 3)
         vts(("po",), ("ps0", 0, 32), 256.0, None, OP.add)
-        vts(("ko",), ("ps1", 0, 32), 31.5, None, OP.add)
+        for h in (0, 1):
+            p = ps(4 + h)
+            mm(p, 260, "ql", 128, "qo", 260 * h, True, False)
+            mm(p, 260, "ql", 640, "qo", 260 * h, False, False)
+            mm(p, 260, "qe", 0, "qo", 260 * h, False, True)
+            act(("cnt", 260 * h, 260 * h + 260), (p, 0, 260), ACT.Copy)
+        act(("cg",), ("cnt",), ACT.Copy, off=("cl16",))
+        vtrans(("ctr",), ("cg",))
+        for b in range(4):
+            mm(ps(6 + b % 2), 512, "qe", 128 * b, qx, 0)
+            act(("dd", 512 * b, 512 * b + 512), (ps(6 + b % 2), 0, 512), ACT.Copy, scale=0.5)
         msk = "msk%d" % t
-        vtt(("em",), ("b5", 1, 5), ("b5", 0, 4), OP.is_equal)
+        lo, up = ("ctr", 0, 128, 32), ("ctr", 128, 256, 32)
+        vtt(("em",), up, lo, OP.is_equal)
         vtt(("dm",), ("em",), ("dum",), OP.mult)
-        vtt(("mk",), ("b5", 0, 4), ("dm",), OP.max)
-        vtt(("pk",), ("b5", 1, 5), ("dm",), OP.max)
+        vtt(("mk",), lo, ("dm",), OP.max)
+        vtt(("pk",), up, ("dm",), OP.max)
         vcopy(("mk16",), ("mk",))
-        vts(("pk16",), ("pk",), 1.0, None, OP.subtract)
+        vts(("pk16",), ("pk",), 1.0, 512.0, OP.subtract, OP.min)
         vscatter((msk,), ("neg",), ("mk16",))
         vscatter(("lsw",), ("vals",), ("po",))
         vtrans(("ltr",), ("lsw",))
-        for gg in (0, 1):
-            vtt(("lj", 16 * gg, 16 * gg + 16), ("ltr", 16 * gg, 512, 32), ("ltr", 16 * gg + 1, 512, 32), OP.add)
+        vgather(("lj",), ("ltr",), ("l2",))
         vtrans(("lk",), ("lj",))
-        vcopy(("l16",), ("lk",))
-        for b in (0, 2, 1, 3):
-            o, i = ("sd", 512 * b, 512 * b + 512), ("dd", 512 * b, 512 * b + 512)
-            if b < 2:
-                vgather(o, i, ("l16",))
-            else:
-                act(o, i, ACT.Copy, off=("l16",))
-        for b in (0, 2, 1, 3):
-            vscan(("sc", 576 * b, 576 * b + 512), (msk, 0, 512), ("sd", 512 * b, 512 * b + 512))
-            o, i = ("at", b, 256, 4), ("sc", 576 * b, 576 * b + 576)
-            if b < 3:
+        vts(("l16",), ("lk",), 256.0, None, OP.add)
+        vgather(("sd", 0, 512), ("dd", 0, 512), ("l16",))
+        vgather(("sd", 512, 768), ("dd", 512, 1024), ("l16", 0, 16))
+        for b in (2, 3):
+            act(("sd", 512 * b, 512 * b + 512), ("dd", 512 * b, 512 * b + 512), ACT.Copy, off=("l16",))
+        act(("sd", 768, 1024), ("dd", 512, 1024), ACT.Copy, off=("l16", 16, 32))
+        for b in (0, 2, 3, 1):
+            vscan(("sc", 528 * b, 528 * b + 512), (msk, 0, 512), ("sd", 512 * b, 512 * b + 512))
+            o, i = ("at", b, 256, 4), ("sc", 528 * b, 528 * b + 513)
+            if b != 1:
                 act(o, i, ACT.Copy, scale=2.0, off=("pk16",))
             else:
                 vts(o, i, 2.0, None, OP.mult, off=("pk16",))
         quant(qa, 0, 128, "at", 0, 512)
         send(t)
+        aside.append(("@ws", 1))
         for b in range(4):
             mm(ps(b), 128, "qe", 128 * b, qa, 0)
         for b in range(4):
-            act(("own", 64 * b, 64 * b + 64), (ps(b), 0, 64), ACT.Copy)
+            for s in (0, 1):
+                act(("own", 256 * s + b, 256 * s + 256, 4), (ps(b), 0, 64), ACT.Copy)
         if t == 0:
             for b in range(4):
-                act(("ebt", 512 * b + b, 512 * b + 512, 4), ("idm",), ACT.Copy, scale=0.5)
+                act(("wtt", 48 + 5 * b, 560, 64), ("gw0",), ACT.Copy)
+            quant("qn", 0, 144, "wtt", 0, 576)
+            vts(("zh", 0, 516), ("ze", 0, 516), 0.5, None, OP.mult)
+            for c in range(4):
+                quant("qh", 128 * c, 128 + 128 * c, "zh", 3 - c, 515 - c)
             quant("qv", 0, 128, "vs", 0, 512)
-            quant("qh", 0, 512, "ebt", 0, 2048)
+            fill(("msk1",), BIG)
+        quant("qd", 0, 130, "bt", 4, 524)
+        quant("qc", 0, 128, "bt", 1, 513)
+        for q in range(4):
+            mm("ps7", 128, "qn", 12 - 4 * q, "qd" if q % 2 else "qb", q - q % 2, q == 0, q == 3)
+        vts(("ko",), ("ps7", 0, 128, 4), 31.5, None, OP.add)
+        for b in range(4):
+            mm(ps(b), 128, "qn", 12 + b - b % 2, "qc" if b % 2 else "qb", 0)
+            act(("kf", b, 512, 4), (ps(b), 0, 128), ACT.Identity, bias=31.5)
+        dma("y", "dk%d" % t, T.kl[8 * t:8 * t + 8, :], T.kf[0:128:16, :], [R("kf")], [])
         for b in (2, 3, 0):
             mm(ps(HB[b]), 512, "qh", 128 * b, qx, 0)
-        for b in range(4):
-            mm(ps(b), 256, "qe", 128 * b, lc, 0, pre=[("ar%d" % t, arrive(0))])
-        for s in range(4):
+        aside.pop()
+        lots = [(lc, 0, len(first), ("sa", "ca")), (lc, 64 * len(first), len(late), ("cb",)), (lf, 0, len(handed), ("fw",))]
+        lots = [x for x in lots if x[2]]
+        for z, (buf, a, n, sems) in enumerate(lots):
             for b in range(4):
-                o, w = ("mm", 64 * b, 64 * b + 64), ("own" if s == 0 else "mm", 64 * b, 64 * b + 64)
-                vtt(o, (ps(b), 64 * s, 64 * s + 64), w, OP.max)
-        for b in range(4):
-            mm(ps(b), 192, "qe", 128 * b, lc, 256, pre=[("br%d" % t, arrive(1))])
-        for s in range(3):
-            for b in range(4):
-                w = ("mm", 64 * b, 64 * b + 64)
-                vtt(("zt", b, 256, 4) if s == 2 else w, (ps(b), 64 * s, 64 * s + 64), w, OP.max)
+                mm(ps(b), 64 * n, "qe", 128 * b, buf, a, pre=[(s + str(t), arrive[s]) for s in sems])
+            if z < len(lots) - 1:
+                for s in range(0, n, 2):
+                    k = min(2, n - s)
+                    for b in range(4):
+                        w = ("own", b, 256 * k, 4)
+                        vtt(w, (ps(b), 64 * s, 64 * (s + k)), w, OP.max)
+                if z == len(lots) - 2:
+                    vtt(("mm",), ("own", 0, 256), ("own", 256, 512), OP.max)
+            else:
+                for s in range(n):
+                    for b in range(4):
+                        w = ("mm", b, 256, 4)
+                        vtt(("zt", b, 256, 4) if s == n - 1 else w, (ps(b), 64 * s, 64 * s + 64), w, OP.max)
         quant("qz", 0, 128, "zt", 0, 512)
-        for b in range(4):
+        for b in (0, 2, 1, 3):
             mm(ps(b), 128, "qw", 128 * b, "qz", 0)
-        for b in range(4):
-            vts(("gt", b, 256, 4), (ps(b), 0, 64), 0.0, 0.015625, OP.max, OP.mult)
+        for b in (0, 2, 1, 3):
+            o, i = ("gt", b, 256, 4), (ps(b), 0, 64)
+            if b in (0, 1):
+                act(o, i, ACT.Relu, scale=0.015625)
+            else:
+                vts(o, i, 0.0, 0.015625, OP.max, OP.mult)
         quant("qg", 0, 128, "gt", 0, 512)
         for b in (0, 2, 1, 3):
             mm(ps(b), 128, "qe", 128 * b, "qg", 0)
@@ -628,16 +665,17 @@ def rank_program(g, core, T, topo):
             else:
                 act(o, i, ACT.Copy, scale=0.5)
         for h in (0, 1):
-            mine = (2, 3) if h == 0 else (2, 3, 0)
-            off = ("ko", 16 * h, 16 * h + 16)
+            mine = MINE[t][h]
+            a, z = CUTS[t + 1][h], CUTS[t + 1][h + 1]
+            off = ("ko", a // 16, z // 16)
             for b in mine:
-                act(("ge", 1024 * h + 256 * b, 1024 * h + 256 * b + 256), ("gb", 64 * b, 64 * b + 64), ACT.Copy, off=off)
+                act(("ge", 512 * b + a, 512 * b + z), ("gb", 64 * b, 64 * b + 64), ACT.Copy, off=off)
             for b in [b for b in range(4) if b not in mine] + list(mine):
-                o = (new, 1024 * h + b, 1024 * h + 1024, 4)
+                o = (new, 4 * a + b, 4 * z, 4)
                 if b in mine:
-                    vtt(o, (ps(HB[b]), 256 * h, 256 * h + 256), ("ge", 1024 * h + 256 * b, 1024 * h + 256 * b + 256), OP.add)
+                    vtt(o, (ps(HB[b]), a, z), ("ge", 512 * b + a, 512 * b + z), OP.add)
                 else:
-                    vtt(o, ("gb", 64 * b, 64 * b + 64), ("dd", 512 * b + 256 * h, 512 * b + 256 * h + 256), OP.add, off=off)
+                    vtt(o, ("gb", 64 * b, 64 * b + 64), ("dd", 512 * b + a, 512 * b + z), OP.add, off=off)
         for h in (0, 1):
             key_half(t + 1, new, h)
 
@@ -648,8 +686,9 @@ def rank_program(g, core, T, topo):
         _PLAN.extend(plan(ops, TRIES))
     for i in _PLAN:
         issue(ops[i])
-    count["ar0"] = count["ar1"] = arrive(0)
-    count["br0"] = count["br1"] = arrive(1)
+    for t in range(ROUNDS):
+        for s in arrive:
+            count[s + str(t)] = arrive[s]
     for s in SEMAPHORES:
         if count[s]:
             wait("q", s, count[s])

@@ -5,15 +5,25 @@ OP, ACT, AX = AluOpType, ActivationFunctionType, AxisListType
 ROUNDS = 2
 BIG = 2.0 ** 60
 M16 = 3072.0
-TRIES = 24
-SG = 3
+TRIES = 8
+STEPS = 60000
+HEAT = 0.3
+CASES = ((1.0, 1.1, 0.1, 1.0, 1.0, 1.0), (1.1, 1.2, 0.2, 1.3, 1.25, 1.6), (1.3, 1.8, 0.15, 1.0, 1.0, 1.2),
+         (1.0, 1.0, 0.12, 0.8, 0.75, 0.6))
+SG = 4
 SR = 12 + 16 * SG
 RW = 775.5
 RS = 264.0
-FWD = 2
-STHR = (7, 8)
-CUTS = ((0, 256, 512), (0, 384, 512), (0, 384, 512))
+STHR = (5, 4, 2, 2)
+CUTS = ((0, 384, 512), (0, 384, 512), (0, 384, 512))
 MINE = (((2, 3), (2, 3, 0)), ((2, 3), (2, 3, 0)))
+FWD = 2
+SLOTS = "nhlf"
+CALLS = ((0, "h", 4, "ca"), (1, "hl", 4, "sa"), (0, "l", 0, "cb"), (1, "f", 0, "fa"))
+LATS = (2.2, 2.4, 2.6, 2.5)
+HANDS = ((0, "h", 8, "ca", "fa"),)
+LOTS = ((0, 2, ("sa", "ca")), (2, 2, ("cb",)), (4, 2, ("fa",)))
+WIDE = 2
 
 SCRATCH = {}
 
@@ -30,47 +40,45 @@ def _codes(names, n):
 
 
 _b("xs st1 st2 dd sd ge", 2048)
-_b("us vs at zt gt vals lsw ltr ktt prt own", 512)
+_b("us vs at zt gt vals lsw ltr prt own bu kx one", 512)
+_b("hor", 128)
 _b("sj", 1024)
-_b("bt zu zl ze zh", 528)
+_b("dsr bt zu zl ze zh", 528)
 _b("gw0", 8)
-_b("kc", 66)
+_b("kc kn", 66)
 _b("wtt", 576)
 _b("ot", 2080)
 _b("tt", 560)
-_b("dsr msk0 msk1", 592)
+_b("msk0 msk1", 1104)
 _b("sc", 2112)
 _b("neg", 64)
-_b("mm gb", 256)
+_b("mm gb cg ctr", 256)
 _b("hi", 140)
 _b("lj lk", 32)
 _b("rw rv", 140, "float32")
 _b("kf yb", 512, "float32")
 _b("cnt", 520, "float32")
-_b("cg ctr", 256, "float32")
-_b("kng", 32, "float32")
 _b("ci", 16, "float32")
 _b("em dm mk pk dum c16", 4, "float32")
 _b("c2", 2, "float32")
-_b("i4", 1, "float32")
-_b("ip ia", 1, "int32")
+_b("i2 i3", 1, "float32")
+_b("ip ia ib", 1, "int32")
 _b("po ko l16", 32, "uint16")
 _b("cl16", 16, "uint16")
 _b("mk16 pk16", 4, "uint16")
 _b("l2", 2, "uint16")
-_codes("qu qv qk qc qa0 qa1 qz qg", 128)
+_codes("qu qv qc qz qg qj", 128)
 _codes("qb qd", 130)
 _codes("qn", 144)
 _codes("qx0 qx1 qx2 qw qe qh", 512)
 _codes("ql", 1152)
 _codes("qo", 520)
 _codes("qt", 140)
-_codes("lc0 lc1", 448)
-_codes("lf0 lf1", 192)
+_codes("lc0 lc1", 576)
 for _i in range(8):
     SCRATCH["ps%d" % _i] = ("psum", [128, 512], "float32")
 
-SEMAPHORES = ["cv", "cs", "ct", "cq", "sa0", "sa1", "ca0", "ca1", "cb0", "cb1", "fw0", "fw1", "sent",
+SEMAPHORES = ["cv", "cs", "ct", "cq", "nr0", "nr1", "sa0", "sa1", "ca0", "ca1", "cb0", "cb1", "fa0", "fa1", "sent",
               "dx0", "dx1", "du", "dv", "dwc", "dws", "dk0", "dk1", "dy0", "dy1", "do0", "do1", "ds"]
 
 _MASKS = {}
@@ -147,22 +155,95 @@ def plan(ops, tries):
             t[i] = lo if early else lo + d
         return t
 
-    def run(order, tensor, wake, others):
-        t = [0.0] * n
-        free = {}
-        end = 0.0
+    queue = ["vstqyn".index(e) for e in eng]
+    cases = []
+    for f, tensor, wake, others, gather, scatter in CASES:
+        k = [tensor if o["e"] == "t" else others if o["e"] == "n" else gather if o["kind"] == 1 else scatter if o["kind"] == 2
+             else f if o["sem"] is None else 1.0 for o in ops]
+        cases.append(([0.0 if eng[i] == "n" else hold[i] * k[i] for i in every], [lat[i] * k[i] for i in every],
+                      [[(j, 0.0 if free_of(j, i) else wake) for j in pred[i]] for i in every]))
+
+    def run(order):
+        total = 0.0
+        for h, l, pr in cases:
+            t = [0.0] * n
+            free = [0.0] * 6
+            for i in order:
+                q = queue[i]
+                s = free[q] if q < 5 else 0.0
+                for j, w in pr[i]:
+                    x = t[j] + w
+                    if x > s:
+                        s = x
+                free[q] = s + h[i]
+                t[i] = s + l[i]
+            total += max(t)
+        return total
+
+    def chain(order, case):
+        h, l, pr = case
+        t, why, last, free = [0.0] * n, [None] * n, [None] * 6, [0.0] * 6
         for i in order:
-            s = free.get(eng[i], 0.0)
-            for j in pred[i]:
-                x = t[j] if free_of(j, i) else t[j] + wake
-                if x > s:
-                    s = x
-            f = tensor if eng[i] == "t" else others if eng[i] == "n" else 1.0
-            if eng[i] != "n":
-                free[eng[i]] = s + hold[i] * f
-            t[i] = s + lat[i] * f
-            end = max(end, t[i])
-        return end
+            q = queue[i]
+            s = 0.0
+            for j, w in pr[i]:
+                if t[j] + w > s:
+                    s, why[i] = t[j] + w, (j, 0)
+            if q < 5 and free[q] > s:
+                s, why[i] = free[q], (last[q], 1)
+            free[q], last[q], t[i] = s + h[i], i, s + l[i]
+        i, found = max(every, key=lambda i: t[i]), []
+        while why[i] and why[i][0] is not None:
+            if why[i][1]:
+                found += [(i, -1), (why[i][0], 1)]
+            i = why[i][0]
+        return found
+
+    def polish(score, order, steps):
+        seed = 7
+        best = (score, list(order))
+        for k in range(steps):
+            if k % 40 == 0:
+                hot = chain(order, cases[k // 40 % len(cases)])
+            seed = (seed * 1103515245 + 12345) % 2147483648
+            if seed >> 25 & 1:
+                i, way = hot[(seed >> 8) % len(hot)]
+                a = order.index(i)
+            else:
+                a = (seed >> 8) % n
+                i, way = order[a], 1 if seed >> 24 & 1 else -1
+            if queue[i] > 3:
+                continue
+            seed = (seed * 1103515245 + 12345) % 2147483648
+            far = 1 + (seed >> 10) % 4
+            stop = set(succ[i] if way > 0 else pred[i])
+            z, to, drag = a + way, None, []
+            while 0 <= z < n and far:
+                x = order[z]
+                if x in stop:
+                    if queue[x] == queue[i]:
+                        break
+                    drag.append(x)
+                    stop.update(succ[x] if way > 0 else pred[x])
+                elif queue[x] == queue[i]:
+                    to, far = z, far - 1
+                z += way
+            if to is None:
+                continue
+            lo, hi = min(a, to), max(a, to) + 1
+            part = order[lo:hi]
+            along = [x for x in part if x == i or x in drag]
+            stay = [x for x in part if x != i and x not in drag]
+            order[lo:hi] = stay + along if way > 0 else along + stay
+            s = run(order)
+            seed = (seed * 1103515245 + 12345) % 2147483648
+            if s <= score + HEAT * (1.0 - k / steps) * (seed >> 8) / 8388608:
+                score = s
+                if s < best[0]:
+                    best = (s, list(order))
+            else:
+                order[lo:hi] = part
+        return best
     best, seed = None, 1
     for k in range(tries):
         way = [0.0] * n
@@ -173,12 +254,12 @@ def plan(ops, tries):
         t = place(sorted(every, key=lambda i: (-way[i], i)), True)
         for _ in range(3):
             order = sorted(every, key=lambda i: (t[i], i))
-            score = sum(run(order, *v) for v in ((1.0, 0.1, 1.0), (1.0, 0.18, 1.3), (2.0, 0.18, 1.0), (1.0, 0.25, 0.8)))
+            score = run(order)
             if best is None or score < best[0]:
                 best = (score, order)
             late = place(sorted(every, key=lambda i: (-(t[i] + lat[i]), -i)), False)
             t = place(sorted(every, key=lambda i: (-late[i], i)), True)
-    return best[1]
+    return polish(best[0], best[1], STEPS)[1]
 
 
 def prog(g, T):
@@ -258,12 +339,21 @@ def rank_program(g, core, T, topo):
     V, S, PE = g.vector, g.scalar, g.tensor
     ops = []
     CYC = 0.00083
-    own_calls = [0]
+    marks = [0]
     aside = []
 
-    def emit(e, call, reads, writes, cost, sem=None, lat=None, pre=()):
+    def mark(name):
+        marks[0] += 1
+        return (name, 1 << marks[0])
+
+    def marked(name):
+        return (name, (1 << marks[0] + 1) - 1)
+
+    def emit(e, call, reads, writes, cost, sem=None, lat=None, pre=(), kind=0):
+        if aside == [("@ws", 1)]:
+            writes = writes + [mark("@a")]
         ops.append({"e": e, "call": call, "reads": reads + aside, "writes": writes, "sem": sem, "pre": list(pre),
-                    "hold": cost, "lat": cost if lat is None else lat})
+                    "kind": kind, "hold": cost, "lat": cost if lat is None else lat})
 
     def R(name, a=0, b=None, st=1):
         if name[:2] == "ps":
@@ -298,6 +388,9 @@ def rank_program(g, core, T, topo):
         if isinstance(s1, tuple):
             s1, r1 = both(s1)
             rs.append(r1)
+        if isinstance(s2, tuple):
+            s2, r2 = both(s2)
+            rs.append(r2)
         cost = vcost(o, i)
         if off:
             fa, fr = both(off)
@@ -305,7 +398,7 @@ def rank_program(g, core, T, topo):
             rs.append(fr)
             cost = 0.05 + 1.5 * CYC * size(o)
         if op1 is None:
-            emit("v", lambda: V.tensor_scalar(oa, ia, s1, None, op0), rs, [orr], cost)
+            emit("v", lambda: V.tensor_scalar(oa, ia, s1, None, op0), rs, [orr], cost, kind=1 if off else 0)
         else:
             emit("v", lambda: V.tensor_scalar(oa, ia, s1, s2, op0, op1), rs, [orr], cost)
 
@@ -320,19 +413,19 @@ def rank_program(g, core, T, topo):
             cost = 0.05 + 1.5 * CYC * size(o)
         elif i0[0][:2] != "ps":
             cost = 0.05 + CYC * max(64, 1.5 * size(o))
-        emit("v", lambda: V.tensor_tensor(oa, a0, a1, op), rs, [orr], cost)
+        emit("v", lambda: V.tensor_tensor(oa, a0, a1, op), rs, [orr], cost, kind=1 if off else 0)
 
-    def vscan(o, mask, data):
-        (oa, orr), (ma, mr), (da, dr) = both(o), both(mask), both(data)
-        emit("v", lambda: V.tensor_tensor_scan(oa, ma, da, -BIG, OP.min, OP.max), [mr, dr], [orr], vcost(o, data))
+    def vscan(o, d0, d1, first, op0, op1):
+        (oa, orr), (ma, mr), (da, dr) = both(o), both(d0), both(d1)
+        emit("v", lambda: V.tensor_tensor_scan(oa, ma, da, first, op0, op1), [mr, dr], [orr], vcost(o, d1))
 
     def vgather(o, i, off):
         (oa, orr), (ia, ir), (fa, fr) = both(o), both(i), both(off)
-        emit("v", lambda: V.tensor_copy(oa, ia.indirect(fa)), [ir, fr], [orr], 0.05 + 1.5 * CYC * size(o))
+        emit("v", lambda: V.tensor_copy(oa, ia.indirect(fa)), [ir, fr], [orr], 0.05 + 1.5 * CYC * size(o), kind=1)
 
     def vscatter(o, i, off):
         (oa, orr), (ia, ir), (fa, fr) = both(o), both(i), both(off)
-        emit("v", lambda: V.tensor_copy(oa.indirect(fa), ia), [ir, fr], [orr], 0.05 + 3.0 * CYC * size(i))
+        emit("v", lambda: V.tensor_copy(oa.indirect(fa), ia), [ir, fr], [orr], 0.05 + 3.0 * CYC * size(i), kind=2)
 
     def vtrans(o, i):
         (oa, orr), (ia, ir) = both(o), both(i)
@@ -352,9 +445,6 @@ def rank_program(g, core, T, topo):
         if isinstance(bias, tuple):
             bias, r1 = both(bias)
             rs.append(r1)
-        if isinstance(scale, tuple):
-            scale, r1 = both(scale)
-            rs.append(r1)
         cost = 0.065 + CYC * size(o) + more
         if off:
             fa, fr = both(off)
@@ -366,7 +456,7 @@ def rank_program(g, core, T, topo):
             ws.append(ar)
             emit("s", lambda: S.activation(oa, ia, f, bias=bias, scale=scale, accum_out=aa), rs, ws, cost + 0.02)
         else:
-            emit("s", lambda: S.activation(oa, ia, f, bias=bias, scale=scale), rs, ws, cost)
+            emit("s", lambda: S.activation(oa, ia, f, bias=bias, scale=scale), rs, ws, cost, kind=1 if off else 0)
 
     def mm(ps, n, w, wa, x, xa, start=True, stop=True, pre=()):
         emit("t", lambda: PE.matmul_mx(T[ps][:, 0:n], T[w][:, wa:wa + 128], T[w + "s"][:, wa:wa + 128],
@@ -376,32 +466,31 @@ def rank_program(g, core, T, topo):
     def dma(q, sem, oap, iap, reads, writes, lat=1.5):
         emit(q, lambda: eng[q].dma_start(oap, iap), reads, writes, 0.06, sem=sem, lat=lat)
 
-    def mark():
-        own_calls[0] += 1
-        return ("@g", 1 << own_calls[0])
-
     def sel(o, i, pattern, cmp, fillv, base, cm):
         (oa, orr), (ia, ir) = both(o), both(i)
-        emit("q", lambda: g.affine_select(oa, ia, pattern, cmp, fillv, base, cm), [ir], [orr, mark()], 0.17 + 2 * CYC * size(o))
+        emit("q", lambda: g.affine_select(oa, ia, pattern, cmp, fillv, base, cm), [ir], [orr, mark("@g")], 0.17 + 2 * CYC * size(o))
 
     def iota(o, pattern, base, cm):
         oa, orr = both(o)
         cost = 0.13 + 2 * CYC * size(o)
         if SCRATCH[o[0]][2] == "int32":
-            emit("q", lambda: g.iota(oa, pattern, base, cm), [], [orr, mark()], cost)
+            emit("q", lambda: g.iota(oa, pattern, base, cm), [], [orr, mark("@g")], cost)
         else:
-            emit("q", lambda: g.iota(oa, pattern, base, cm, allow_small_or_imprecise_dtypes=True), [], [orr, mark()], cost)
+            emit("q", lambda: g.iota(oa, pattern, base, cm, allow_small_or_imprecise_dtypes=True), [], [orr, mark("@g")], cost)
 
-    dma("y", "dx0", T.xs[:, 0:1024], T.x[:, 0:1024], [], [R("xs", 0, 1024)], lat=2.2)
+    cut = 4 * CUTS[0][1]
+    dma("y", "dx0", T.xs[:, 0:cut], T.x[:, 0:cut], [], [R("xs", 0, cut)], lat=2.5)
     dma("s", "du", T.us[:, 0:512], T.u[:, 0:512], [], [R("us")], lat=2.0)
-    dma("y", "dx1", T.xs[:, 1024:2048], T.x[:, 1024:2048], [], [R("xs", 1024, 2048)], lat=2.8)
+    dma("y", "dx1", T.xs[:, cut:2048], T.x[:, cut:2048], [], [R("xs", cut, 2048)], lat=2.8)
     dma("y", "dwc", T.qw[:, 0:512].bitcast(dt.uint8), T.wc[:, 0:2048], [], [R("qw")], lat=4.0)
     dma("y", "dws", T.qws[:, 0:512], T.ws[:, 0:512], [], [R("qws")], lat=4.0)
     dma("y", "dv", T.vs[:, 0:512], T.v[:, 0:512], [], [R("vs")], lat=4.0)
 
-    iota(("dsr",), [[1, 592]], -3, -4)
-    act(("zu", 0, 516), ("dsr", 0, 516), ACT.Sigmoid, bias=-128.0, scale=256.0, more=1.3, ws=[("@s", 1)])
-    act(("zl", 0, 516), ("dsr", 0, 516), ACT.Sigmoid, bias=-128.0, scale=-256.0, rs=[("@s", 1)])
+    iota(("dsr", 0, 64), [[1, 64]], -3, -4)
+    iota(("dsr", 64, 516), [[1, 452]], 61, -4)
+    act(("zl", 0, 64), ("dsr", 0, 64), ACT.Sigmoid, bias=-128.0, scale=-256.0, more=1.3, ws=[("@s", 1)])
+    act(("zl", 64, 516), ("dsr", 64, 516), ACT.Sigmoid, bias=-128.0, scale=-256.0, rs=[("@s", 1)])
+    vts(("zu", 0, 516), ("dsr", 0, 516), 0.0, None, OP.is_gt)
     sel(("zu", 3, 515, 4), ("zu", 3, 515, 4), [[-1, 128]], OP.not_equal, 512.0, 0, 1)
     sel(("zl", 3, 515, 4), ("zl", 3, 515, 4), [[-1, 128]], OP.not_equal, -512.0, 0, 1)
     vts(("ze", 0, 516), ("dsr", 0, 516), 0.0, None, OP.is_equal)
@@ -409,41 +498,40 @@ def rank_program(g, core, T, topo):
         quant("ql", 128 + 128 * c, 256 + 128 * c, "zu", 3 - c, 515 - c)
         quant("ql", 640 + 128 * c, 768 + 128 * c, "zl", 3 - c, 515 - c)
         quant("qe", 128 * c, 128 + 128 * c, "ze", 3 - c, 515 - c)
-    fill(("gw0",), 0.0)
-    fill(("ktt",), 0.0)
-    fill(("prt",), 0.0)
+    iota(("gw0",), [[0, 8]], 0, 0)
+    fill(("one",), 1.0)
+    quant("qj", 0, 128, "one", 0, 512)
+    fill(("hor",), 0.5)
+    fill(("hor", 0, 128, 16), 0.0)
+    fill(("hor", 6, 128, 16), -4096.0)
     fill(("rw", 0, SR), RS)
     fill(("rw", SR, 140), RW)
-    fill(("bt", 512, 528), 0.0)
-    fill(("sc", 512, 2112, 528), 0.0)
+    iota(("bt", 512, 528), [[0, 16]], 0, 0)
+    iota(("sc", 512, 2112, 528), [[0, 4]], 0, 0)
     for i in range(6):
         sel(("gw0",), ("gw0",), [[-16, 8]], OP.not_equal, 2.0 ** (i - 1), -i, 1)
-    for b in range(4):
-        vcopy(("ktt", 5 * b, 128, 16), ("gw0",))
-    quant("qk", 0, 128, "ktt", 0, 512)
     quant("qu", 0, 128, "us", 0, 512)
     iota(("kc", 0, 65), [[1, 65]], -32, 0)
-    sel(("prt", 0, 512, 4), ("prt", 0, 512, 4), [[-1, 4], [-4, 32]], OP.not_equal, 0.0625, 0, 1)
-    sel(("prt", 1, 512, 4), ("prt", 1, 512, 4), [[-1, 4], [-4, 32]], OP.not_equal, 32.0, 0, 1)
+    iota(("kn", 0, 65), [[-256, 65]], 8192, 0)
+    sel(("prt",), ("one",), [[-1, 4], [-4, 32], [0, 4]], OP.is_equal, 0.0, 0, 1)
     quant("ql", 0, 128, "prt", 0, 512)
-    iota(("tt", 2, 560, 4), [[0, 140]], 0, 0)
-    iota(("tt", 3, 560, 4), [[0, 140]], 0, 0)
-    iota(("vals",), [[1, 512]], -256, 0)
+    iota(("tt",), [[0, 560]], 0, 0)
+    iota(("vals",), [[1, 128], [128, 4]], -256, 0)
     iota(("ip",), [[0, 1]], 0, 1)
-    iota(("c2",), [[2, 2]], 0, 0)
-    iota(("c16",), [[64, 4]], 4 * 513, 0)
-    iota(("ci",), [[4, 2], [64, 4], [1, 2]], 0, 0)
+    iota(("c2",), [[1, 2]], 0, 0)
+    iota(("c16",), [[32, 4]], 2 * 513, 0)
+    iota(("ci",), [[2, 2], [32, 4], [1, 2]], 0, 0)
     vts(("ia",), ("ip",), 15, None, OP.bitwise_and)
-    vts(("i4",), ("ia",), 4.0, None, OP.mult)
-    for a in range(4):
-        emit("v", lambda a=a: V.tensor_scalar(T.cl16[32 * a:32 * a + 32, :], T.ci[32 * a:32 * a + 32, :], T.i4[32 * a:32 * a + 32, :],
-                                              260.0 * (a // 2) + 2.0 * (a % 2), OP.add, OP.add),
-             [R("ci"), R("i4")], [("cl16", 1 << a)], 0.1)
-    vts(("l2",), ("c2",), ("i4",), 8.0, OP.add, OP.mult)
-    vts(("dum",), ("c16",), ("i4",), 0.25, OP.add, OP.mult)
-    sel(("msk0",), ("dsr",), [[0, 592]], OP.is_gt, BIG, -1, 0)
+    vts(("i2",), ("ia",), 2.0, None, OP.mult)
+    vts(("ib",), ("ip",), 5, None, OP.arith_shift_right)
+    vts(("i3",), ("ib",), 130.0, ("i2",), OP.mult, OP.add)
+    vts(("cl16",), ("ci",), ("i3",), None, OP.add)
+    vts(("l2",), ("c2",), ("i2",), 16.0, OP.add, OP.mult)
+    vts(("dum",), ("c16",), ("i2",), 0.5, OP.add, OP.mult)
+    sel(("msk0", 0, 512), ("dsr", 0, 512), [[0, 512]], OP.is_gt, BIG, -1, 0)
     sel(("neg",), ("dsr", 0, 64), [[0, 64]], OP.is_gt, -BIG, -1, 0)
-    for n in ("at", "zt", "gt"):
+    iota(("at", 0, 256), [[0, 256]], 0, 0)
+    for n in ("zt", "gt"):
         iota((n, 256, 512), [[0, 256]], 0, 0)
     iota(("wtt",), [[0, 576]], 0, 0)
 
@@ -455,15 +543,25 @@ def rank_program(g, core, T, topo):
         a, b = topo.chip(core), topo.chip(other(x))
         return 0 if topo.mates(a, b) else 1 if topo.same_plane(a, b) else 2
     level = sorted([x for x in range(1, N) if x != near and topo.die(other(x)) == topo.die(core)], key=lambda x: -hops(x))
-    handed = level[:FWD]
-    late = level[FWD:] + [x ^ near for x in level[FWD:]]
-    first = handed + [near]
-    slot = {x: 64 * k for k, x in enumerate(first + late)}
+    far = level + [x ^ near for x in level[FWD:]]
+    named = {"h": far[:FWD], "l": far[FWD:], "n": [near], "f": [x ^ near for x in far[:FWD]]}
+
+    def ranks(who):
+        return sum([named[c] for c in who], [])
+    slot = {x: 128 + 64 * k for k, x in enumerate(ranks(SLOTS))}
+    back = 64 * len(far)
     fmask = topo.mask(core, other(level[0]))
-    nmask = topo.mask(core, other(near)) & ~fmask
-    nf, nn = bin(fmask).count("1"), bin(nmask).count("1")
-    arrive = {"sa": nf * (len(handed) + len(late)) + nn, "ca": nf * len(handed) + nn, "cb": nf * len(late),
-              "fw": 2 * nn if handed else 0}
+    rest = [e for e in topo.engines(core, other(near)) if not fmask >> e & 1]
+    nf = bin(fmask).count("1")
+
+    def some(k):
+        return sum(1 << e for e in rest[:k])
+    arrive = {"nr": 0}
+    for plane, who, k, sem in CALLS:
+        arrive[sem] = arrive.get(sem, 0) + nf * len(ranks(who))
+        arrive["nr"] += k
+    for plane, who, k, after, sem in HANDS:
+        arrive[sem] = arrive.get(sem, 0) + k
 
     def view(name, a, b, plane):
         return T[name + "s"][:, a:b] if plane else T[name][:, a:b].bitcast(dt.uint8)
@@ -473,38 +571,34 @@ def rank_program(g, core, T, topo):
         return DstId(rid=rid, pnc=pid)
 
     def send(t):
-        qa, lc, lf = "qa%d" % t, "lc%d" % t, "lf%d" % t
+        lc = "lc%d" % t
 
-        def call(xs, plane, sem):
+        def call(plane, who, k, sem):
             ts = []
-            for group, m in (([x for x in xs if x != near], fmask), ([x for x in xs if x == near], nmask)):
+            for group, m, s in ((ranks(who), fmask, sem), ([near] if k else [], some(k), "nr")):
                 if group:
-                    ts.append(RemoteDMATransfer(dst_ids=[dst(x) for x in group], dma_engine_mask=m, remote_sem=T.sem[sem],
-                                                srcs=[view(qa, 0, 64, plane)],
+                    ts.append(RemoteDMATransfer(dst_ids=[dst(x) for x in group], dma_engine_mask=m, remote_sem=T.sem[s + str(t)],
+                                                srcs=[view(lc, 64, 128, plane)],
                                                 dsts=[view(lc, slot[x], slot[x] + 64, plane) for x in group]))
                     count["sent"] += bin(m).count("1")
             g.remote_dma_fused(ts, local_sem=T.sem.sent)
 
-        def hand(plane):
-            w = 64 * len(handed)
-            g.remote_dma_fused([RemoteDMATransfer(dst_ids=[dst(near)], dma_engine_mask=nmask, remote_sem=T.sem["fw%d" % t],
-                                                  srcs=[view(lc, 0, w, plane)], dsts=[view(lf, 0, w, plane)])],
+        def hand(plane, who, k, sem):
+            a, z = min(slot[x] for x in ranks(who)), max(slot[x] for x in ranks(who)) + 64
+            g.remote_dma_fused([RemoteDMATransfer(dst_ids=[dst(near)], dma_engine_mask=some(k), remote_sem=T.sem[sem + str(t)],
+                                                  srcs=[view(lc, a, z, plane)], dsts=[view(lc, back + a, back + z, plane)])],
                                local_sem=T.sem.sent)
-            count["sent"] += nn
-        every = ("@g", (1 << own_calls[0] + 1) - 1)
-        emit("q", lambda: call(first + late, 1, "sa%d" % t), [R(qa), every], [("@q", 1), ("@ws", 1)], 0.4, sem="sent")
-        emit("q", lambda: call(first, 0, "ca%d" % t), [R(qa)], [("@q", 1), ("@wa", 1)], 0.4, sem="sent")
-        if late:
-            emit("q", lambda: call(late, 0, "cb%d" % t), [R(qa)], [("@q", 1), ("@wb", 1)], 0.4, sem="sent")
-        emit("n", None, [("@ws", 1)], [("@as", 1)], 0.0, lat=2.0)
-        emit("n", None, [("@wa", 1)], [R(lc, 0, 64 * len(first))], 0.0, lat=2.6)
-        if late:
-            emit("n", None, [("@wb", 1)], [R(lc, 64 * len(first), 448)], 0.0, lat=3.2)
-        if handed:
-            emit("q", lambda: hand(1), [("@as", 1)], [("@q", 1)], 0.4, sem="sent", pre=[("sa%d" % t, arrive["sa"])])
-            emit("q", lambda: hand(0), [R(lc, 0, 64 * len(first))], [("@q", 1), ("@wf", 1)], 0.4, sem="sent",
-                 pre=[("ca%d" % t, arrive["ca"])])
-            emit("n", None, [("@wf", 1)], [R(lf)], 0.0, lat=1.5)
+            count["sent"] += k
+        every = marked("@g")
+        for z, c in enumerate(CALLS):
+            emit("q", lambda c=c: call(*c), [R(lc, 0, 128), every], [("@q", 1), ("@ws", 1), ("@w", 1 << z)], 0.4, sem="sent")
+            emit("n", None, [("@w", 1 << z)], [("@" + c[3], 1 << z)], 0.0, lat=LATS[z])
+            if c[2]:
+                emit("n", None, [("@w", 1 << z)], [("@nr", 1 << z)], 0.0, lat=1.7)
+        for z, (plane, who, k, after, sem) in enumerate(HANDS):
+            emit("q", lambda c=(plane, who, k, sem): hand(*c), [("@" + after, 255)], [("@q", 1), ("@h", 1 << z)], 0.4, sem="sent",
+                 pre=[(after + str(t), arrive[after])])
+            emit("n", None, [("@h", 1 << z)], [("@" + sem, 16 << z)], 0.0, lat=1.5)
 
     def ps(i):
         return "ps%d" % i
@@ -515,60 +609,59 @@ def rank_program(g, core, T, topo):
         a, z = CUTS[t][h], CUTS[t][h + 1]
         quant(qx, a, z, state, 4 * a, 4 * z)
         if t < ROUNDS:
-            mm(ps(h), z - a, "qu", 0, qx, a)
-            act(("bt", a, z), (ps(h), 0, z - a), ACT.Sign, bias=-(2.0 ** -100))
+            for c in range(a, z, 128):
+                mm(ps(c // 128), 128, qx, c, "qu", 0)
+                act(("bu", c, c + 128), (ps(c // 128), 0, 128), ACT.Sign, bias=-(2.0 ** -100))
+                vscan(("kx", c, c + 128), ("hor",), ("bu", c, c + 128), 0.0, OP.mult, OP.add)
         else:
             mm(ps(h), z - a, "qv", 0, qx, a)
-            act(("yb", a, z), (ps(h), 0, z - a), ACT.Copy)
-            dma("y", "do%d" % h, T.oc[:, 4 * a:4 * z], T[qx][:, a:z].bitcast(dt.uint8), [R(qx, a, z)], [])
-            dma("s", "dy%d" % h, T.y[:, a:z], T.yb[:, a:z], [R("yb", a, z)], [])
+            if h:
+                vcopy(("yb", a, z), (ps(h), 0, z - a))
+            else:
+                act(("yb", a, z), (ps(h), 0, z - a), ACT.Copy)
+            dma("y", "do%d" % h, T.oc[:, 4 * a:4 * z], T[qx][:, a:z].bitcast(dt.uint8), [R(qx, a, z)], [], lat=1.7 if h else 2.1)
+            dma("y" if h else "s", "dy%d" % h, T.y[:, a:z], T.yb[:, a:z], [R("yb", a, z)], [], lat=1.6 if h else 2.1)
 
     key_half(0, "xs", 0)
     key_half(0, "xs", 1)
     for t in range(ROUNDS):
-        qx, qa, lc, lf = "qx%d" % t, "qa%d" % t, "lc%d" % t, "lf%d" % t
+        qx, lc = "qx%d" % t, "lc%d" % t
         new = "st%d" % (t + 1)
-        quant("qb", 0, 130, "bt", 0, 520)
-        mm("ps3", 128, "qb", 0, "qk", 0)
-        mm("ps2", 128, "qb", 0, "qk", 0)
-        act(("kng",), ("ps3", 0, 32), ACT.Copy, scale=-256.0)
-        for h in (0, 1):
-            for z in range(16):
-                c = 16 * h + z
-                o = ("ot", 1040 * h + z, 1040 * h + 1040, 16)
-                if z >= 16 - STHR[h]:
-                    act(o, ("kc", 0, 65), ACT.Sigmoid, bias=("kng", c, c + 1), scale=256.0, rs=[("@s", 1)])
+        for a in range(4):
+            for z in range(8):
+                c = 128 * (z % 4) + 32 * a + 16 * (z // 4) + 6
+                o = ("ot", 520 * a + z, 520 * a + 520, 8)
+                if z >= 8 - STHR[a]:
+                    act(o, ("kc", 0, 65), ACT.Sigmoid, bias=("kx", c, c + 1), scale=256.0, rs=[("@s", 1)])
                 else:
-                    vts(o, ("kc", 0, 65), ("ps2", c, c + 1), None, OP.is_gt)
-            quant("qo", 260 * h, 260 * h + 260, "ot", 1040 * h, 1040 * h + 1040)
-        for h in (0, 1):
+                    vts(o, ("kn", 0, 65), ("kx", c, c + 1), None, OP.is_lt)
+            quant("qo", 130 * a, 130 * a + 130, "ot", 520 * a, 520 * a + 520)
+        for a in range(4):
             for c in range(4):
-                p = ps(4 * (1 - h) + c)
-                mm(p, 256, "ql", 128 + 128 * c, "qo", 260 * h + 4, True, False)
-                mm(p, 256, "ql", 640 + 128 * c, "qo", 260 * h, False, True)
-                for gg in range(4):
-                    k = 12 + 16 * (4 * h + gg) + c
+                p = ps(4 * (1 - a % 2) + c)
+                mm(p, 128, "ql", 128 + 128 * c, "qo", 130 * a + 2, True, False)
+                mm(p, 128, "ql", 640 + 128 * c, "qo", 130 * a, False, True)
+                for gg in range(2):
+                    k = 12 + 16 * (2 * a + gg) + c
                     if k >= SR:
-                        vreduce(("rw", k, k + 1), (p, gg, 256, 4), OP.max)
+                        vreduce(("rw", k, k + 1), (p, gg, 128, 2), OP.max)
                     else:
-                        z = 64 * (4 * gg + c)
-                        act(("sj", z, z + 64), (p, gg, 256, 4), ACT.Relu, bias=-511.5, accum=("rw", k, k + 1))
+                        z = 64 * (4 * (2 * a + gg) + c)
+                        act(("sj", z, z + 64), (p, gg, 128, 2), ACT.Relu, bias=-511.5, accum=("rw", k, k + 1))
         for o in ("hi", "rv"):
-            act((o, 0, SR), ("rw", 0, SR), ACT.Identity, bias=M16 - RS)
-            vts((o, SR, 140), ("rw", SR, 140), M16 - RW, None, OP.add)
-        act(("tt", 0, 560, 4), ("hi",), ACT.Identity, bias=-M16)
-        vtt(("tt", 1, 560, 4), ("rv",), ("hi",), OP.subtract)
+            act((o, 12, SR), ("rw", 12, SR), ACT.Identity, bias=M16 - RS)
+        vts(("hi", SR, 128), ("rw", SR, 128), M16 - RW, None, OP.add)
+        act(("rv", SR, 128), ("rw", SR, 128), ACT.Identity, bias=M16 - RW)
+        act(("tt", 48, 512, 4), ("hi", 12, 128), ACT.Identity, bias=-M16 / 512, scale=1.0 / 512)
+        vtt(("tt", 49, 512, 4), ("rv", 12, 128), ("hi", 12, 128), OP.subtract)
         quant("qt", 0, 140, "tt", 0, 560)
         for q in range(4):
             mm("ps0", 128, "qt", 12 - 4 * q, "ql", 32 * q, q == 0, q == 3)
-        vts(("po",), ("ps0", 0, 32), 256.0, None, OP.add)
+        vts(("po",), ("ps0", 0, 32), 32.0, 256.0, OP.mult, OP.add)
         for h in (0, 1):
-            p = ps(4 + h)
-            mm(p, 260, "ql", 128, "qo", 260 * h, True, False)
-            mm(p, 260, "ql", 640, "qo", 260 * h, False, False)
-            mm(p, 260, "qe", 0, "qo", 260 * h, False, True)
-            act(("cnt", 260 * h, 260 * h + 260), (p, 0, 260), ACT.Copy)
-        act(("cg",), ("cnt",), ACT.Copy, off=("cl16",))
+            mm(ps(4 + h), 260, "qj", 0, "qo", 260 * h)
+            act(("cnt", 260 * h, 260 * h + 260), (ps(4 + h), 0, 260), ACT.Copy)
+        act(("cg",), ("cnt",), ACT.Identity, bias=-256.0, off=("cl16",))
         vtrans(("ctr",), ("cg",))
         for b in range(4):
             mm(ps(6 + b % 2), 512, "qe", 128 * b, qx, 0)
@@ -577,10 +670,10 @@ def rank_program(g, core, T, topo):
         lo, up = ("ctr", 0, 128, 32), ("ctr", 128, 256, 32)
         vtt(("em",), up, lo, OP.is_equal)
         vtt(("dm",), ("em",), ("dum",), OP.mult)
-        vtt(("mk",), lo, ("dm",), OP.max)
-        vtt(("pk",), up, ("dm",), OP.max)
-        vcopy(("mk16",), ("mk",))
-        vts(("pk16",), ("pk",), 1.0, 512.0, OP.subtract, OP.min)
+        vtt(("mk",), lo, ("dm",), OP.add)
+        vtt(("pk",), up, ("dm",), OP.add)
+        vts(("mk16",), ("mk",), 256.0, None, OP.add)
+        vts(("pk16",), ("pk",), 255.0, 512.0, OP.add, OP.min)
         vscatter((msk,), ("neg",), ("mk16",))
         vscatter(("lsw",), ("vals",), ("po",))
         vtrans(("ltr",), ("lsw",))
@@ -593,20 +686,15 @@ def rank_program(g, core, T, topo):
             act(("sd", 512 * b, 512 * b + 512), ("dd", 512 * b, 512 * b + 512), ACT.Copy, off=("l16",))
         act(("sd", 768, 1024), ("dd", 512, 1024), ACT.Copy, off=("l16", 16, 32))
         for b in (0, 2, 3, 1):
-            vscan(("sc", 528 * b, 528 * b + 512), (msk, 0, 512), ("sd", 512 * b, 512 * b + 512))
-            o, i = ("at", b, 256, 4), ("sc", 528 * b, 528 * b + 513)
+            vscan(("sc", 528 * b, 528 * b + 512), (msk, 0, 512), ("sd", 512 * b, 512 * b + 512), -BIG, OP.min, OP.max)
+            o, i = ("at", 256 + b, 512, 4), ("sc", 528 * b, 528 * b + 513)
             if b != 1:
                 act(o, i, ACT.Copy, scale=2.0, off=("pk16",))
             else:
                 vts(o, i, 2.0, None, OP.mult, off=("pk16",))
-        quant(qa, 0, 128, "at", 0, 512)
+        quant(lc, 0, 128, "at", 0, 512)
         send(t)
         aside.append(("@ws", 1))
-        for b in range(4):
-            mm(ps(b), 128, "qe", 128 * b, qa, 0)
-        for b in range(4):
-            for s in (0, 1):
-                act(("own", 256 * s + b, 256 * s + 256, 4), (ps(b), 0, 64), ACT.Copy)
         if t == 0:
             for b in range(4):
                 act(("wtt", 48 + 5 * b, 560, 64), ("gw0",), ACT.Copy)
@@ -615,7 +703,10 @@ def rank_program(g, core, T, topo):
             for c in range(4):
                 quant("qh", 128 * c, 128 + 128 * c, "zh", 3 - c, 515 - c)
             quant("qv", 0, 128, "vs", 0, 512)
-            fill(("msk1",), BIG)
+            fill(("msk1", 0, 512), BIG)
+        mm("ps0", 512, "qu", 0, qx, 0)
+        act(("bt", 0, 512), ("ps0", 0, 512), ACT.Sign, bias=-(2.0 ** -100))
+        quant("qb", 0, 130, "bt", 0, 520)
         quant("qd", 0, 130, "bt", 4, 524)
         quant("qc", 0, 128, "bt", 1, 513)
         for q in range(4):
@@ -628,24 +719,27 @@ def rank_program(g, core, T, topo):
         for b in (2, 3, 0):
             mm(ps(HB[b]), 512, "qh", 128 * b, qx, 0)
         aside.pop()
-        lots = [(lc, 0, len(first), ("sa", "ca")), (lc, 64 * len(first), len(late), ("cb",)), (lf, 0, len(handed), ("fw",))]
-        lots = [x for x in lots if x[2]]
-        for z, (buf, a, n, sems) in enumerate(lots):
+        aside.extend([("@nr", 4095), marked("@a")])
+        for b in range(4):
+            mm(ps(b), 128, "qe", 128 * b, lc, 64, pre=[("nr%d" % t, arrive["nr"])])
+            act(("own", b, 512, 4), (ps(b), 0, 128), ACT.Copy)
+        del aside[:]
+        for z, (a, n, sems) in enumerate(LOTS):
+            aside.extend([("@" + s, 4095) for s in sems] + [marked("@a")])
             for b in range(4):
-                mm(ps(b), 64 * n, "qe", 128 * b, buf, a, pre=[(s + str(t), arrive[s]) for s in sems])
-            if z < len(lots) - 1:
-                for s in range(0, n, 2):
-                    k = min(2, n - s)
-                    for b in range(4):
-                        w = ("own", b, 256 * k, 4)
-                        vtt(w, (ps(b), 64 * s, 64 * (s + k)), w, OP.max)
-                if z == len(lots) - 2:
+                mm(ps(b), 64 * n, "qe", 128 * b, lc, 64 * (3 + a), pre=[(s + str(t), arrive[s]) for s in sems])
+            del aside[:]
+            if z < WIDE:
+                for b in range(4):
+                    w = ("own", b, 512, 4)
+                    vtt(w, (ps(b), 0, 128), w, OP.max)
+                if z == WIDE - 1:
                     vtt(("mm",), ("own", 0, 256), ("own", 256, 512), OP.max)
             else:
                 for s in range(n):
                     for b in range(4):
                         w = ("mm", b, 256, 4)
-                        vtt(("zt", b, 256, 4) if s == n - 1 else w, (ps(b), 64 * s, 64 * s + 64), w, OP.max)
+                        vtt(("zt", b, 256, 4) if (z, s) == (len(LOTS) - 1, n - 1) else w, (ps(b), 64 * s, 64 * s + 64), w, OP.max)
         quant("qz", 0, 128, "zt", 0, 512)
         for b in (0, 2, 1, 3):
             mm(ps(b), 128, "qw", 128 * b, "qz", 0)

@@ -5,25 +5,21 @@ OP, ACT, AX = AluOpType, ActivationFunctionType, AxisListType
 ROUNDS = 2
 BIG = 2.0 ** 60
 M16 = 3072.0
-TRIES = 8
-STEPS = 60000
-HEAT = 0.3
-CASES = ((1.0, 1.1, 0.1, 1.0, 1.0, 1.0), (1.1, 1.2, 0.2, 1.3, 1.25, 1.6), (1.3, 1.8, 0.15, 1.0, 1.0, 1.2),
-         (1.0, 1.0, 0.12, 0.8, 0.75, 0.6))
 SG = 4
-SR = 12 + 16 * SG
 RW = 775.5
 RS = 264.0
-STHR = (5, 4, 2, 2)
-CUTS = ((0, 384, 512), (0, 384, 512), (0, 384, 512))
-MINE = (((2, 3), (2, 3, 0)), ((2, 3), (2, 3, 0)))
+WHO = "vvvs" * 2 + "vvvv" * 2 + "vsvs" + "vvss" * 3
+PLACES = ((4, 6, (4, 5, 6, 7)), (0, 2, (0, 1, 2, 3)), (6, 8, (4, 5, 6, 7)), (2, 4, (0, 1, 2, 3)))
+CB, DB, PB = 4, (6, 7, 6, 7), 0
+CUTS = ((0, 384, 512), (0, 384, 512), (0, 320, 512))
+MINE = (((2, 3), (2, 3)), ((2, 3), (2, 3, 0)))
+VG = 12
 FWD = 2
 SLOTS = "nhlf"
 CALLS = ((0, "h", 4, "ca"), (1, "hl", 4, "sa"), (0, "l", 0, "cb"), (1, "f", 0, "fa"))
-LATS = (2.2, 2.4, 2.6, 2.5)
-HANDS = ((0, "h", 8, "ca", "fa"),)
-LOTS = ((0, 2, ("sa", "ca")), (2, 2, ("cb",)), (4, 2, ("fa",)))
-WIDE = 2
+HANDS = ((0, "h", 8, "ca", "ha"),)
+LOTS = ((0, 1, 4, ("nr",)), (1, 2, 0, ("sa", "ca")), (3, 2, 4, ("cb",)), (5, 2, 0, ("fa", "ha")))
+ORDER = ("0001020304050614150u0v0r1l1n1o0t0s070a0d1v1h0b1908090c131i221w1z12161k1j171b0q1t0w1a181g0e0h0k25231x200o0f0l241y210n2627282d292b2e3330342f2a2g2c2h313u3t3q351f2u2v2x3p2q2i2r2m4g2z3o2y320i3n2j2n364e3s3r4d4f4h3f3g3v3b3c37383j2w2s2t2p2k2l2o1e3k44483w493x4540414c3h4i4j3a3d3e4k3l3m4p4q3i391c4x4y4l4r4s4z504m4t4u4o4n4w4v4a3y42463z431p4b475d54525e5f5g1m53510g561d5h55575i0p0m0j1r5j5k5l58595a5b5m5c5s5z1q5t0x0y1s1u0z1011605v5u615x5w5n635y62705o5q5p5r65646b6766696d6c686a6e6f6n716p6o6r6q6g6h726y73746s757c7g76777a7e7h7d7b7f7p787l7n7j6z6t6x6u6w6v797m7q7o7k7u7s7r7t7y7w7v7x8280817z86848583888a89876i8c8e8d8b8g8i8h6j6k8o8q8n8p8f8k8m8j8l8s8u8r8t8w8y8v8x7i6m6l9192959493969899979a9d9b9e9c8z909h9f9i9g9k9j9za09m9l9o9na29pa1a4a39q9t9w9r9x9ua5a69s9ya7b29va9b4adaaafbta8acagaeabboayb3ahazb0cicfbnb5b1b6chbpbubqamanaiajauavaqapaobrbscjcebvcccdarbjbbcgbkbfbgbhalaxakb7bcawbwbxc8b8blckbmbibdb9baatasc9c4c0c1cxcyctcubec5clcmczd0cwcvcncocpbybzcac3cbc2c7c6cqddcscrded3d1dfdgdkdmd4d2dhd5d6d7d8d9dadbdidjdsdcdndldqdoeldpdrdtdzdue0dwdve1dye5e6e2e3e7ebdxede4e9ece8eaemeeefepeneof1exf2evezf0faeqereseweyetf6f8f4egeheuf9f7f5fbfefdfffceif3fkflfnfmfifgfhfjfofpfrfqftfsfvfufwg0fzfyg3fxg2g1ejekgbg8g9gag7g4g5g6gfgcgdgegjggghgigngqgrgogpgugsgvgtgwgmgzgxh0gyglgkh4h2h3h1h5h6hhhgh8hjh7h9hahihlhbhkhmhehnhqhrhshthuhchohdhphfhv")
 
 SCRATCH = {}
 
@@ -39,50 +35,48 @@ def _codes(names, n):
         SCRATCH[name + "s"] = ("sbuf", [128, n], "uint8")
 
 
-_b("xs st1 st2 dd sd ge", 2048)
-_b("us vs at zt gt vals lsw ltr prt own bu kx one", 512)
+_b("xs st1 st2 dd sd ge sj", 2048)
+_b("us vs at zt gt vals prt bu kx", 512)
+_b("lsw ltr", 1024)
 _b("hor", 128)
-_b("sj", 1024)
-_b("dsr bt zu zl ze zh", 528)
 _b("gw0", 8)
+_b("dsr bt zu zl ze zh", 528)
 _b("kc kn", 66)
 _b("wtt", 576)
-_b("ot", 2080)
+_b("ot sc", 2112)
 _b("tt", 560)
 _b("msk0 msk1", 1104)
-_b("sc", 2112)
 _b("neg", 64)
 _b("mm gb cg ctr", 256)
 _b("hi", 140)
-_b("lj lk", 32)
 _b("rw rv", 140, "float32")
 _b("kf yb", 512, "float32")
-_b("cnt", 520, "float32")
+_b("cnt", 132, "float32")
 _b("ci", 16, "float32")
 _b("em dm mk pk dum c16", 4, "float32")
 _b("c2", 2, "float32")
-_b("i2 i3", 1, "float32")
-_b("ip ia ib", 1, "int32")
+_b("i2 i4 pc", 1, "float32")
+_b("ip ia ic", 1, "int32")
 _b("po ko l16", 32, "uint16")
 _b("cl16", 16, "uint16")
 _b("mk16 pk16", 4, "uint16")
 _b("l2", 2, "uint16")
-_codes("qu qv qc qz qg qj", 128)
+_codes("qu qv qc qz qg", 128)
 _codes("qb qd", 130)
 _codes("qn", 144)
+_codes("qj", 224)
 _codes("qx0 qx1 qx2 qw qe qh", 512)
 _codes("ql", 1152)
-_codes("qo", 520)
+_codes("qo", 528)
 _codes("qt", 140)
 _codes("lc0 lc1", 576)
 for _i in range(8):
     SCRATCH["ps%d" % _i] = ("psum", [128, 512], "float32")
 
-SEMAPHORES = ["cv", "cs", "ct", "cq", "nr0", "nr1", "sa0", "sa1", "ca0", "ca1", "cb0", "cb1", "fa0", "fa1", "sent",
-              "dx0", "dx1", "du", "dv", "dwc", "dws", "dk0", "dk1", "dy0", "dy1", "do0", "do1", "ds"]
+SEMAPHORES = ["cv", "cs", "ct", "cq", "nr0", "nr1", "sa0", "sa1", "ca0", "ca1", "cb0", "cb1", "fa0", "fa1", "ha0", "ha1",
+              "sent", "dx0", "dx1", "du", "dv", "dwc", "dws", "dk0", "dk1", "dy0", "dy1", "do0", "do1", "ds"]
 
 _MASKS = {}
-_PLAN = []
 
 
 def _cols(a, b, st):
@@ -92,174 +86,6 @@ def _cols(a, b, st):
             m |= 1 << i
         _MASKS[(a, b, st)] = m
     return _MASKS[(a, b, st)]
-
-
-def plan(ops, tries):
-    wr, rd, pred = {}, {}, []
-    for i, o in enumerate(ops):
-        p = set()
-        for name, m in o["reads"]:
-            for wm, j in wr.get(name, []):
-                if wm & m:
-                    p.add(j)
-            if name[:2] == "ps":
-                for rm, j in rd.get(name, []):
-                    if ops[j]["e"] != o["e"]:
-                        p.add(j)
-        for name, m in o["writes"]:
-            for om, j in wr.get(name, []) + rd.get(name, []):
-                if om & m:
-                    p.add(j)
-        p.discard(i)
-        for name, m in o["writes"]:
-            wr[name] = [w for w in wr.get(name, []) if w[0] & ~m] + [(m, i)]
-            rd[name] = [r for r in rd.get(name, []) if r[0] & ~m]
-        for name, m in o["reads"]:
-            rd[name] = rd.get(name, []) + [(m, i)]
-        pred.append(sorted(p))
-    n = len(ops)
-    every = range(n)
-    succ = [[] for _ in ops]
-    for i in every:
-        for j in pred[i]:
-            succ[j].append(i)
-    eng = [o["e"] for o in ops]
-    hold = [o["hold"] for o in ops]
-    lat = [o["lat"] for o in ops]
-    WAKE = 0.18
-
-    def free_of(j, i):
-        return eng[j] == "t" and eng[i] == "t" or eng[i] == "n"
-
-    def gap(j, i):
-        return lat[j] if free_of(j, i) else lat[j] + WAKE
-
-    def place(order, early):
-        t = [0.0] * n
-        busy = {e: [] for e in eng}
-        for i in order:
-            d = hold[i]
-            if early:
-                lo = max([0.0] + [t[j] + gap(j, i) for j in pred[i]])
-            else:
-                lo = max([lat[i]] + [t[k] + gap(i, k) for k in succ[i]]) - d
-            if eng[i] != "n":
-                b = busy[eng[i]]
-                z = len(b)
-                while z and b[z - 1][1] > lo + 1e-9:
-                    z -= 1
-                while z < len(b) and b[z][0] < lo + d - 1e-9:
-                    lo = max(lo, b[z][1])
-                    z += 1
-                b.insert(z, (lo, lo + d))
-            t[i] = lo if early else lo + d
-        return t
-
-    queue = ["vstqyn".index(e) for e in eng]
-    cases = []
-    for f, tensor, wake, others, gather, scatter in CASES:
-        k = [tensor if o["e"] == "t" else others if o["e"] == "n" else gather if o["kind"] == 1 else scatter if o["kind"] == 2
-             else f if o["sem"] is None else 1.0 for o in ops]
-        cases.append(([0.0 if eng[i] == "n" else hold[i] * k[i] for i in every], [lat[i] * k[i] for i in every],
-                      [[(j, 0.0 if free_of(j, i) else wake) for j in pred[i]] for i in every]))
-
-    def run(order):
-        total = 0.0
-        for h, l, pr in cases:
-            t = [0.0] * n
-            free = [0.0] * 6
-            for i in order:
-                q = queue[i]
-                s = free[q] if q < 5 else 0.0
-                for j, w in pr[i]:
-                    x = t[j] + w
-                    if x > s:
-                        s = x
-                free[q] = s + h[i]
-                t[i] = s + l[i]
-            total += max(t)
-        return total
-
-    def chain(order, case):
-        h, l, pr = case
-        t, why, last, free = [0.0] * n, [None] * n, [None] * 6, [0.0] * 6
-        for i in order:
-            q = queue[i]
-            s = 0.0
-            for j, w in pr[i]:
-                if t[j] + w > s:
-                    s, why[i] = t[j] + w, (j, 0)
-            if q < 5 and free[q] > s:
-                s, why[i] = free[q], (last[q], 1)
-            free[q], last[q], t[i] = s + h[i], i, s + l[i]
-        i, found = max(every, key=lambda i: t[i]), []
-        while why[i] and why[i][0] is not None:
-            if why[i][1]:
-                found += [(i, -1), (why[i][0], 1)]
-            i = why[i][0]
-        return found
-
-    def polish(score, order, steps):
-        seed = 7
-        best = (score, list(order))
-        for k in range(steps):
-            if k % 40 == 0:
-                hot = chain(order, cases[k // 40 % len(cases)])
-            seed = (seed * 1103515245 + 12345) % 2147483648
-            if seed >> 25 & 1:
-                i, way = hot[(seed >> 8) % len(hot)]
-                a = order.index(i)
-            else:
-                a = (seed >> 8) % n
-                i, way = order[a], 1 if seed >> 24 & 1 else -1
-            if queue[i] > 3:
-                continue
-            seed = (seed * 1103515245 + 12345) % 2147483648
-            far = 1 + (seed >> 10) % 4
-            stop = set(succ[i] if way > 0 else pred[i])
-            z, to, drag = a + way, None, []
-            while 0 <= z < n and far:
-                x = order[z]
-                if x in stop:
-                    if queue[x] == queue[i]:
-                        break
-                    drag.append(x)
-                    stop.update(succ[x] if way > 0 else pred[x])
-                elif queue[x] == queue[i]:
-                    to, far = z, far - 1
-                z += way
-            if to is None:
-                continue
-            lo, hi = min(a, to), max(a, to) + 1
-            part = order[lo:hi]
-            along = [x for x in part if x == i or x in drag]
-            stay = [x for x in part if x != i and x not in drag]
-            order[lo:hi] = stay + along if way > 0 else along + stay
-            s = run(order)
-            seed = (seed * 1103515245 + 12345) % 2147483648
-            if s <= score + HEAT * (1.0 - k / steps) * (seed >> 8) / 8388608:
-                score = s
-                if s < best[0]:
-                    best = (s, list(order))
-            else:
-                order[lo:hi] = part
-        return best
-    best, seed = None, 1
-    for k in range(tries):
-        way = [0.0] * n
-        for i in range(n - 1, -1, -1):
-            seed = (seed * 1103515245 + 12345) % 2147483648
-            w = lat[i] * (1.0 + (0.8 * seed / 2147483648 - 0.4 if k else 0.0))
-            way[i] = max([w] + [w + gap(i, x) - lat[i] + way[x] for x in succ[i]])
-        t = place(sorted(every, key=lambda i: (-way[i], i)), True)
-        for _ in range(3):
-            order = sorted(every, key=lambda i: (t[i], i))
-            score = run(order)
-            if best is None or score < best[0]:
-                best = (score, order)
-            late = place(sorted(every, key=lambda i: (-(t[i] + lat[i]), -i)), False)
-            t = place(sorted(every, key=lambda i: (-late[i], i)), True)
-    return polish(best[0], best[1], STEPS)[1]
 
 
 def prog(g, T):
@@ -308,11 +134,7 @@ def prog(g, T):
                         if not (r[2] == e and e != "dma" and r[0] & ~m == 0)] + [(m, tok, e)]
 
     def issue(o):
-        e = o["e"]
-        if e == "n":
-            return
-        reads = [r for r in o["reads"] if r[0][0] != "@"]
-        writes = [w for w in o["writes"] if w[0][0] != "@"]
+        e, reads, writes = o["e"], o["reads"], o["writes"]
         for s, v in o["pre"]:
             wait(e, s, v)
         n = need(e, reads, writes)
@@ -338,22 +160,9 @@ def rank_program(g, core, T, topo):
     eng, count, wait, issue = prog(g, T)
     V, S, PE = g.vector, g.scalar, g.tensor
     ops = []
-    CYC = 0.00083
-    marks = [0]
-    aside = []
 
-    def mark(name):
-        marks[0] += 1
-        return (name, 1 << marks[0])
-
-    def marked(name):
-        return (name, (1 << marks[0] + 1) - 1)
-
-    def emit(e, call, reads, writes, cost, sem=None, lat=None, pre=(), kind=0):
-        if aside == [("@ws", 1)]:
-            writes = writes + [mark("@a")]
-        ops.append({"e": e, "call": call, "reads": reads + aside, "writes": writes, "sem": sem, "pre": list(pre),
-                    "kind": kind, "hold": cost, "lat": cost if lat is None else lat})
+    def emit(e, call, reads, writes, sem=None, pre=()):
+        ops.append({"e": e, "call": call, "reads": reads, "writes": writes, "sem": sem, "pre": list(pre)})
 
     def R(name, a=0, b=None, st=1):
         if name[:2] == "ps":
@@ -367,20 +176,13 @@ def rank_program(g, core, T, topo):
     def both(x):
         return A(*x), R(*x)
 
-    def size(x):
-        return len(range(x[1] if len(x) > 1 else 0, x[2] if len(x) > 2 else SCRATCH[x[0]][1][1], x[3] if len(x) > 3 else 1))
-
-    def vcost(*xs, half=True):
-        short = all(SCRATCH[x[0]][2] in ("bfloat16", "uint16") for x in xs)
-        return 0.05 + CYC * max(64, max(size(x) for x in xs) * (0.5 if short and half else 1.0))
-
     def fill(x, c):
         a, r = both(x)
-        emit("v", lambda: V.memset(a, c), [], [r], vcost(x))
+        emit("v", lambda: V.memset(a, c), [], [r])
 
     def vcopy(o, i):
         (oa, orr), (ia, ir) = both(o), both(i)
-        emit("v", lambda: V.tensor_copy(oa, ia), [ir], [orr], vcost(o, i))
+        emit("v", lambda: V.tensor_copy(oa, ia), [ir], [orr])
 
     def vts(o, i, s1, s2, op0, op1=None, off=None):
         (oa, orr), (ia, ir) = both(o), both(i)
@@ -391,105 +193,94 @@ def rank_program(g, core, T, topo):
         if isinstance(s2, tuple):
             s2, r2 = both(s2)
             rs.append(r2)
-        cost = vcost(o, i)
         if off:
             fa, fr = both(off)
             ia = ia.indirect(fa)
             rs.append(fr)
-            cost = 0.05 + 1.5 * CYC * size(o)
         if op1 is None:
-            emit("v", lambda: V.tensor_scalar(oa, ia, s1, None, op0), rs, [orr], cost, kind=1 if off else 0)
+            emit("v", lambda: V.tensor_scalar(oa, ia, s1, None, op0), rs, [orr])
         else:
-            emit("v", lambda: V.tensor_scalar(oa, ia, s1, s2, op0, op1), rs, [orr], cost)
+            emit("v", lambda: V.tensor_scalar(oa, ia, s1, s2, op0, op1), rs, [orr])
 
     def vtt(o, i0, i1, op, off=None):
         (oa, orr), (a0, r0), (a1, r1) = both(o), both(i0), both(i1)
         rs = [r0, r1]
-        cost = vcost(o, i1, half=False)
         if off:
             fa, fr = both(off)
             a0 = a0.indirect(fa)
             rs.append(fr)
-            cost = 0.05 + 1.5 * CYC * size(o)
-        elif i0[0][:2] != "ps":
-            cost = 0.05 + CYC * max(64, 1.5 * size(o))
-        emit("v", lambda: V.tensor_tensor(oa, a0, a1, op), rs, [orr], cost, kind=1 if off else 0)
+        emit("v", lambda: V.tensor_tensor(oa, a0, a1, op), rs, [orr])
 
     def vscan(o, d0, d1, first, op0, op1):
         (oa, orr), (ma, mr), (da, dr) = both(o), both(d0), both(d1)
-        emit("v", lambda: V.tensor_tensor_scan(oa, ma, da, first, op0, op1), [mr, dr], [orr], vcost(o, d1))
+        emit("v", lambda: V.tensor_tensor_scan(oa, ma, da, first, op0, op1), [mr, dr], [orr])
 
     def vgather(o, i, off):
         (oa, orr), (ia, ir), (fa, fr) = both(o), both(i), both(off)
-        emit("v", lambda: V.tensor_copy(oa, ia.indirect(fa)), [ir, fr], [orr], 0.05 + 1.5 * CYC * size(o), kind=1)
+        emit("v", lambda: V.tensor_copy(oa, ia.indirect(fa)), [ir, fr], [orr])
 
     def vscatter(o, i, off):
         (oa, orr), (ia, ir), (fa, fr) = both(o), both(i), both(off)
-        emit("v", lambda: V.tensor_copy(oa.indirect(fa), ia), [ir, fr], [orr], 0.05 + 3.0 * CYC * size(i), kind=2)
+        emit("v", lambda: V.tensor_copy(oa.indirect(fa), ia), [ir, fr], [orr])
 
     def vtrans(o, i):
         (oa, orr), (ia, ir) = both(o), both(i)
-        emit("v", lambda: V.transpose(oa, ia), [ir], [orr], vcost(o, i))
+        emit("v", lambda: V.transpose(oa, ia), [ir], [orr])
 
     def vreduce(o, i, op):
         (oa, orr), (ia, ir) = both(o), both(i)
-        emit("v", lambda: V.tensor_reduce(oa, ia, AX.X, op), [ir], [orr], vcost(i, half=False))
+        emit("v", lambda: V.tensor_reduce(oa, ia, AX.X, op), [ir], [orr])
 
     def quant(q, a, b, x, xa, xb):
-        emit("v", lambda: V.quantize_mx(T[q][:, a:b], T[q + "s"][:, a:b], T[x][:, xa:xb]),
-             [R(x, xa, xb)], [R(q, a, b)], 0.012 + 0.00022 * (xb - xa))
+        emit("v", lambda: V.quantize_mx(T[q][:, a:b], T[q + "s"][:, a:b], T[x][:, xa:xb]), [R(x, xa, xb)], [R(q, a, b)])
 
-    def act(o, i, f, bias=0.0, scale=1.0, off=None, accum=None, more=0.0, rs=(), ws=()):
+    def act(o, i, f, bias=0.0, scale=1.0, off=None, accum=None):
         (oa, orr), (ia, ir) = both(o), both(i)
-        rs, ws = [ir] + list(rs), [orr] + list(ws)
+        rs, ws = [ir], [orr]
         if isinstance(bias, tuple):
             bias, r1 = both(bias)
             rs.append(r1)
-        cost = 0.065 + CYC * size(o) + more
         if off:
             fa, fr = both(off)
             ia = ia.indirect(fa)
             rs.append(fr)
-            cost = 0.065 + 1.5 * CYC * size(o)
         if accum:
             aa, ar = both(accum)
-            ws.append(ar)
-            emit("s", lambda: S.activation(oa, ia, f, bias=bias, scale=scale, accum_out=aa), rs, ws, cost + 0.02)
+            emit("s", lambda: S.activation(oa, ia, f, bias=bias, scale=scale, accum_out=aa), rs, ws + [ar])
         else:
-            emit("s", lambda: S.activation(oa, ia, f, bias=bias, scale=scale), rs, ws, cost, kind=1 if off else 0)
+            emit("s", lambda: S.activation(oa, ia, f, bias=bias, scale=scale), rs, ws)
 
     def mm(ps, n, w, wa, x, xa, start=True, stop=True, pre=()):
         emit("t", lambda: PE.matmul_mx(T[ps][:, 0:n], T[w][:, wa:wa + 128], T[w + "s"][:, wa:wa + 128],
                                        T[x][:, xa:xa + n], T[x + "s"][:, xa:xa + n], start, stop),
-             [R(w, wa, wa + 128), R(w + "s", wa, wa + 128), R(x, xa, xa + n)], [R(ps)], 0.5 * CYC * (n + 16), pre=pre)
+             [R(w, wa, wa + 128), R(w + "s", wa, wa + 128), R(x, xa, xa + n)], [R(ps)], pre=pre)
 
-    def dma(q, sem, oap, iap, reads, writes, lat=1.5):
-        emit(q, lambda: eng[q].dma_start(oap, iap), reads, writes, 0.06, sem=sem, lat=lat)
+    def dma(q, sem, oap, iap, reads, writes):
+        emit(q, lambda: eng[q].dma_start(oap, iap), reads, writes, sem=sem)
 
     def sel(o, i, pattern, cmp, fillv, base, cm):
         (oa, orr), (ia, ir) = both(o), both(i)
-        emit("q", lambda: g.affine_select(oa, ia, pattern, cmp, fillv, base, cm), [ir], [orr, mark("@g")], 0.17 + 2 * CYC * size(o))
+        emit("q", lambda: g.affine_select(oa, ia, pattern, cmp, fillv, base, cm), [ir], [orr])
 
     def iota(o, pattern, base, cm):
         oa, orr = both(o)
-        cost = 0.13 + 2 * CYC * size(o)
         if SCRATCH[o[0]][2] == "int32":
-            emit("q", lambda: g.iota(oa, pattern, base, cm), [], [orr, mark("@g")], cost)
+            emit("q", lambda: g.iota(oa, pattern, base, cm), [], [orr])
         else:
-            emit("q", lambda: g.iota(oa, pattern, base, cm, allow_small_or_imprecise_dtypes=True), [], [orr, mark("@g")], cost)
+            emit("q", lambda: g.iota(oa, pattern, base, cm, allow_small_or_imprecise_dtypes=True), [], [orr])
 
     cut = 4 * CUTS[0][1]
-    dma("y", "dx0", T.xs[:, 0:cut], T.x[:, 0:cut], [], [R("xs", 0, cut)], lat=2.5)
-    dma("s", "du", T.us[:, 0:512], T.u[:, 0:512], [], [R("us")], lat=2.0)
-    dma("y", "dx1", T.xs[:, cut:2048], T.x[:, cut:2048], [], [R("xs", cut, 2048)], lat=2.8)
-    dma("y", "dwc", T.qw[:, 0:512].bitcast(dt.uint8), T.wc[:, 0:2048], [], [R("qw")], lat=4.0)
-    dma("y", "dws", T.qws[:, 0:512], T.ws[:, 0:512], [], [R("qws")], lat=4.0)
-    dma("y", "dv", T.vs[:, 0:512], T.v[:, 0:512], [], [R("vs")], lat=4.0)
+    dma("y", "dx0", T.xs[:, 0:cut], T.x[:, 0:cut], [], [R("xs", 0, cut)])
+    dma("s", "du", T.us[:, 0:512], T.u[:, 0:512], [], [R("us")])
+    dma("y", "dx1", T.xs[:, cut:2048], T.x[:, cut:2048], [], [R("xs", cut, 2048)])
+    dma("y", "dwc", T.qw[:, 0:512].bitcast(dt.uint8), T.wc[:, 0:2048], [], [R("qw")])
+    dma("y", "dws", T.qws[:, 0:512], T.ws[:, 0:512], [], [R("qws")])
+    dma("y", "dv", T.vs[:, 0:512], T.v[:, 0:512], [], [R("vs")])
 
     iota(("dsr", 0, 64), [[1, 64]], -3, -4)
     iota(("dsr", 64, 516), [[1, 452]], 61, -4)
-    act(("zl", 0, 64), ("dsr", 0, 64), ACT.Sigmoid, bias=-128.0, scale=-256.0, more=1.3, ws=[("@s", 1)])
-    act(("zl", 64, 516), ("dsr", 64, 516), ACT.Sigmoid, bias=-128.0, scale=-256.0, rs=[("@s", 1)])
+    act(("zl", 0, 64), ("dsr", 0, 64), ACT.Sigmoid, bias=-128.0, scale=-256.0)
+    act(("zl", 64, 516), ("dsr", 64, 516), ACT.Sigmoid, bias=-128.0, scale=-256.0)
     vts(("zu", 0, 516), ("dsr", 0, 516), 0.0, None, OP.is_gt)
     sel(("zu", 3, 515, 4), ("zu", 3, 515, 4), [[-1, 128]], OP.not_equal, 512.0, 0, 1)
     sel(("zl", 3, 515, 4), ("zl", 3, 515, 4), [[-1, 128]], OP.not_equal, -512.0, 0, 1)
@@ -498,42 +289,44 @@ def rank_program(g, core, T, topo):
         quant("ql", 128 + 128 * c, 256 + 128 * c, "zu", 3 - c, 515 - c)
         quant("ql", 640 + 128 * c, 768 + 128 * c, "zl", 3 - c, 515 - c)
         quant("qe", 128 * c, 128 + 128 * c, "ze", 3 - c, 515 - c)
+    SR = 12 + 16 * SG
     iota(("gw0",), [[0, 8]], 0, 0)
-    fill(("one",), 1.0)
-    quant("qj", 0, 128, "one", 0, 512)
     fill(("hor",), 0.5)
     fill(("hor", 0, 128, 16), 0.0)
     fill(("hor", 6, 128, 16), -4096.0)
-    fill(("rw", 0, SR), RS)
-    fill(("rw", SR, 140), RW)
-    iota(("bt", 512, 528), [[0, 16]], 0, 0)
-    iota(("sc", 512, 2112, 528), [[0, 4]], 0, 0)
+    fill(("rw", 0, SR), RW)
+    fill(("rw", SR, 140), RS)
     for i in range(6):
         sel(("gw0",), ("gw0",), [[-16, 8]], OP.not_equal, 2.0 ** (i - 1), -i, 1)
-    quant("qu", 0, 128, "us", 0, 512)
-    iota(("kc", 0, 65), [[1, 65]], -32, 0)
-    iota(("kn", 0, 65), [[-256, 65]], 8192, 0)
-    sel(("prt",), ("one",), [[-1, 4], [-4, 32], [0, 4]], OP.is_equal, 0.0, 0, 1)
-    quant("ql", 0, 128, "prt", 0, 512)
-    iota(("tt",), [[0, 560]], 0, 0)
-    iota(("vals",), [[1, 128], [128, 4]], -256, 0)
+    iota(("kc",), [[1, 33], [32, 2]], -32, 0)
+    iota(("kn",), [[-256, 33], [-8192, 2]], 8192, 0)
     iota(("ip",), [[0, 1]], 0, 1)
-    iota(("c2",), [[1, 2]], 0, 0)
-    iota(("c16",), [[32, 4]], 2 * 513, 0)
-    iota(("ci",), [[2, 2], [32, 4], [1, 2]], 0, 0)
     vts(("ia",), ("ip",), 15, None, OP.bitwise_and)
+    iota(("lsw",), [[0, 1024]], 0, 0)
+    iota(("bt", 512, 528), [[0, 16]], 0, 0)
+    iota(("sc", 512, 2112, 528), [[0, 4]], 0, 0)
+    quant("qu", 0, 128, "us", 0, 512)
+    sel(("prt",), ("lsw", 512, 1024), [[-1, 4], [-4, 32], [0, 4]], OP.not_equal, 1.0, 0, 1)
+    iota(("lsw", 384, 512), [[0, 128]], 1, 0)
+    quant("qj", 0, 224, "lsw", 0, 896)
+    quant("ql", 0, 128, "prt", 0, 512)
+    act(("tt", 0, 512), ("dsr", 0, 512), ACT.Copy, scale=0.0)
+    act(("tt", 512, 560), ("dsr", 0, 48), ACT.Copy, scale=0.0)
+    iota(("vals",), [[1, 128], [128, 4]], -256, 0)
+    iota(("c2",), [[512, 2]], -520, 0)
+    iota(("c16",), [[32, 4]], 2 * 513, 0)
+    for z in (0, 1):
+        iota(("ci", 8 * z, 8 * z + 8), [[1, 2], [32, 2], [66, 2]], 2 * z, 0)
     vts(("i2",), ("ia",), 2.0, None, OP.mult)
-    vts(("ib",), ("ip",), 5, None, OP.arith_shift_right)
-    vts(("i3",), ("ib",), 130.0, ("i2",), OP.mult, OP.add)
-    vts(("cl16",), ("ci",), ("i3",), None, OP.add)
-    vts(("l2",), ("c2",), ("i2",), 16.0, OP.add, OP.mult)
+    vts(("cl16",), ("ci",), ("i2",), None, OP.add)
+    vts(("ic",), ("ip",), 16, None, OP.bitwise_and)
+    vts(("pc",), ("ic",), 519.5, None, OP.add)
+    act(("i4",), ("i2",), ACT.Identity, bias=("pc",), scale=16.0)
+    vts(("l2",), ("c2",), ("i4",), 0.5, OP.add, OP.add)
     vts(("dum",), ("c16",), ("i2",), 0.5, OP.add, OP.mult)
     sel(("msk0", 0, 512), ("dsr", 0, 512), [[0, 512]], OP.is_gt, BIG, -1, 0)
     sel(("neg",), ("dsr", 0, 64), [[0, 64]], OP.is_gt, -BIG, -1, 0)
     iota(("at", 0, 256), [[0, 256]], 0, 0)
-    for n in ("zt", "gt"):
-        iota((n, 256, 512), [[0, 256]], 0, 0)
-    iota(("wtt",), [[0, 576]], 0, 0)
 
     def other(x):
         return T.cores[rank ^ x]
@@ -589,20 +382,14 @@ def rank_program(g, core, T, topo):
                                                   srcs=[view(lc, a, z, plane)], dsts=[view(lc, back + a, back + z, plane)])],
                                local_sem=T.sem.sent)
             count["sent"] += k
-        every = marked("@g")
-        for z, c in enumerate(CALLS):
-            emit("q", lambda c=c: call(*c), [R(lc, 0, 128), every], [("@q", 1), ("@ws", 1), ("@w", 1 << z)], 0.4, sem="sent")
-            emit("n", None, [("@w", 1 << z)], [("@" + c[3], 1 << z)], 0.0, lat=LATS[z])
-            if c[2]:
-                emit("n", None, [("@w", 1 << z)], [("@nr", 1 << z)], 0.0, lat=1.7)
-        for z, (plane, who, k, after, sem) in enumerate(HANDS):
-            emit("q", lambda c=(plane, who, k, sem): hand(*c), [("@" + after, 255)], [("@q", 1), ("@h", 1 << z)], 0.4, sem="sent",
-                 pre=[(after + str(t), arrive[after])])
-            emit("n", None, [("@h", 1 << z)], [("@" + sem, 16 << z)], 0.0, lat=1.5)
+        for c in CALLS:
+            emit("q", lambda c=c: call(*c), [R(lc, 0, 128)], [], sem="sent")
+        for plane, who, k, after, sem in HANDS:
+            emit("q", lambda c=(plane, who, k, sem): hand(*c), [], [], sem="sent", pre=[(after + str(t), arrive[after])])
 
     def ps(i):
         return "ps%d" % i
-    HB = {2: 4, 3: 5, 0: 6}
+    HB = {2: 4, 3: 5, 0: 6, 1: 7}
 
     def key_half(t, state, h):
         qx = "qx%d" % t
@@ -619,53 +406,55 @@ def rank_program(g, core, T, topo):
                 vcopy(("yb", a, z), (ps(h), 0, z - a))
             else:
                 act(("yb", a, z), (ps(h), 0, z - a), ACT.Copy)
-            dma("y", "do%d" % h, T.oc[:, 4 * a:4 * z], T[qx][:, a:z].bitcast(dt.uint8), [R(qx, a, z)], [], lat=1.7 if h else 2.1)
-            dma("y" if h else "s", "dy%d" % h, T.y[:, a:z], T.yb[:, a:z], [R("yb", a, z)], [], lat=1.6 if h else 2.1)
+            dma("y", "do%d" % h, T.oc[:, 4 * a:4 * z], T[qx][:, a:z].bitcast(dt.uint8), [R(qx, a, z)], [])
+            for k in range(4 * h):
+                dma("y", "ds", T.osc[4 * k:4 * k + 4, :], T[qx + "s"][32 * k:32 * k + 4, :], [R(qx)], [])
+            dma("y" if h else "s", "dy%d" % h, T.y[:, a:z], T.yb[:, a:z], [R("yb", a, z)], [])
 
     key_half(0, "xs", 0)
     key_half(0, "xs", 1)
     for t in range(ROUNDS):
         qx, lc = "qx%d" % t, "lc%d" % t
         new = "st%d" % (t + 1)
-        for a in range(4):
-            for z in range(8):
-                c = 128 * (z % 4) + 32 * a + 16 * (z // 4) + 6
-                o = ("ot", 520 * a + z, 520 * a + 520, 8)
-                if z >= 8 - STHR[a]:
-                    act(o, ("kc", 0, 65), ACT.Sigmoid, bias=("kx", c, c + 1), scale=256.0, rs=[("@s", 1)])
-                else:
-                    vts(o, ("kn", 0, 65), ("kx", c, c + 1), None, OP.is_lt)
-            quant("qo", 130 * a, 130 * a + 130, "ot", 520 * a, 520 * a + 520)
-        for a in range(4):
-            for c in range(4):
-                p = ps(4 * (1 - a % 2) + c)
-                mm(p, 128, "ql", 128 + 128 * c, "qo", 130 * a + 2, True, False)
-                mm(p, 128, "ql", 640 + 128 * c, "qo", 130 * a, False, True)
-                for gg in range(2):
-                    k = 12 + 16 * (2 * a + gg) + c
-                    if k >= SR:
-                        vreduce(("rw", k, k + 1), (p, gg, 128, 2), OP.max)
+        for g0, g1, banks in PLACES:
+            n = 66 * (g1 - g0)
+            for gg in range(g0, g1):
+                for c in range(4):
+                    k, o = 128 * c + 16 * gg + 6, ("ot", 264 * gg + c, 264 * gg + 264, 4)
+                    if WHO[4 * gg + c] == "s":
+                        act(o, ("kc",), ACT.Sigmoid, bias=("kx", k, k + 1), scale=256.0)
                     else:
-                        z = 64 * (4 * (2 * a + gg) + c)
-                        act(("sj", z, z + 64), (p, gg, 128, 2), ACT.Relu, bias=-511.5, accum=("rw", k, k + 1))
-        for o in ("hi", "rv"):
-            act((o, 12, SR), ("rw", 12, SR), ACT.Identity, bias=M16 - RS)
-        vts(("hi", SR, 128), ("rw", SR, 128), M16 - RW, None, OP.add)
-        act(("rv", SR, 128), ("rw", SR, 128), ACT.Identity, bias=M16 - RW)
-        act(("tt", 48, 512, 4), ("hi", 12, 128), ACT.Identity, bias=-M16 / 512, scale=1.0 / 512)
+                        vts(o, ("kn",), ("kx", k, k + 1), None, OP.is_lt)
+            quant("qo", 66 * g0, 66 * g1, "ot", 264 * g0, 264 * g1)
+            for c in range(4):
+                p = ps(banks[c])
+                mm(p, n - 2, "ql", 128 + 128 * c, "qo", 66 * g0 + 2, True, False)
+                mm(p, n - 2, "ql", 640 + 128 * c, "qo", 66 * g0, False, True)
+                for gg in range(g0, g1):
+                    k, i = 12 + 16 * gg + c, (p, 66 * (gg - g0), 66 * (gg - g0) + 64)
+                    if k < SR:
+                        vreduce(("rw", k, k + 1), i, OP.max)
+                    else:
+                        z = 64 * (4 * gg + c)
+                        act(("sj", z, z + 64), i, ACT.Relu, bias=-511.5, accum=("rw", k, k + 1))
+        vts(("hi", 12, SR), ("rw", 12, SR), M16 - RW, None, OP.add)
+        act(("rv", 12, SR), ("rw", 12, SR), ACT.Identity, bias=M16 - RW)
+        vts(("hi", SR, 128), ("rw", SR, 128), M16 - RS, None, OP.add)
+        act(("rv", SR, 128), ("rw", SR, 128), ACT.Identity, bias=M16 - RS)
+        act(("tt", 48, 512, 4), ("hi", 12, 128), ACT.Identity, bias=-2 * M16, scale=2.0)
         vtt(("tt", 49, 512, 4), ("rv", 12, 128), ("hi", 12, 128), OP.subtract)
         quant("qt", 0, 140, "tt", 0, 560)
         for q in range(4):
-            mm("ps0", 128, "qt", 12 - 4 * q, "ql", 32 * q, q == 0, q == 3)
-        vts(("po",), ("ps0", 0, 32), 32.0, 256.0, OP.mult, OP.add)
-        for h in (0, 1):
-            mm(ps(4 + h), 260, "qj", 0, "qo", 260 * h)
-            act(("cnt", 260 * h, 260 * h + 260), (ps(4 + h), 0, 260), ACT.Copy)
+            mm(ps(PB), 128, "qt", 12 - 4 * q, "ql", 32 * q, q == 0, q == 3)
+        vts(("po",), (ps(PB), 0, 32), ("pc",), None, OP.add)
+        for a in range(4):
+            mm(ps(CB), 132, "qj", 96 - 32 * a, "qo", 132 * a, a == 0, a == 3)
+        act(("cnt",), (ps(CB), 0, 132), ACT.Copy)
         act(("cg",), ("cnt",), ACT.Identity, bias=-256.0, off=("cl16",))
         vtrans(("ctr",), ("cg",))
         for b in range(4):
-            mm(ps(6 + b % 2), 512, "qe", 128 * b, qx, 0)
-            act(("dd", 512 * b, 512 * b + 512), (ps(6 + b % 2), 0, 512), ACT.Copy, scale=0.5)
+            mm(ps(DB[b]), 512, "qe", 128 * b, qx, 0)
+            act(("dd", 512 * b, 512 * b + 512), (ps(DB[b]), 0, 512), ACT.Copy, scale=0.5)
         msk = "msk%d" % t
         lo, up = ("ctr", 0, 128, 32), ("ctr", 128, 256, 32)
         vtt(("em",), up, lo, OP.is_equal)
@@ -677,14 +466,12 @@ def rank_program(g, core, T, topo):
         vscatter((msk,), ("neg",), ("mk16",))
         vscatter(("lsw",), ("vals",), ("po",))
         vtrans(("ltr",), ("lsw",))
-        vgather(("lj",), ("ltr",), ("l2",))
-        vtrans(("lk",), ("lj",))
-        vts(("l16",), ("lk",), 256.0, None, OP.add)
+        vts(("l16",), ("ltr",), 256.0, None, OP.add, off=("l2",))
         vgather(("sd", 0, 512), ("dd", 0, 512), ("l16",))
-        vgather(("sd", 512, 768), ("dd", 512, 1024), ("l16", 0, 16))
+        vgather(("sd", 512, 512 + 16 * VG), ("dd", 512, 1024), ("l16", 0, VG))
         for b in (2, 3):
             act(("sd", 512 * b, 512 * b + 512), ("dd", 512 * b, 512 * b + 512), ACT.Copy, off=("l16",))
-        act(("sd", 768, 1024), ("dd", 512, 1024), ACT.Copy, off=("l16", 16, 32))
+        act(("sd", 512 + 16 * VG, 1024), ("dd", 512, 1024), ACT.Copy, off=("l16", VG, 32))
         for b in (0, 2, 3, 1):
             vscan(("sc", 528 * b, 528 * b + 512), (msk, 0, 512), ("sd", 512 * b, 512 * b + 512), -BIG, OP.min, OP.max)
             o, i = ("at", 256 + b, 512, 4), ("sc", 528 * b, 528 * b + 513)
@@ -694,8 +481,10 @@ def rank_program(g, core, T, topo):
                 vts(o, i, 2.0, None, OP.mult, off=("pk16",))
         quant(lc, 0, 128, "at", 0, 512)
         send(t)
-        aside.append(("@ws", 1))
         if t == 0:
+            for n in ("zt", "gt"):
+                iota((n, 256, 512), [[0, 256]], 0, 0)
+            fill(("wtt",), 0.0)
             for b in range(4):
                 act(("wtt", 48 + 5 * b, 560, 64), ("gw0",), ACT.Copy)
             quant("qn", 0, 144, "wtt", 0, 576)
@@ -716,30 +505,19 @@ def rank_program(g, core, T, topo):
             mm(ps(b), 128, "qn", 12 + b - b % 2, "qc" if b % 2 else "qb", 0)
             act(("kf", b, 512, 4), (ps(b), 0, 128), ACT.Identity, bias=31.5)
         dma("y", "dk%d" % t, T.kl[8 * t:8 * t + 8, :], T.kf[0:128:16, :], [R("kf")], [])
-        for b in (2, 3, 0):
-            mm(ps(HB[b]), 512, "qh", 128 * b, qx, 0)
-        aside.pop()
-        aside.extend([("@nr", 4095), marked("@a")])
         for b in range(4):
-            mm(ps(b), 128, "qe", 128 * b, lc, 64, pre=[("nr%d" % t, arrive["nr"])])
-            act(("own", b, 512, 4), (ps(b), 0, 128), ACT.Copy)
-        del aside[:]
-        for z, (a, n, sems) in enumerate(LOTS):
-            aside.extend([("@" + s, 4095) for s in sems] + [marked("@a")])
+            mm(ps(b), 128, "qe", 128 * b, lc, 0)
+            act(("mm", b, 256, 4), (ps(b), 64, 128), ACT.Copy)
+        for z, (a, n, k, sems) in enumerate(LOTS):
             for b in range(4):
-                mm(ps(b), 64 * n, "qe", 128 * b, lc, 64 * (3 + a), pre=[(s + str(t), arrive[s]) for s in sems])
-            del aside[:]
-            if z < WIDE:
+                mm(ps(k + b), 128, "qe", 128 * b, lc, 64 * (a + n), pre=[(s + str(t), arrive[s]) for s in sems])
+            for s in range(n):
                 for b in range(4):
-                    w = ("own", b, 512, 4)
-                    vtt(w, (ps(b), 0, 128), w, OP.max)
-                if z == WIDE - 1:
-                    vtt(("mm",), ("own", 0, 256), ("own", 256, 512), OP.max)
-            else:
-                for s in range(n):
-                    for b in range(4):
-                        w = ("mm", b, 256, 4)
-                        vtt(("zt", b, 256, 4) if (z, s) == (len(LOTS) - 1, n - 1) else w, (ps(b), 64 * s, 64 * s + 64), w, OP.max)
+                    w = ("mm", b, 256, 4)
+                    vtt(("zt", b, 256, 4) if (z, s) == (len(LOTS) - 1, n - 1) else w,
+                        (ps(k + b), 64 * (s + 2 - n), 64 * (s + 3 - n)), w, OP.max)
+        for b in MINE[t][1]:
+            mm(ps(HB[b]), 512, "qh", 128 * b, qx, 0)
         quant("qz", 0, 128, "zt", 0, 512)
         for b in (0, 2, 1, 3):
             mm(ps(b), 128, "qw", 128 * b, "qz", 0)
@@ -770,16 +548,10 @@ def rank_program(g, core, T, topo):
                     vtt(o, (ps(HB[b]), a, z), ("ge", 512 * b + a, 512 * b + z), OP.add)
                 else:
                     vtt(o, ("gb", 64 * b, 64 * b + 64), ("dd", 512 * b + a, 512 * b + z), OP.add, off=off)
-        for h in (0, 1):
             key_half(t + 1, new, h)
 
-    qx = "qx%d" % ROUNDS
-    for k in range(4):
-        dma("y", "ds", T.osc[4 * k:4 * k + 4, :], T[qx + "s"][32 * k:32 * k + 4, :], [R(qx)], [])
-    if not _PLAN:
-        _PLAN.extend(plan(ops, TRIES))
-    for i in _PLAN:
-        issue(ops[i])
+    for i in range(0, len(ORDER), 2):
+        issue(ops[int(ORDER[i:i + 2], 36)])
     for t in range(ROUNDS):
         for s in arrive:
             count[s + str(t)] = arrive[s]

from concourse.bass import DstId, RemoteDMATransfer
from concourse.mybir import dt, AluOpType, AxisListType, ActivationFunctionType

OP, ACT, AX = AluOpType, ActivationFunctionType, AxisListType
ROUNDS = 2
BIG = 2.0 ** 60
M16 = 3072.0
SG = 4
RW = 775.5
RS = 264.0
WHO = "vvvs" * 2 + "vvvv" * 2 + "vsvs" + "vvss" * 3
PLACES = ((4, 6, (4, 5, 6, 7)), (0, 2, (0, 1, 2, 3)), (6, 8, (4, 5, 6, 7)), (2, 4, (0, 1, 2, 3)))
CB, DB, PB = 4, (6, 7, 6, 7), 0
CUTS = ((0, 384, 512), (0, 384, 512), (0, 320, 512))
MINE = (((2, 3), (2, 3)), ((2, 3), (2, 3, 0)))
VG = 12
FWD = 2
SLOTS = "nhlf"
CALLS = ((0, "h", 4, "ca"), (1, "hl", 4, "sa"), (0, "l", 0, "cb"), (1, "f", 0, "fa"))
HANDS = ((0, "h", 8, "ca", "ha"),)
LOTS = ((0, 1, 4, ("nr",)), (1, 2, 0, ("sa", "ca")), (3, 2, 4, ("cb",)), (5, 2, 0, ("fa", "ha")))
ORDER = ("0001020304050614150u0v0r1l1n1o0t0s070a0d1v1h0b1908090c131i221w1z12161k1j171b0q1t0w1a181g0e0h0k25231x200o0f0l241y210n2627282d292b2e3330342f2a2g2c2h313u3t3q351f2u2v2x3p2q2i2r2m4g2z3o2y320i3n2j2n364e3s3r4d4f4h3f3g3v3b3c37383j2w2s2t2p2k2l2o1e3k44483w493x4540414c3h4i4j3a3d3e4k3l3m4p4q3i391c4x4y4l4r4s4z504m4t4u4o4n4w4v4a3y42463z431p4b475d54525e5f5g1m53510g561d5h55575i0p0m0j1r5j5k5l58595a5b5m5c5s5z1q5t0x0y1s1u0z1011605v5u615x5w5n635y62705o5q5p5r65646b6766696d6c686a6e6f6n716p6o6r6q6g6h726y73746s757c7g76777a7e7h7d7b7f7p787l7n7j6z6t6x6u6w6v797m7q7o7k7u7s7r7t7y7w7v7x8280817z86848583888a89876i8c8e8d8b8g8i8h6j6k8o8q8n8p8f8k8m8j8l8s8u8r8t8w8y8v8x7i6m6l9192959493969899979a9d9b9e9c8z909h9f9i9g9k9j9za09m9l9o9na29pa1a4a39q9t9w9r9x9ua5a69s9ya7b29va9b4adaaafbta8acagaeabboayb3ahazb0cicfbnb5b1b6chbpbubqamanaiajauavaqapaobrbscjcebvcccdarbjbbcgbkbfbgbhalaxakb7bcawbwbxc8b8blckbmbibdb9baatasc9c4c0c1cxcyctcubec5clcmczd0cwcvcncocpbybzcac3cbc2c7c6cqddcscrded3d1dfdgdkdmd4d2dhd5d6d7d8d9dadbdidjdsdcdndldqdoeldpdrdtdzdue0dwdve1dye5e6e2e3e7ebdxede4e9ece8eaemeeefepeneof1exf2evezf0faeqereseweyetf6f8f4egeheuf9f7f5fbfefdfffceif3fkflfnfmfifgfhfjfofpfrfqftfsfvfufwg0fzfyg3fxg2g1ejekgbg8g9gag7g4g5g6gfgcgdgegjggghgigngqgrgogpgugsgvgtgwgmgzgxh0gyglgkh4h2h3h1h5h6hhhgh8hjh7h9hahihlhbhkhmhehnhqhrhshthuhchohdhphfhv")

SCRATCH = {}


def _b(names, n, dtype="bfloat16"):
    for name in names.split():
        SCRATCH[name] = ("sbuf", [128, n], dtype)


def _codes(names, n):
    for name in names.split():
        SCRATCH[name] = ("sbuf", [128, n], "float8_e4m3fn_x4")
        SCRATCH[name + "s"] = ("sbuf", [128, n], "uint8")


_b("xs st1 st2 dd sd ge sj", 2048)
_b("us vs at zt gt vals prt bu kx", 512)
_b("lsw ltr", 1024)
_b("hor", 128)
_b("gw0", 8)
_b("dsr bt zu zl ze zh", 528)
_b("kc kn", 66)
_b("wtt", 576)
_b("ot sc", 2112)
_b("tt", 560)
_b("msk0 msk1", 1104)
_b("neg", 64)
_b("mm gb cg ctr", 256)
_b("hi", 140)
_b("rw rv", 140, "float32")
_b("kf yb", 512, "float32")
_b("cnt", 132, "float32")
_b("ci", 16, "float32")
_b("em dm mk pk dum c16", 4, "float32")
_b("c2", 2, "float32")
_b("i2 i4 pc", 1, "float32")
_b("ip ia ic", 1, "int32")
_b("po ko l16", 32, "uint16")
_b("cl16", 16, "uint16")
_b("mk16 pk16", 4, "uint16")
_b("l2", 2, "uint16")
_codes("qu qv qc qz qg", 128)
_codes("qb qd", 130)
_codes("qn", 144)
_codes("qj", 224)
_codes("qx0 qx1 qx2 qw qe qh", 512)
_codes("ql", 1152)
_codes("qo", 528)
_codes("qt", 140)
_codes("lc0 lc1", 576)
for _i in range(8):
    SCRATCH["ps%d" % _i] = ("psum", [128, 512], "float32")

SEMAPHORES = ["cv", "cs", "ct", "cq", "nr0", "nr1", "sa0", "sa1", "ca0", "ca1", "cb0", "cb1", "fa0", "fa1", "ha0", "ha1",
              "sent", "dx0", "dx1", "du", "dv", "dwc", "dws", "dk0", "dk1", "dy0", "dy1", "do0", "do1", "ds"]

_MASKS = {}


def _cols(a, b, st):
    if (a, b, st) not in _MASKS:
        m = 0
        for i in range(a, b, st):
            m |= 1 << i
        _MASKS[(a, b, st)] = m
    return _MASKS[(a, b, st)]


def prog(g, T):
    eng = {"v": g.vector, "s": g.scalar, "t": g.tensor, "q": g, "y": g.sync}
    csem = {"v": "cv", "s": "cs", "t": "ct", "q": "cq"}
    count = {s: 0 for s in SEMAPHORES}
    known = {e: {} for e in eng}
    snap = {}
    wr, rd = {}, {}

    def wait(e, sem, val):
        if known[e].get(sem, 0) < val:
            eng[e].wait_ge(T.sem[sem], val)
            for s, k in snap.get((sem, val), {}).items():
                if known[e].get(s, 0) < k:
                    known[e][s] = k
            known[e][sem] = val

    def need(e, reads, writes):
        n = {}

        def add(tok):
            if n.get(tok[0], 0) < tok[1]:
                n[tok[0]] = tok[1]
        for name, m in reads:
            psum = name[:2] == "ps"
            for wm, tok, we in wr.get(name, []):
                if wm & m and not (psum and we == e):
                    add(tok)
            if psum:
                for rm, tok, re_ in rd.get(name, []):
                    if re_ != e:
                        add(tok)
        for name, m in writes:
            for om, tok, oe in wr.get(name, []) + rd.get(name, []):
                if om & m and not (e == "t" and oe == "t"):
                    add(tok)
        return n

    def note(e, reads, writes, tok):
        for name, m in writes:
            wr[name] = [w for w in wr.get(name, []) if w[0] & ~m] + [(m, tok, e)]
            rd[name] = [r for r in rd.get(name, []) if r[0] & ~m]
        for name, m in reads:
            rd[name] = [r for r in rd.get(name, [])
                        if not (r[2] == e and e != "dma" and r[0] & ~m == 0)] + [(m, tok, e)]

    def issue(o):
        e, reads, writes = o["e"], o["reads"], o["writes"]
        for s, v in o["pre"]:
            wait(e, s, v)
        n = need(e, reads, writes)
        for s in sorted(n, key=lambda s: -n[s]):
            wait(e, s, n[s])
        if o["sem"] == "sent":
            o["call"]()
            return
        s = o["sem"] or csem[e]
        k = 16 if o["sem"] else 1
        o["call"]().then_inc(T.sem[s], k)
        count[s] += k
        snap[(s, count[s])] = dict(known[e])
        note("dma" if o["sem"] else e, reads, writes, (s, count[s]))
    return eng, count, wait, issue


def rank_program(g, core, T, topo):
    rank = T.rank_of(core)
    if rank is None:
        return
    N = len(T.cores)
    eng, count, wait, issue = prog(g, T)
    V, S, PE = g.vector, g.scalar, g.tensor
    ops = []

    def emit(e, call, reads, writes, sem=None, pre=()):
        ops.append({"e": e, "call": call, "reads": reads, "writes": writes, "sem": sem, "pre": list(pre)})

    def R(name, a=0, b=None, st=1):
        if name[:2] == "ps":
            return (name, 1)
        return (name, _cols(a, SCRATCH[name][1][1] if b is None else b, st))

    def A(name, a=0, b=None, st=1):
        b = SCRATCH[name][1][1] if b is None else b
        return T[name][:, a:b] if st == 1 else T[name][:, a:b:st]

    def both(x):
        return A(*x), R(*x)

    def fill(x, c):
        a, r = both(x)
        emit("v", lambda: V.memset(a, c), [], [r])

    def vcopy(o, i):
        (oa, orr), (ia, ir) = both(o), both(i)
        emit("v", lambda: V.tensor_copy(oa, ia), [ir], [orr])

    def vts(o, i, s1, s2, op0, op1=None, off=None):
        (oa, orr), (ia, ir) = both(o), both(i)
        rs = [ir]
        if isinstance(s1, tuple):
            s1, r1 = both(s1)
            rs.append(r1)
        if isinstance(s2, tuple):
            s2, r2 = both(s2)
            rs.append(r2)
        if off:
            fa, fr = both(off)
            ia = ia.indirect(fa)
            rs.append(fr)
        if op1 is None:
            emit("v", lambda: V.tensor_scalar(oa, ia, s1, None, op0), rs, [orr])
        else:
            emit("v", lambda: V.tensor_scalar(oa, ia, s1, s2, op0, op1), rs, [orr])

    def vtt(o, i0, i1, op, off=None):
        (oa, orr), (a0, r0), (a1, r1) = both(o), both(i0), both(i1)
        rs = [r0, r1]
        if off:
            fa, fr = both(off)
            a0 = a0.indirect(fa)
            rs.append(fr)
        emit("v", lambda: V.tensor_tensor(oa, a0, a1, op), rs, [orr])

    def vscan(o, d0, d1, first, op0, op1):
        (oa, orr), (ma, mr), (da, dr) = both(o), both(d0), both(d1)
        emit("v", lambda: V.tensor_tensor_scan(oa, ma, da, first, op0, op1), [mr, dr], [orr])

    def vgather(o, i, off):
        (oa, orr), (ia, ir), (fa, fr) = both(o), both(i), both(off)
        emit("v", lambda: V.tensor_copy(oa, ia.indirect(fa)), [ir, fr], [orr])

    def vscatter(o, i, off):
        (oa, orr), (ia, ir), (fa, fr) = both(o), both(i), both(off)
        emit("v", lambda: V.tensor_copy(oa.indirect(fa), ia), [ir, fr], [orr])

    def vtrans(o, i):
        (oa, orr), (ia, ir) = both(o), both(i)
        emit("v", lambda: V.transpose(oa, ia), [ir], [orr])

    def vreduce(o, i, op):
        (oa, orr), (ia, ir) = both(o), both(i)
        emit("v", lambda: V.tensor_reduce(oa, ia, AX.X, op), [ir], [orr])

    def quant(q, a, b, x, xa, xb):
        emit("v", lambda: V.quantize_mx(T[q][:, a:b], T[q + "s"][:, a:b], T[x][:, xa:xb]), [R(x, xa, xb)], [R(q, a, b)])

    def act(o, i, f, bias=0.0, scale=1.0, off=None, accum=None):
        (oa, orr), (ia, ir) = both(o), both(i)
        rs, ws = [ir], [orr]
        if isinstance(bias, tuple):
            bias, r1 = both(bias)
            rs.append(r1)
        if off:
            fa, fr = both(off)
            ia = ia.indirect(fa)
            rs.append(fr)
        if accum:
            aa, ar = both(accum)
            emit("s", lambda: S.activation(oa, ia, f, bias=bias, scale=scale, accum_out=aa), rs, ws + [ar])
        else:
            emit("s", lambda: S.activation(oa, ia, f, bias=bias, scale=scale), rs, ws)

    def mm(ps, n, w, wa, x, xa, start=True, stop=True, pre=()):
        emit("t", lambda: PE.matmul_mx(T[ps][:, 0:n], T[w][:, wa:wa + 128], T[w + "s"][:, wa:wa + 128],
                                       T[x][:, xa:xa + n], T[x + "s"][:, xa:xa + n], start, stop),
             [R(w, wa, wa + 128), R(w + "s", wa, wa + 128), R(x, xa, xa + n)], [R(ps)], pre=pre)

    def dma(q, sem, oap, iap, reads, writes):
        emit(q, lambda: eng[q].dma_start(oap, iap), reads, writes, sem=sem)

    def sel(o, i, pattern, cmp, fillv, base, cm):
        (oa, orr), (ia, ir) = both(o), both(i)
        emit("q", lambda: g.affine_select(oa, ia, pattern, cmp, fillv, base, cm), [ir], [orr])

    def iota(o, pattern, base, cm):
        oa, orr = both(o)
        if SCRATCH[o[0]][2] == "int32":
            emit("q", lambda: g.iota(oa, pattern, base, cm), [], [orr])
        else:
            emit("q", lambda: g.iota(oa, pattern, base, cm, allow_small_or_imprecise_dtypes=True), [], [orr])

    cut = 4 * CUTS[0][1]
    dma("y", "dx0", T.xs[:, 0:cut], T.x[:, 0:cut], [], [R("xs", 0, cut)])
    dma("s", "du", T.us[:, 0:512], T.u[:, 0:512], [], [R("us")])
    dma("y", "dx1", T.xs[:, cut:2048], T.x[:, cut:2048], [], [R("xs", cut, 2048)])
    dma("y", "dwc", T.qw[:, 0:512].bitcast(dt.uint8), T.wc[:, 0:2048], [], [R("qw")])
    dma("y", "dws", T.qws[:, 0:512], T.ws[:, 0:512], [], [R("qws")])
    dma("y", "dv", T.vs[:, 0:512], T.v[:, 0:512], [], [R("vs")])

    iota(("dsr", 0, 64), [[1, 64]], -3, -4)
    iota(("dsr", 64, 516), [[1, 452]], 61, -4)
    act(("zl", 0, 64), ("dsr", 0, 64), ACT.Sigmoid, bias=-128.0, scale=-256.0)
    act(("zl", 64, 516), ("dsr", 64, 516), ACT.Sigmoid, bias=-128.0, scale=-256.0)
    vts(("zu", 0, 516), ("dsr", 0, 516), 0.0, None, OP.is_gt)
    sel(("zu", 3, 515, 4), ("zu", 3, 515, 4), [[-1, 128]], OP.not_equal, 512.0, 0, 1)
    sel(("zl", 3, 515, 4), ("zl", 3, 515, 4), [[-1, 128]], OP.not_equal, -512.0, 0, 1)
    vts(("ze", 0, 516), ("dsr", 0, 516), 0.0, None, OP.is_equal)
    for c in range(4):
        quant("ql", 128 + 128 * c, 256 + 128 * c, "zu", 3 - c, 515 - c)
        quant("ql", 640 + 128 * c, 768 + 128 * c, "zl", 3 - c, 515 - c)
        quant("qe", 128 * c, 128 + 128 * c, "ze", 3 - c, 515 - c)
    SR = 12 + 16 * SG
    iota(("gw0",), [[0, 8]], 0, 0)
    fill(("hor",), 0.5)
    fill(("hor", 0, 128, 16), 0.0)
    fill(("hor", 6, 128, 16), -4096.0)
    fill(("rw", 0, SR), RW)
    fill(("rw", SR, 140), RS)
    for i in range(6):
        sel(("gw0",), ("gw0",), [[-16, 8]], OP.not_equal, 2.0 ** (i - 1), -i, 1)
    iota(("kc",), [[1, 33], [32, 2]], -32, 0)
    iota(("kn",), [[-256, 33], [-8192, 2]], 8192, 0)
    iota(("ip",), [[0, 1]], 0, 1)
    vts(("ia",), ("ip",), 15, None, OP.bitwise_and)
    iota(("lsw",), [[0, 1024]], 0, 0)
    iota(("bt", 512, 528), [[0, 16]], 0, 0)
    iota(("sc", 512, 2112, 528), [[0, 4]], 0, 0)
    quant("qu", 0, 128, "us", 0, 512)
    sel(("prt",), ("lsw", 512, 1024), [[-1, 4], [-4, 32], [0, 4]], OP.not_equal, 1.0, 0, 1)
    iota(("lsw", 384, 512), [[0, 128]], 1, 0)
    quant("qj", 0, 224, "lsw", 0, 896)
    quant("ql", 0, 128, "prt", 0, 512)
    act(("tt", 0, 512), ("dsr", 0, 512), ACT.Copy, scale=0.0)
    act(("tt", 512, 560), ("dsr", 0, 48), ACT.Copy, scale=0.0)
    iota(("vals",), [[1, 128], [128, 4]], -256, 0)
    iota(("c2",), [[512, 2]], -520, 0)
    iota(("c16",), [[32, 4]], 2 * 513, 0)
    for z in (0, 1):
        iota(("ci", 8 * z, 8 * z + 8), [[1, 2], [32, 2], [66, 2]], 2 * z, 0)
    vts(("i2",), ("ia",), 2.0, None, OP.mult)
    vts(("cl16",), ("ci",), ("i2",), None, OP.add)
    vts(("ic",), ("ip",), 16, None, OP.bitwise_and)
    vts(("pc",), ("ic",), 519.5, None, OP.add)
    act(("i4",), ("i2",), ACT.Identity, bias=("pc",), scale=16.0)
    vts(("l2",), ("c2",), ("i4",), 0.5, OP.add, OP.add)
    vts(("dum",), ("c16",), ("i2",), 0.5, OP.add, OP.mult)
    sel(("msk0", 0, 512), ("dsr", 0, 512), [[0, 512]], OP.is_gt, BIG, -1, 0)
    sel(("neg",), ("dsr", 0, 64), [[0, 64]], OP.is_gt, -BIG, -1, 0)
    iota(("at", 0, 256), [[0, 256]], 0, 0)

    def other(x):
        return T.cores[rank ^ x]
    near = [x for x in range(1, N) if topo.chip(other(x)) == topo.chip(core)][0]

    def hops(x):
        a, b = topo.chip(core), topo.chip(other(x))
        return 0 if topo.mates(a, b) else 1 if topo.same_plane(a, b) else 2
    level = sorted([x for x in range(1, N) if x != near and topo.die(other(x)) == topo.die(core)], key=lambda x: -hops(x))
    far = level + [x ^ near for x in level[FWD:]]
    named = {"h": far[:FWD], "l": far[FWD:], "n": [near], "f": [x ^ near for x in far[:FWD]]}

    def ranks(who):
        return sum([named[c] for c in who], [])
    slot = {x: 128 + 64 * k for k, x in enumerate(ranks(SLOTS))}
    back = 64 * len(far)
    fmask = topo.mask(core, other(level[0]))
    rest = [e for e in topo.engines(core, other(near)) if not fmask >> e & 1]
    nf = bin(fmask).count("1")

    def some(k):
        return sum(1 << e for e in rest[:k])
    arrive = {"nr": 0}
    for plane, who, k, sem in CALLS:
        arrive[sem] = arrive.get(sem, 0) + nf * len(ranks(who))
        arrive["nr"] += k
    for plane, who, k, after, sem in HANDS:
        arrive[sem] = arrive.get(sem, 0) + k

    def view(name, a, b, plane):
        return T[name + "s"][:, a:b] if plane else T[name][:, a:b].bitcast(dt.uint8)

    def dst(x):
        rid, pid = topo.addr(other(x))[:2]
        return DstId(rid=rid, pnc=pid)

    def send(t):
        lc = "lc%d" % t

        def call(plane, who, k, sem):
            ts = []
            for group, m, s in ((ranks(who), fmask, sem), ([near] if k else [], some(k), "nr")):
                if group:
                    ts.append(RemoteDMATransfer(dst_ids=[dst(x) for x in group], dma_engine_mask=m, remote_sem=T.sem[s + str(t)],
                                                srcs=[view(lc, 64, 128, plane)],
                                                dsts=[view(lc, slot[x], slot[x] + 64, plane) for x in group]))
                    count["sent"] += bin(m).count("1")
            g.remote_dma_fused(ts, local_sem=T.sem.sent)

        def hand(plane, who, k, sem):
            a, z = min(slot[x] for x in ranks(who)), max(slot[x] for x in ranks(who)) + 64
            g.remote_dma_fused([RemoteDMATransfer(dst_ids=[dst(near)], dma_engine_mask=some(k), remote_sem=T.sem[sem + str(t)],
                                                  srcs=[view(lc, a, z, plane)], dsts=[view(lc, back + a, back + z, plane)])],
                               local_sem=T.sem.sent)
            count["sent"] += k
        for c in CALLS:
            emit("q", lambda c=c: call(*c), [R(lc, 0, 128)], [], sem="sent")
        for plane, who, k, after, sem in HANDS:
            emit("q", lambda c=(plane, who, k, sem): hand(*c), [], [], sem="sent", pre=[(after + str(t), arrive[after])])

    def ps(i):
        return "ps%d" % i
    HB = {2: 4, 3: 5, 0: 6, 1: 7}

    def key_half(t, state, h):
        qx = "qx%d" % t
        a, z = CUTS[t][h], CUTS[t][h + 1]
        quant(qx, a, z, state, 4 * a, 4 * z)
        if t < ROUNDS:
            for c in range(a, z, 128):
                mm(ps(c // 128), 128, qx, c, "qu", 0)
                act(("bu", c, c + 128), (ps(c // 128), 0, 128), ACT.Sign, bias=-(2.0 ** -100))
                vscan(("kx", c, c + 128), ("hor",), ("bu", c, c + 128), 0.0, OP.mult, OP.add)
        else:
            mm(ps(h), z - a, "qv", 0, qx, a)
            if h:
                vcopy(("yb", a, z), (ps(h), 0, z - a))
            else:
                act(("yb", a, z), (ps(h), 0, z - a), ACT.Copy)
            dma("y", "do%d" % h, T.oc[:, 4 * a:4 * z], T[qx][:, a:z].bitcast(dt.uint8), [R(qx, a, z)], [])
            for k in range(4 * h):
                dma("y", "ds", T.osc[4 * k:4 * k + 4, :], T[qx + "s"][32 * k:32 * k + 4, :], [R(qx)], [])
            dma("y" if h else "s", "dy%d" % h, T.y[:, a:z], T.yb[:, a:z], [R("yb", a, z)], [])

    key_half(0, "xs", 0)
    key_half(0, "xs", 1)
    for t in range(ROUNDS):
        qx, lc = "qx%d" % t, "lc%d" % t
        new = "st%d" % (t + 1)
        for g0, g1, banks in PLACES:
            n = 66 * (g1 - g0)
            for gg in range(g0, g1):
                for c in range(4):
                    k, o = 128 * c + 16 * gg + 6, ("ot", 264 * gg + c, 264 * gg + 264, 4)
                    if WHO[4 * gg + c] == "s":
                        act(o, ("kc",), ACT.Sigmoid, bias=("kx", k, k + 1), scale=256.0)
                    else:
                        vts(o, ("kn",), ("kx", k, k + 1), None, OP.is_lt)
            quant("qo", 66 * g0, 66 * g1, "ot", 264 * g0, 264 * g1)
            for c in range(4):
                p = ps(banks[c])
                mm(p, n - 2, "ql", 128 + 128 * c, "qo", 66 * g0 + 2, True, False)
                mm(p, n - 2, "ql", 640 + 128 * c, "qo", 66 * g0, False, True)
                for gg in range(g0, g1):
                    k, i = 12 + 16 * gg + c, (p, 66 * (gg - g0), 66 * (gg - g0) + 64)
                    if k < SR:
                        vreduce(("rw", k, k + 1), i, OP.max)
                    else:
                        z = 64 * (4 * gg + c)
                        act(("sj", z, z + 64), i, ACT.Relu, bias=-511.5, accum=("rw", k, k + 1))
        vts(("hi", 12, SR), ("rw", 12, SR), M16 - RW, None, OP.add)
        act(("rv", 12, SR), ("rw", 12, SR), ACT.Identity, bias=M16 - RW)
        vts(("hi", SR, 128), ("rw", SR, 128), M16 - RS, None, OP.add)
        act(("rv", SR, 128), ("rw", SR, 128), ACT.Identity, bias=M16 - RS)
        act(("tt", 48, 512, 4), ("hi", 12, 128), ACT.Identity, bias=-2 * M16, scale=2.0)
        vtt(("tt", 49, 512, 4), ("rv", 12, 128), ("hi", 12, 128), OP.subtract)
        quant("qt", 0, 140, "tt", 0, 560)
        for q in range(4):
            mm(ps(PB), 128, "qt", 12 - 4 * q, "ql", 32 * q, q == 0, q == 3)
        vts(("po",), (ps(PB), 0, 32), ("pc",), None, OP.add)
        for a in range(4):
            mm(ps(CB), 132, "qj", 96 - 32 * a, "qo", 132 * a, a == 0, a == 3)
        act(("cnt",), (ps(CB), 0, 132), ACT.Copy)
        act(("cg",), ("cnt",), ACT.Identity, bias=-256.0, off=("cl16",))
        vtrans(("ctr",), ("cg",))
        for b in range(4):
            mm(ps(DB[b]), 512, "qe", 128 * b, qx, 0)
            act(("dd", 512 * b, 512 * b + 512), (ps(DB[b]), 0, 512), ACT.Copy, scale=0.5)
        msk = "msk%d" % t
        lo, up = ("ctr", 0, 128, 32), ("ctr", 128, 256, 32)
        vtt(("em",), up, lo, OP.is_equal)
        vtt(("dm",), ("em",), ("dum",), OP.mult)
        vtt(("mk",), lo, ("dm",), OP.add)
        vtt(("pk",), up, ("dm",), OP.add)
        vts(("mk16",), ("mk",), 256.0, None, OP.add)
        vts(("pk16",), ("pk",), 255.0, 512.0, OP.add, OP.min)
        vscatter((msk,), ("neg",), ("mk16",))
        vscatter(("lsw",), ("vals",), ("po",))
        vtrans(("ltr",), ("lsw",))
        vts(("l16",), ("ltr",), 256.0, None, OP.add, off=("l2",))
        vgather(("sd", 0, 512), ("dd", 0, 512), ("l16",))
        vgather(("sd", 512, 512 + 16 * VG), ("dd", 512, 1024), ("l16", 0, VG))
        for b in (2, 3):
            act(("sd", 512 * b, 512 * b + 512), ("dd", 512 * b, 512 * b + 512), ACT.Copy, off=("l16",))
        act(("sd", 512 + 16 * VG, 1024), ("dd", 512, 1024), ACT.Copy, off=("l16", VG, 32))
        for b in (0, 2, 3, 1):
            vscan(("sc", 528 * b, 528 * b + 512), (msk, 0, 512), ("sd", 512 * b, 512 * b + 512), -BIG, OP.min, OP.max)
            o, i = ("at", 256 + b, 512, 4), ("sc", 528 * b, 528 * b + 513)
            if b != 1:
                act(o, i, ACT.Copy, scale=2.0, off=("pk16",))
            else:
                vts(o, i, 2.0, None, OP.mult, off=("pk16",))
        quant(lc, 0, 128, "at", 0, 512)
        send(t)
        if t == 0:
            for n in ("zt", "gt"):
                iota((n, 256, 512), [[0, 256]], 0, 0)
            fill(("wtt",), 0.0)
            for b in range(4):
                act(("wtt", 48 + 5 * b, 560, 64), ("gw0",), ACT.Copy)
            quant("qn", 0, 144, "wtt", 0, 576)
            vts(("zh", 0, 516), ("ze", 0, 516), 0.5, None, OP.mult)
            for c in range(4):
                quant("qh", 128 * c, 128 + 128 * c, "zh", 3 - c, 515 - c)
            quant("qv", 0, 128, "vs", 0, 512)
            fill(("msk1", 0, 512), BIG)
        mm("ps0", 512, "qu", 0, qx, 0)
        act(("bt", 0, 512), ("ps0", 0, 512), ACT.Sign, bias=-(2.0 ** -100))
        quant("qb", 0, 130, "bt", 0, 520)
        quant("qd", 0, 130, "bt", 4, 524)
        quant("qc", 0, 128, "bt", 1, 513)
        for q in range(4):
            mm("ps7", 128, "qn", 12 - 4 * q, "qd" if q % 2 else "qb", q - q % 2, q == 0, q == 3)
        vts(("ko",), ("ps7", 0, 128, 4), 31.5, None, OP.add)
        for b in range(4):
            mm(ps(b), 128, "qn", 12 + b - b % 2, "qc" if b % 2 else "qb", 0)
            act(("kf", b, 512, 4), (ps(b), 0, 128), ACT.Identity, bias=31.5)
        dma("y", "dk%d" % t, T.kl[8 * t:8 * t + 8, :], T.kf[0:128:16, :], [R("kf")], [])
        for b in range(4):
            mm(ps(b), 128, "qe", 128 * b, lc, 0)
            act(("mm", b, 256, 4), (ps(b), 64, 128), ACT.Copy)
        for z, (a, n, k, sems) in enumerate(LOTS):
            for b in range(4):
                mm(ps(k + b), 128, "qe", 128 * b, lc, 64 * (a + n), pre=[(s + str(t), arrive[s]) for s in sems])
            for s in range(n):
                for b in range(4):
                    w = ("mm", b, 256, 4)
                    vtt(("zt", b, 256, 4) if (z, s) == (len(LOTS) - 1, n - 1) else w,
                        (ps(k + b), 64 * (s + 2 - n), 64 * (s + 3 - n)), w, OP.max)
        for b in MINE[t][1]:
            mm(ps(HB[b]), 512, "qh", 128 * b, qx, 0)
        quant("qz", 0, 128, "zt", 0, 512)
        for b in (0, 2, 1, 3):
            mm(ps(b), 128, "qw", 128 * b, "qz", 0)
        for b in (0, 2, 1, 3):
            o, i = ("gt", b, 256, 4), (ps(b), 0, 64)
            if b in (0, 1):
                act(o, i, ACT.Relu, scale=0.015625)
            else:
                vts(o, i, 0.0, 0.015625, OP.max, OP.mult)
        quant("qg", 0, 128, "gt", 0, 512)
        for b in (0, 2, 1, 3):
            mm(ps(b), 128, "qe", 128 * b, "qg", 0)
        for b in (0, 2, 1, 3):
            o, i = ("gb", 64 * b, 64 * b + 64), (ps(b), 0, 64)
            if b in (0, 1):
                vts(o, i, 0.5, None, OP.mult)
            else:
                act(o, i, ACT.Copy, scale=0.5)
        for h in (0, 1):
            mine = MINE[t][h]
            a, z = CUTS[t + 1][h], CUTS[t + 1][h + 1]
            off = ("ko", a // 16, z // 16)
            for b in mine:
                act(("ge", 512 * b + a, 512 * b + z), ("gb", 64 * b, 64 * b + 64), ACT.Copy, off=off)
            for b in [b for b in range(4) if b not in mine] + list(mine):
                o = (new, 4 * a + b, 4 * z, 4)
                if b in mine:
                    vtt(o, (ps(HB[b]), a, z), ("ge", 512 * b + a, 512 * b + z), OP.add)
                else:
                    vtt(o, ("gb", 64 * b, 64 * b + 64), ("dd", 512 * b + a, 512 * b + z), OP.add, off=off)
            key_half(t + 1, new, h)

    for i in range(0, len(ORDER), 2):
        issue(ops[int(ORDER[i:i + 2], 36)])
    for t in range(ROUNDS):
        for s in arrive:
            count[s + str(t)] = arrive[s]
    for s in SEMAPHORES:
        if count[s]:
            wait("q", s, count[s])
